import numpy as np, ml_dtypes
CORES = [48,51,52,55]
N = 4
import mx_ref
BF = ml_dtypes.bfloat16
def gentries(a):
    return np.ascontiguousarray(a.reshape(8, 16, -1).transpose(0, 2, 1)).reshape(8, -1)
def gtable(e):
    e = np.asarray(e); return np.ascontiguousarray(e.reshape(8, -1, 16).transpose(0, 2, 1)).reshape(128, -1).astype(np.int32)
def gcols(t, e):
    v = np.concatenate([t.reshape(8, 16, -1, 4), np.zeros((8, 16, 1, 4), BF)], axis=2)
    return np.ascontiguousarray(np.stack([v[g][:, e[g]] for g in range(8)])).reshape(128, -1)
def tile(rs):
    return np.stack(rs, axis=2).reshape(128, -1).astype(BF)
def pick(q, e):
    c = np.concatenate([q[0].reshape(128, -1, 4), np.zeros((128, 1, 4), np.uint8)], axis=1); s = np.concatenate([q[1], np.ones((16, 1), np.uint8)], axis=1)
    return (np.ascontiguousarray(c[:, e].reshape(128, -1)), np.ascontiguousarray(s[:, e]))
def join(*qs):
    return (np.concatenate([q[0] for q in qs], axis=1), np.concatenate([q[1] for q in qs], axis=1))
def put(q, e, v):
    c, s = q[0].reshape(128, -1, 4).copy(), q[1].copy(); c[:, e] = v[0].reshape(128, -1, 4); s[:, e] = v[1]
    return (c.reshape(128, -1), s)
def pk(c, s):
    return (np.ascontiguousarray(c), mx_ref.live(s))
def emit(q):
    return q[0], q[1]
def packed(v, rng):
    q = [mx_ref.quantize(np.ascontiguousarray(v[r])) for r in range(N)]
    return np.stack([a for a, b in q]), np.stack([mx_ref.plane(b, rng) for a, b in q])
def values_of_codes():
    e, c = np.zeros((128, 128, 4), np.float32), np.zeros((128, 2, 4), np.uint8)
    e[np.arange(128), np.arange(128), 0] = 1
    c[:127, :, 0] = np.arange(256).reshape(2, 128).T[:127]
    return mx_ref.matmul(mx_ref.quantize(e.reshape(128, 512).astype(BF)), (c.reshape(128, 8), np.full((16, 2), 127, np.uint8))).T.reshape(-1).astype(np.float64)
CODE_VALUE, SCALE_VALUE = values_of_codes(), 2.0 ** (np.arange(256) - 127.0)
def decode(q):
    return (CODE_VALUE[q[0]].reshape(16, 8, -1, 4) * SCALE_VALUE[q[1]][:, None, :, None] + 0.0).reshape(128, -1).astype(np.float32)
def f(rng, *shape):
    return mx_ref.flush((rng.standard_normal(shape, dtype=np.float32) * np.exp2(rng.integers(-2, 3, shape[:-1] + (1,)))).astype(BF))
def wide(rng, *shape, cols=0):
    v = rng.standard_normal(shape, dtype=np.float32) * np.exp2(rng.integers(-12, 13, shape)).astype(np.float32)
    if cols: v *= np.repeat(np.exp2(rng.integers(-cols, cols + 1, shape[:-2] + (1, shape[-1] // 4))) * (rng.random(shape[:-2] + (1, shape[-1] // 4)) > 0.0625), 4, axis=-1).astype(np.float32)
    return mx_ref.flush(v.astype(BF))
C, HALF = 448, 224
STEP = [1, 2, 3]
def big(v):
    v = v.astype(np.float32)
    v[np.abs(v) < np.float32(2.0 ** -16)] = 0
    return v.astype(BF)
def numbers_of(rng):
    return {"x": big(f(rng, N, 128, 4 * C)), "u": np.array(f(rng, N, 128, 512)), "v": np.array(f(rng, N, 128, 512))}
def lists(rng):
    e = np.tile(np.arange(C), (N, 8, 1))
    o = rng.permuted(e, axis=2)
    m = np.zeros((N, 8, C), np.int64)
    np.put_along_axis(m, o, o[:, :, np.arange(C) ^ 1], axis=2)
    return rng.permuted(e, axis=2), m
def stored(q, m):
    return {"gq": np.stack([gtable(q[r]) for r in range(N)]), "gm": np.stack([gtable(m[r]) for r in range(N)])}
def layers(rng):
    return big(f(rng, N, 128, 2048)).reshape(N, 8, 16, 4, 8, 16, 4)
def no_layers():
    return np.zeros((N, 8, 16, 4, 8, 16, 4), np.float32)
def weights(rng, w):
    c, p = packed(np.ascontiguousarray(w.astype(BF)).reshape(N, 128, 2048), rng)
    return {"wc": c, "ws": p}
def setup_inputs(rng):
    return {**numbers_of(rng), **stored(*lists(rng)), **weights(rng, layers(rng))}
def setup_inputs_ties(rng):
    d = numbers_of(rng)
    o = rng.permutation(N)
    q, m = lists(rng)
    k = rng.integers(-1, 2, (N, 8, C)).astype(np.float32)
    k[o[0], rng.permutation(8)[:4]] = 0
    k[o[1]] = np.where(rng.permutation(8) < 4, 1, -1)[:, None]
    k[o[3]] = np.where(np.arange(C) < HALF, 1, -3)
    for g in range(8):
        a, b, p = rng.permutation(HALF), HALF + rng.permutation(HALF), rng.permutation(HALF)
        q[o[3], g] = np.concatenate([a, b] if g == 0 else [b, a])
        m[o[3], g, :HALF] = HALF + p
        m[o[3], g, HALF + p] = np.arange(HALF)
    x = d["x"].reshape(N, 8, 16, C, 4)
    x[:, :, 0] = 0
    x[:, :, 0, :, 0] = k.astype(BF)
    u = d["u"].reshape(N, 128, 128, 4)
    u[:, :, ::16] = 0
    for h in range(0, 128, 16): u[:, h, h, 0] = 1
    w = layers(rng)
    w[:, :, :, :, :, 0] = 0
    return {"x": x.reshape(N, 128, 4 * C), "u": u.reshape(N, 128, 512), "v": d["v"], **stored(q, m), **weights(rng, w)}
def setup_inputs_near(rng):
    d = numbers_of(rng)
    o = rng.permutation(N) % 2
    k = np.where(o == 0, 2.0 ** -30, 1.0)
    x = np.zeros((N, 8, 16, C, 4))
    s = rng.integers(-1, 2, (N, 8, C)) * k[:, None, None]
    x[:, :, 0, :, 0] = 1.125 * s
    x[:, :, 1, :, 0] = -1.25 * s
    x[:, :, 7, :, 0] = 2.0 ** -30
    x[:, :, 8, :, 0] = 2.0 ** -30
    for r in range(N):
        at = [0, C - 1, int(rng.integers(C)), int(rng.integers(C))]
        for g, j in zip(rng.permutation(8)[:4], at): x[r, g, 0, j, 0] = 2.0 ** 30 * rng.choice([-1.0, 1.0])
    u = d["u"].reshape(N, 128, 128, 4)
    u[:, :, ::16] = 0
    for h in range(0, 128, 16):
        u[:, h, h, 0] = (1.125 * k).astype(np.float32).astype(BF)
        u[:, h + 1, h, 0] = k.astype(np.float32).astype(BF)
        u[:, h + 9, h, 0] = 2.0 ** -30
    w = no_layers()
    for g in range(8):
        w[:, g, 8, 0, g, 8, 0] = 32
        w[:, g, 1, 0, g, 9, 0] = np.where(o == 0, 2.0 ** -9, 2.0 ** -30)
    return {"x": x.astype(np.float32).reshape(N, 128, 4 * C).astype(BF), "u": u.reshape(N, 128, 512), "v": d["v"], **stored(*lists(rng)), **weights(rng, w)}
def setup_inputs_odd(rng):
    d = numbers_of(rng)
    x = (1.0 + (2 * rng.integers(0, 64, (N, 8, 16, C, 4)) + 1) * 2.0 ** -7) * np.exp2(-rng.integers(0, 7, (N, 8, 16, C, 4)).astype(np.float64)) * rng.choice([-1.0, 1.0], (N, 8, 16, C, 4))
    e = rng.choice([-1.0, 1.0], (N, 8, C)) * 2.0 ** -8
    n = rng.integers(0, 2, (N, 8, C))
    x[:, :, 8:] = 0
    x[:, :, 0, :, 0] = 1.96875 * 2.0 ** 8 * rng.choice([-1.0, 1.0], (N, 8, 1))
    x[:, :, 1, :, 0] = np.where(n == 0, 5.0, 7.0) * e
    x[:, :, 8, :, 0] = np.where(n == 0, -4.5, -7.5) * e
    x[:, :, 10, :, 0] = 1.125 * 2.0 ** -2
    u = d["u"].reshape(N, 128, 128, 4)
    u[:, :, ::16] = 0
    for h in range(0, 128, 16):
        u[:, h + 1, h, 0] = 1
        u[:, h + 8, h, 0] = 1
    w = no_layers()
    for g in range(8):
        w[:, g, 10, 0, g, 9, 0] = 1.75 * 2.0 ** 5
        for b in range(4): w[:, g, 10, b, g, 11:, 0] = rng.choice([1.125, 1.5, 2.0], (N, 5)) * 2.0 ** -9
    return {"x": x.astype(np.float32).reshape(N, 128, 4 * C).astype(BF), "u": u.reshape(N, 128, 512), "v": d["v"], **stored(*lists(rng)), **weights(rng, w)}
def setup_inputs_ends(rng):
    d = numbers_of(rng)
    o, e, h = rng.permutation(N) % 4, rng.permutation(N) % 4, rng.permutation(8)
    s = rng.choice([-1.0, 1.0], (N, 128, C, 4))
    s[o == 0] = -1
    s[o == 1] = rng.choice([-1.0, 1.0], (N, 1, C, 1))[o == 1]
    x = s * (0.955 + 0.02 * rng.random((N, 128, C, 4))) * 2.0 ** 30
    x[o == 3] = 2.0 ** -30
    size = np.where(o == 3, 2.0 ** -30, 2.0 ** 30)
    a = np.stack([rng.permutation(8) % 2 * 2.0 - 1.0 for r in range(N)]) * size[:, None]
    u = d["u"].reshape(N, 128, 128, 4)
    u[:, :, ::16] = a.astype(np.float32).astype(BF)[:, None, :, None]
    v = rng.choice([-1.0, 1.0], (N, 128, 512)) * np.where(o % 2 == 0, 2.0 ** 30, 2.0 ** -30)[:, None, None]
    q, m = lists(rng)
    c = np.arange(C)
    q[e == 0], m[e == 0] = c, C - 1 - c
    q[e == 1], m[e == 1] = C - 1 - c, c ^ 1
    q[e == 2], m[e == 2] = (c + 1) % C, (c + HALF) % C
    w = no_layers()
    i = np.arange(16)
    for r in range(N):
        for b in range(4):
            if o[r] < 3:
                for g in h[:3]: w[r, g, i, b, g, i, b] = -0.125
            w[r, h[4], i, b, h[3], i, b] = 2.0 ** 30 if o[r] == 3 else 2.0 ** -30
    return {"x": x.astype(np.float32).reshape(N, 128, 4 * C).astype(BF), "u": u.reshape(N, 128, 512), "v": v.astype(np.float32).astype(BF), **stored(q, m), **weights(rng, w)}
def setup_inputs_spread(rng):
    d = setup_inputs(rng)
    d["x"] = big(wide(rng, N, 128, 4 * C, cols=6))
    return d
def check_inputs(d):
    b = []
    for k in ("x", "u", "v"):
        a = np.abs(d[k].astype(np.float32))
        if not (np.isfinite(a).all() and ((a == 0) | (a >= 2.0 ** -30) & (a <= 2.0 ** 30)).all()): b.append("a value of " + k)
    none, least, most = [emit(mx_ref.quantize(np.full((128, 16), k, np.float32).astype(BF)))[1][0, 0] for k in (0.0, 2.0 ** -30, 2.0 ** 30)]
    c = np.arange(C)
    for r in range(N):
        if not (np.sort(gentries(d["gq"][r]), axis=1) == c).all(): b.append("gq: not each column once in a group")
        m = gentries(d["gm"][r])
        if not ((m >= 0) & (m < C)).all(): b.append("an entry of gm")
        elif not ((np.take_along_axis(m, m, axis=1) == c) & (m != c)).all(): b.append("gm: not pairs")
        if ((d["wc"][r] == 0x7F) | (d["wc"][r] == 0xFF)).any(): b.append("wc: a code that is no number")
        s = mx_ref.live(d["ws"][r])
        if ((s != none) & ((s < least) | (s > most))).any(): b.append("ws: a scale out of range")
        if (((d["wc"][r].reshape(16, 8, 512, 4) & 0x7F) != 0) & (s == none)[:, None, :, None]).any(): b.append("wc: a code other than zero under the scale of zeros")
    return b
def exchange(s, m):
    bit = np.roll(s[::16] > 0, 1, axis=0)
    return np.where(np.take_along_axis(bit, np.minimum(m, np.arange(C)), axis=1), m, np.arange(C))
def reference(x, u, v, gq, gm, wc, ws):
    qu = [mx_ref.quantize(u[r]) for r in range(N)]
    lay = [pk(wc[r], ws[r]) for r in range(N)]
    kept, pair = [gentries(gq[r]) for r in range(N)], [gentries(gm[r]) for r in range(N)]
    now = [x[r] for r in range(N)]
    for step in STEP:
        mid, back, sent = [], [], []
        for r in range(N):
            q, m = kept[r], pair[r]
            a, b = np.zeros((9, C), np.int64), np.zeros((9, C), np.int64)
            go = exchange(mx_ref.matmul(qu[r], mx_ref.quantize(now[r])), m)
            a[0] = np.arange(C)
            for g in range(8): a[g + 1] = q[g][go[g][a[g]]]
            t = ((now[r].astype(np.float32) + gcols(now[r], a[1:]).astype(np.float32)) * np.float32(0.5)).astype(BF)
            qt = mx_ref.quantize(t)
            go = exchange(mx_ref.matmul(qu[r], qt), m)
            inv = np.argsort(q, axis=1)
            b[8] = a[8]
            for g in range(7, -1, -1): b[g] = go[g][inv[g][b[g + 1]]]
            sent.append(mx_ref.quantize(tile([mx_ref.matmul(pick(lay[r], np.arange(128 * k, 128 * k + 128)), qt) * np.float32(0.03125) for k in range(4)])))
            miss = np.take_along_axis(a[:8] != b[:8], np.minimum(m, np.arange(C)), axis=1)
            kept[r] = np.where(miss, np.take_along_axis(q, m, axis=1), q)
            mid.append(t)
            back.append(b[:8])
        now = [(mid[r].astype(np.float32) + gcols(decode(sent[r ^ step]).astype(BF), back[r]).astype(np.float32)).astype(BF) for r in range(N)]
    y, qo = np.zeros((N, 128, C), np.float32), np.zeros((N, 8, C), np.float32)
    oc, osc = np.zeros((N, 128, 4 * C), np.uint8), np.zeros((N, 16, C), np.uint8)
    for r in range(N):
        q = mx_ref.quantize(now[r])
        y[r] = mx_ref.matmul(mx_ref.quantize(v[r]), q)
        qo[r] = kept[r]
        oc[r], osc[r] = emit(q)
    return {"y": y, "qo": qo, "oc": oc, "osc": osc}

@@ -1,0 +1,433 @@
+from concourse.bass import DstId, RemoteDMATransfer
+from concourse.mybir import dt, AluOpType, ActivationFunctionType
+import comms_topo
+
+STEP = [1, 2, 3]
+C = 448
+CA = 320
+BF, F32, I32, U16, MX, U8 = "bfloat16", "float32", "int32", "uint16", "float8_e4m3fn_x4", "uint8"
+
+SCRATCH = {}
+for _n, _w in (("x0", 1792), ("xt", 1792), ("xh", 1792), ("xg", 1792), ("vt", 1792), ("ht", 1792), ("dd", 1792), ("ut", 512), ("vv", 512),
+               ("wt", 1408), ("eb", 2048), ("zt", 848), ("ident", 128), ("jcol", 128),
+               ("iot", C), ("j16", C), ("j4", C), ("mask16", C), ("mask4", C), ("seg16", C), ("seg4", C), ("masku", 112),
+               ("mf0", C), ("mf1", C), ("mb0", C), ("mb1", C), ("rowq", C), ("rowm", C), ("rowqi", C), ("wA", C), ("wB", C),
+               ("mg", C), ("sc", C), ("sc4", C), ("pu", 112), ("pus", 112), ("nu", C), ("sg", C), ("tab", 16), ("pa", 28), ("ag", 28)):
+    SCRATCH[_n] = ("sbuf", [128, _w], BF)
+for _n, _w in (("uc", 128), ("uq", 128), ("vq", 128), ("wq", 512), ("xc", C), ("vc", C), ("ebc", 512), ("shc", 352), ("zc", 212),
+               ("hc0", C), ("hc1", C), ("hc2", C), ("lc0", C), ("lc1", C), ("lc2", C)):
+    SCRATCH[_n] = ("sbuf", [128, _w], MX)
+    SCRATCH[_n + "p"] = ("sbuf", [128, _w], U8)
+for _n, _w in (("qU", 28), ("mU", 28), ("loU", 28), ("qiU", 28), ("loqU", 28), ("lf", 224), ("lb", 224), ("l4", 112), ("p16", 28),
+               ("a8", 28), ("loP", 28), ("loqP", 28), ("dU", 28), ("ulist", 8), ("qoU", 28)):
+    SCRATCH[_n] = ("sbuf", [128, _w], U16)
+for _n, _w in (("iwb", 224), ("iw", 28), ("qF", 224), ("dF", 224), ("qB", 224), ("dB", 224), ("t1", 112), ("t2", 112), ("t3", 28), ("t4", 28),
+               ("mF", 28), ("t5", 28), ("t6", 28), ("t7", 28), ("t8", 28), ("t9", 28), ("lo", 28), ("loq", 28), ("dhF", 28), ("qhF", 28), ("dhB", 28), ("qhB", 28), ("cp", 1), ("cp16", 1), ("cphi", 1), ("cq", 4), ("ysb", C), ("qrow", C)):
+    SCRATCH[_n] = ("sbuf", [128, _w], F32)
+for _n, _w in (("gqi", 28), ("gmi", 28), ("li", 84), ("pi", 4), ("uli", 16)):
+    SCRATCH[_n] = ("sbuf", [128, _w], I32)
+SCRATCH["dl"] = ("dram", [32, 4, 28], U16)
+for _k in range(8):
+    SCRATCH["P%d" % _k] = ("psum", [128, 512], F32)
+SEMAPHORES = ["v", "s", "t", "gc"] + ["d%d" % k for k in range(40)] + ["arr%d" % k for k in range(3)] + ["snt%d" % k for k in range(3)]
+
+
+def rank_program(g, core, T, topo):
+    rank = T.rank_of(core)
+    if rank is None:
+        return
+    A = AluOpType
+    F = ActivationFunctionType
+    queue = {"v": g.vector, "s": g.scalar, "t": g.tensor, "g": g, "y": g.sync}
+    own = {"v": "v", "s": "s", "t": "t", "g": "gc"}
+    known = {q: {} for q in queue}
+    count, W, R, nd = {}, {}, {}, [0]
+
+    def need(q, toks):
+        best = {}
+        for tok in toks:
+            if tok[0] not in best or best[tok[0]][1] < tok[1]:
+                best[tok[0]] = tok
+        order = sorted(best.values(), key=lambda k: -len(k[2]))
+        for sem, val, snap in order:
+            if known[q].get(sem, 0) < val:
+                queue[q].wait_ge(T.sem[sem], val)
+                known[q][sem] = val
+            for k, x in snap.items():
+                if known[q].get(k, 0) < x:
+                    known[q][k] = x
+
+    def deps(reads, writes):
+        toks = []
+        for k in reads:
+            toks += W[k]
+        for k in writes:
+            toks += W.get(k, []) + list(R.get(k, {}).values())
+        return toks
+
+    def done(tok, reads, writes):
+        for k in writes:
+            W[k] = [tok]
+            R[k] = {}
+        for k in reads:
+            if k not in writes:
+                R.setdefault(k, {})[tok[0]] = tok
+
+    def op(q, reads, writes, call):
+        need(q, deps(reads, writes))
+        sem = own[q]
+        count[sem] = count.get(sem, 0) + 1
+        call().then_inc(T.sem[sem], 1)
+        done((sem, count[sem], dict(known[q])), reads, writes)
+
+    def dma(q, pairs, reads, writes):
+        need(q, deps(reads, writes))
+        sem = "d%d" % nd[0]
+        nd[0] += 1
+        for o, i in pairs:
+            queue[q].dma_start(o, i).then_inc(T.sem[sem], 16)
+        count[sem] = 16 * len(pairs)
+        done((sem, count[sem], dict(known[q])), reads, writes)
+
+    def tt(reads, writes, out, a, b, o):
+        op("v", reads, writes, lambda: g.vector.tensor_tensor(out, a, b, o))
+
+    def ts(reads, writes, out, a, s1, o1, s2=None, o2=None):
+        if o2 is None:
+            op("v", reads, writes, lambda: g.vector.tensor_scalar(out, a, s1, None, o1))
+        else:
+            op("v", reads, writes, lambda: g.vector.tensor_scalar(out, a, s1, s2, o1, o2))
+
+    def cp(reads, writes, out, a):
+        op("v", reads, writes, lambda: g.vector.tensor_copy(out, a))
+
+    def fill(writes, out, c):
+        op("v", [], writes, lambda: g.vector.memset(out, c))
+
+    def act(reads, writes, out, a, f=F.Copy, **kw):
+        op("s", reads, writes, lambda: g.scalar.activation(out, a, f, **kw))
+
+    def quant(reads, writes, c, a, b, src, e):
+        op("v", reads, writes, lambda: g.vector.quantize_mx(T[c][:, a:b], T[c + "p"][:, a:b], src[:, e:e + 4 * (b - a)]))
+
+    def mm(reads, writes, out, w, wa, x, xa, n):
+        op("t", reads, writes, lambda: g.tensor.matmul_mx(out, T[w][:, wa:wa + 128], T[w + "p"][:, wa:wa + 128], T[x][:, xa:xa + n], T[x + "p"][:, xa:xa + n], True, True))
+
+    def scan(reads, writes, out, seg, a):
+        op("v", reads, writes, lambda: g.vector.tensor_tensor_scan(out, seg, a, 0.0, A.mult, A.add))
+
+    dma("y", [(T.gqi[:], T.gq[:])], [], ["gqi"])
+    dma("y", [(T.gmi[:], T.gm[:])], [], ["gmi"])
+    dma("y", [(T.ut[:], T.u[:])], [], ["ut"])
+    dma("s", [(T.x0[:, 0:4 * CA], T.x[:, 0:4 * CA])], [], ["x0A"])
+    dma("s", [(T.x0[:, 4 * CA:], T.x[:, 4 * CA:])], [], ["x0B"])
+    dma("y", [(T.vv[:], T.v[:])], [], ["vv"])
+    dma("y", [(T.wq[:].bitcast(dt.uint8), T.wc[:])], [], ["wqc"])
+    dma("y", [(T.wqp[:], T.ws[:])], [], ["wqp"])
+
+    def iota(key, out, pat, base, cm, flag=True):
+        if flag:
+            op("g", [], [key], lambda: g.iota(out, pat, base, cm, allow_small_or_imprecise_dtypes=True))
+        else:
+            op("g", [], [key], lambda: g.iota(out, pat, base, cm))
+    iota("pi", T.pi[:, 0:1], [[0, 1]], 0, 1, False)
+    iota("uli", T.uli[:, 0:8], [[16, 8]], -16, 0, False)
+    iota("j16", T.j16[:], [[0, 28], [1, 16]], 0, 0)
+    iota("jcol", T.jcol[:], [[1, 128]], 0, 0)
+    iota("iot", T.iot[:], [[1, C]], -224, 0)
+    iota("iwb", T.iwb[:], [[0, 8], [16, 28]], 0, 0)
+    iota("j4", T.j4[:], [[0, 112], [1, 4]], 0, 0)
+    cplo, c896, cpt, cpp = (T.cq[:, k:k + 1] for k in range(4))
+    ts(["pi"], ["pi1"], T.pi[:, 1:2], T.pi[:, 0:1], 15, A.bitwise_and)
+    ts(["pi"], ["pi2"], T.pi[:, 2:3], T.pi[:, 0:1], 2, A.arith_shift_right, 3, A.bitwise_and)
+    ts(["pi"], ["pi3"], T.pi[:, 3:4], T.pi[:, 0:1], 3, A.bitwise_and)
+    ts(["uli"], ["uli2"], T.uli[:, 8:16], T.uli[:, 0:8], 127, A.bitwise_and)
+    cp(["pi"], ["cp"], T.cp[:], T.pi[:, 0:1])
+    cp(["pi1"], ["cp16"], T.cp16[:], T.pi[:, 1:2])
+    cp(["pi2"], ["cphi"], T.cphi[:], T.pi[:, 2:3])
+    cp(["pi3"], ["cplo"], cplo, T.pi[:, 3:4])
+    cp(["uli2"], ["ulist"], T.ulist[:], T.uli[:, 8:16])
+    ts(["cplo"], ["c896"], c896, cplo, 896.0, A.add)
+    ts(["cplo"], ["cpt"], cpt, cplo, 4.0, A.mult, -224.0, A.add)
+    fill(["zt"], T.zt[:], 0.0)
+    fill(["wt"], T.wt[:], 0.0)
+    ts(["j16", "cp16"], ["mask16"], T.mask16[:], T.j16[:], T.cp16[:], A.is_equal)
+    ts(["j16"], ["seg16"], T.seg16[:], T.j16[:], 0.0, A.is_gt)
+    ts(["jcol", "cp"], ["ident"], T.ident[:], T.jcol[:], T.cp[:], A.is_equal)
+    ts(["jcol"], ["tab"], T.tab[:], T.jcol[:, 0:16], -2.0, A.mult, 1.0, A.add)
+    cp(["ident"], ["wt"], T.wt[:, 448:960:4], T.ident[:])
+    quant(["wt"], ["shc"], "shc", 0, 352, T.wt, 0)
+    quant(["zt"], ["zcr"], "zc", 84, 212, T.zt, 336)
+    ts(["iwb", "cp16"], ["iw"], T.iw[:], T.iwb[:, 0:28], T.cp16[:], A.add)
+    ts(["iwb", "cp16"], ["qF0", "qFr"], T.qF[:], T.iwb[:], T.cp16[:], A.add)
+    fill(["dF0", "dFr"], T.dF[:], 0.0)
+
+    cp(["gqi"], ["qU"], T.qU[:], T.gqi[:])
+    act(["iot", "qU"], ["rowq"], T.rowq[:], T.iot[:, 0:C].indirect(T.qU[:, 0:28]))
+    cp(["gqi"], ["qF0"], T.qF[:, 0:28], T.gqi[:])
+    cp(["gmi"], ["mU"], T.mU[:], T.gmi[:])
+    cp(["gmi"], ["mF"], T.mF[:], T.gmi[:])
+    dma("y", [(T.qF[16 * n:128, 28 * n:28 * n + 28], T.qF[0:128 - 16 * n, 0:28]) for n in range(1, 8)], ["qF0"], ["qFr"])
+    tt(["mF", "iw"], ["lo"], T.lo[:], T.mF[:], T.iw[:], A.min)
+    quant(["ut"], ["uc"], "uc", 0, 128, T.ut, 0)
+    cp(["lo"], ["loU"], T.loU[:], T.lo[:])
+    tt(["rowq", "mU", "mask16"], ["mg"], T.mg[:], T.rowq[:, 0:C].indirect(T.mU[:, 0:28]), T.mask16[:], A.mult)
+    scan(["seg16", "mg"], ["sc"], T.sc[:], T.seg16[:], T.mg[:])
+    ts(["sc"], ["t6"], T.t6[:], T.sc[:, 15:C:16], 224.0, A.add)
+    tt(["t6", "qF0"], ["dF0"], T.dF[:, 0:28], T.t6[:], T.qF[:, 0:28], A.subtract)
+    dma("y", [(T.dF[16 * n:128, 28 * n:28 * n + 28], T.dF[0:128 - 16 * n, 0:28]) for n in range(1, 8)], ["dF0"], ["dFr"])
+    for a, b in ((0, 848), (848, 1696), (1696, 2048)):
+        act(["zt"], ["eb%d" % a], T.eb[:, a:b], T.zt[:, 0:b - a])
+    for b in range(4):
+        act(["ident", "eb0", "eb848", "eb1696"], ["ebi%d" % b], T.eb[:, 512 * b + b:512 * b + 512:4], T.ident[:])
+    cp(["uc", "ulist"], ["uqc"], T.uq[:, 0:128].bitcast(dt.uint32), T.uc[:, 0:128].bitcast(dt.uint32).indirect(T.ulist[:, 0:8]))
+    cp(["uc", "ulist"], ["uqs"], T.uqp[:, 0:128], T.ucp[:, 0:128].indirect(T.ulist[:, 0:8]))
+
+    def score(src, key, c, part):
+        a, b, bank = (0, CA, "P0") if part == "A" else (CA, C, "P3")
+        quant([key + part], [c + part], c, a, b, src, 4 * a)
+        mm(["uqc", "uqs", c + part], [bank], T[bank][:, 0:b - a], "uq", 0, c, a, b - a)
+
+    def sign(part):
+        a, b, bank = (0, CA, "P0") if part == "A" else (CA, C, "P3")
+        act([bank], ["sg" + part], T.sg[:, a:b], T[bank][:, 0:b - a], F.Sign, bias=-(2.0 ** -93))
+
+    def halve(src, key, a, b, piece):
+        act([key], ["xh%d" % piece], T.xh[:, a:b], src[:, a:b], F.Copy, scale=0.5)
+
+    XH = ["xh0", "xh1", "xh2"]
+    score(T.x0, "x0", "xc", "A")
+    score(T.x0, "x0", "xc", "B")
+    sign("A")
+    sign("B")
+    quant(["vv"], ["vq"], "vq", 0, 128, T.vv, 0)
+    ts(["dF0"], ["dhF"], T.dhF[:], T.dF[:, 0:28], 0.5, A.mult)
+    tt(["dhF", "qF0"], ["qhF"], T.qhF[:], T.dhF[:], T.qF[:, 0:28], A.add)
+    quant(["ebi0", "ebi1", "ebi2", "ebi3"], ["ebc"], "ebc", 0, 512, T.eb, 0)
+    halve(T.x0, "x0A", 0, 512, 0)
+    halve(T.x0, "x0A", 512, 4 * CA, 1)
+    halve(T.x0, "x0B", 4 * CA, 4 * C, 2)
+    tt(["cpt", "cphi"], ["cpp"], cpp, cpt, T.cphi[:], A.add)
+
+    def late_constants():
+        ts(["j4", "cphi"], ["mask4"], T.mask4[:], T.j4[:], T.cphi[:], A.is_equal)
+        ts(["j4"], ["seg4"], T.seg4[:], T.j4[:], 0.0, A.is_gt)
+        ts(["j4", "cplo"], ["masku"], T.masku[:], T.j4[:, 0:112], cplo, A.is_equal)
+        ts(["iwb", "cpp"], ["ag0", "ag"], T.ag[:], T.iwb[:, 0:28], cpp, A.add)
+
+    def turned(src, dst):
+        cp([src], ["li"], T.li[:, 0:28], T[src][:])
+        ts(["li"], ["li1"], T.li[:, 28:56], T.li[:, 0:28], 3, A.bitwise_and)
+        ts(["li"], ["li2"], T.li[:, 56:84], T.li[:, 0:28], 2, A.arith_shift_right, 3, A.bitwise_and)
+        tt(["li1", "li2"], ["t9"], T.t9[:], T.li[:, 28:56], T.li[:, 56:84], A.subtract)
+        ts(["t9"], ["t5"], T.t5[:], T.t9[:], 3.0, A.mult)
+        tt(["t5", src], ["t6"], T.t6[:], T.t5[:], T[src][:], A.add)
+        cp(["t6"], [dst], T[dst][:], T.t6[:])
+
+    def back_tables_1():
+        cp(["iot", "qU"], ["rowqi"], T.rowqi[:, 0:C].indirect(T.qU[:, 0:28]), T.iot[:])
+
+    def back_tables_2():
+        tt(["rowqi", "mask16"], ["mg"], T.mg[:], T.rowqi[:], T.mask16[:], A.mult)
+        scan(["seg16", "mg"], ["sc"], T.sc[:], T.seg16[:], T.mg[:])
+        ts(["sc"], ["qiU"], T.qiU[:], T.sc[:, 15:C:16], 224.0, A.add)
+        ts(["sc"], ["qB0"], T.qB[:, 0:28], T.sc[:, 15:C:16], 224.0, A.add)
+        dma("y", [(T.qB[0:128 - 16 * n, 28 * n:28 * n + 28], T.qB[16 * n:128, 0:28]) for n in range(1, 8)], ["qB0"], ["qBr"])
+        tt(["rowm", "qiU", "mask16"], ["mg"], T.mg[:], T.rowm[:, 0:C].indirect(T.qiU[:, 0:28]), T.mask16[:], A.mult)
+        scan(["seg16", "mg"], ["sc"], T.sc[:], T.seg16[:], T.mg[:])
+        ts(["sc"], ["t7"], T.t7[:], T.sc[:, 15:C:16], 224.0, A.add)
+        tt(["t7", "qB0"], ["dB0"], T.dB[:, 0:28], T.t7[:], T.qB[:, 0:28], A.subtract)
+        dma("y", [(T.dB[0:128 - 16 * n, 28 * n:28 * n + 28], T.dB[16 * n:128, 0:28]) for n in range(1, 8)], ["dB0"], ["dBr"])
+        tt(["t7", "qB0"], ["loq"], T.loq[:], T.t7[:], T.qB[:, 0:28], A.min)
+        ts(["dB0"], ["dhB"], T.dhB[:], T.dB[:, 0:28], 0.5, A.mult)
+        cp(["loq"], ["loqU"], T.loqU[:], T.loq[:])
+        tt(["dhB", "qB0"], ["qhB"], T.qhB[:], T.dhB[:], T.qB[:, 0:28], A.add)
+
+    def spread(lo, mask, lst, q, d, way):
+        tt(["sgA", "sgB", lo, mask], ["mg"], T.mg[:], T.sg[:, 0:C].indirect(T[lo][:, 0:28]), T[mask][:], A.mult)
+        scan(["seg16", "mg"], ["sc"], T.sc[:], T.seg16[:], T.mg[:])
+        dh, qh = ("dhF", "qhF") if lst == "lf" else ("dhB", "qhB")
+        ts(["sc"], ["zt"], T.zt[:, 336:448:4], T.sc[:, 15:C:16], 0.0, A.is_gt)
+        tt(["sc", dh], ["t3"], T.t3[:], T.sc[:, 15:C:16], T[dh][:], A.mult)
+        quant(["zt"], ["zc"], "zc", 0, 128, T.zt, 0)
+        tt(["t3", qh], ["t4"], T.t4[:], T.t3[:], T[qh][:], A.add)
+        cp(["t4"], [lst + "o"], T[lst][:, 0:28], T.t4[:])
+        for bank, ns in (("P1", (1, 2, 3)), ("P2", (4, 5, 6, 7))):
+            need("t", deps(["zc", "zcr", "shc"], [bank]))
+            for n in ns:
+                s0, z0 = 112 + way * 16 * n, 84 - 28 * (n - ns[0])
+                i = g.tensor.matmul_mx(T[bank][:, 0:128], T.shc[:, s0:s0 + 128], T.shcp[:, s0:s0 + 128], T.zc[:, z0:z0 + 128], T.zcp[:, z0:z0 + 128], n == ns[0], n == ns[-1])
+            count["t"] = count.get("t", 0) + 1
+            i.then_inc(T.sem["t"], 1)
+            done(("t", count["t"], dict(known["t"])), ["zc", "zcr", "shc"], [bank])
+
+    def prep(k, part, lst, q, d):
+        bank, a, n = ("P1", 28, 84) if part == "A" else ("P2", 112, 112)
+        if k == 0:
+            tt([bank, d + "r"], ["t1"], T.t1[:, 0:n], T[bank][:, 0:n], T[d][:, a:a + n], A.mult)
+        if k == 1:
+            tt(["t1", q + "r"], ["t2"], T.t2[:, 0:n], T.t1[:, 0:n], T[q][:, a:a + n], A.add)
+        if k == 2:
+            cp(["t2"], [lst + part], T[lst][:, a:a + n], T.t2[:, 0:n])
+
+    def gather(i, lst, nv):
+        src = "iot" if i == 0 else ("wB", "wA")[i % 2]
+        dst = ("wA", "wB")[i % 2]
+        key = ["iot"] if i == 0 else [src + "v", src + "s"]
+        lk = lst + ("o" if i == 0 else "A" if i < 4 else "B")
+        if nv:
+            cp(key + [lk], [dst + "v"] + ([dst + "s"] if nv == 28 else []), T[dst][:, 0:16 * nv], T[src][:, 0:C].indirect(T[lst][:, 28 * i:28 * i + nv]))
+        if nv < 28:
+            act(key + [lk], [dst + "s"] + ([dst + "v"] if nv == 0 else []), T[dst][:, 16 * nv:C], T[src][:, 0:C].indirect(T[lst][:, 28 * i + nv:28 * i + 28]))
+
+    def offsets(src, off, offkeys):
+        tt([src + "v", src + "s", "mask4"] + offkeys, ["mg"], T.mg[:], T[src][:, 0:C].indirect(off), T.mask4[:], A.mult)
+        scan(["seg4", "mg"], ["sc4"], T.sc4[:], T.seg4[:], T.mg[:])
+        ts(["sc4", "c896"], ["l4"], T.l4[:], T.sc4[:, 3:C:4], 4.0, A.mult, c896, A.add)
+
+    def move(out, okey, win, wkeys, base, bkeys, part):
+        a, b = (0, CA) if part == "A" else (CA, C)
+        tt(wkeys + ["l4"] + bkeys, [okey + part], out[:, 4 * a:4 * b], win[:, 0:4 * C].indirect(T.l4[:, a // 4:b // 4]), base[:, 4 * a:4 * b], A.add)
+
+    mf, mb = "mask16", "mask16"
+    for r in range(3):
+        dst = T.cores[rank ^ STEP[r]]
+        hc, lc = "hc%d" % r, "lc%d" % r
+        dma("y", [(T.xg[:], T.xh[:])], XH, ["xg"])
+        spread("loU", mf, "lf", "qF", "dF", -1)
+        gather(0, "lf", 0 if r == 0 else 4)
+        for k in range(3):
+            prep(k, "A", "lf", "qF", "dF")
+        if r == 0:
+            for k in range(3):
+                prep(k, "B", "lf", "qF", "dF")
+            for k in range(1, 7):
+                gather(k, "lf", 0)
+                if k == 2:
+                    act(["iwb", "cp16"], ["qB0", "qBr"], T.qB[:], T.iwb[:], F.Identity, bias=T.cp16[:])
+                    act(["wt"], ["dB0", "dBr"], T.dB[:], T.wt[:, 0:224])
+                    act(["iot", "mU"], ["rowm"], T.rowm[:], T.iot[:, 0:C].indirect(T.mU[:, 0:28]))
+            late_constants()
+            back_tables_1()
+            back_tables_2()
+        else:
+            gather(1, "lf", 10)
+            prep(0, "B", "lf", "qF", "dF")
+            gather(2, "lf", 8)
+            prep(1, "B", "lf", "qF", "dF")
+            gather(3, "lf", 10)
+            prep(2, "B", "lf", "qF", "dF")
+            gather(4, "lf", 0)
+            nxt = "mb%d" % (r % 2)
+            tt(["nu", "loqP", mb], [nxt], T[nxt][:], T.nu[:, 0:C].indirect(T.loqP[:, 0:28]), T[mb][:], A.mult)
+            mb = nxt
+            gather(5, "lf", 14)
+            gather(6, "lf", 14)
+        offsets("wA", T.lf[:, 196:224], ["lfB"])
+        move(T.vt, "vt", T.xh, XH, T.xg, ["xg"], "A")
+        score(T.vt, "vt", "vc", "A")
+        sign("A")
+
+        def layer(b, part):
+            a, e = (0, CA) if part == "A" else (CA, C)
+            bank = "P%d" % (4 + b)
+            mm(["wqc", "wqp", "vc" + part], [bank], T[bank][:, 0:e - a], "wq", 128 * b, "vc", a, e - a)
+            act([bank], ["ht%d%s" % (b, part)], T.ht[:, 4 * a + b:4 * e:4], T[bank][:, 0:e - a], F.Copy, scale=0.03125)
+        layer(0, "A")
+        move(T.vt, "vt", T.xh, XH, T.xg, ["xg"], "B")
+        mm(["wqc", "wqp", "vcA"], ["P5"], T.P5[:, 0:CA], "wq", 128, "vc", 0, CA)
+        score(T.vt, "vt", "vc", "B")
+        sign("B")
+        act(["P5"], ["ht1A"], T.ht[:, 1:4 * CA:4], T.P5[:, 0:CA], F.Copy, scale=0.03125)
+        layer(2, "A")
+        layer(3, "A")
+        for b in range(4):
+            layer(b, "B")
+        tt(["sc4", "masku"], ["pu"], T.pu[:], T.sc4[:, 3:C:4], T.masku[:], A.mult)
+        scan(["seg4", "pu"], ["pus"], T.pus[:], T.seg4[:, 0:112], T.pu[:])
+        ts(["pus"], ["p16"], T.p16[:], T.pus[:, 3:112:4], 224.0, A.add)
+        cp(["pus"], ["pa"], T.pa[:], T.pus[:, 3:112:4])
+        dma("y", [(T.dl[k:32:4, :, :], T.p16[k:128:4, :]) for k in range(4)], ["p16"], ["dl"])
+        dma("y", [(T.ag[16:128, :], T.pa[0:112, :])], ["pa"], ["ag"])
+        dma("y", [(T.a8[16 * k:16 * k + 16, :], T.dl[28:32, :, :]) for k in range(8)], ["dl"], ["a8"])
+        spread("loqU", mb, "lb", "qB", "dB", 1)
+        quant(["ht%d%s" % (b, k) for b in range(4) for k in "AB"], [hc], hc, 0, C, T.ht, 0)
+        need("g", W[hc])
+        rid, pid, _ = topo.addr(dst)
+        mask, ne = topo.mask(core, dst), len(topo.engines(core, dst))
+        arr, snt = "arr%d" % r, "snt%d" % r
+        g.remote_dma(out_ap=T[lc][:, 0:C].bitcast(dt.uint8), in_ap=T[hc][:, 0:C].bitcast(dt.uint8), remote_sem=T.sem[arr], local_sem=T.sem[snt], pid=pid, routing_id=rid, dma_engine_mask=mask)
+        g.remote_dma(out_ap=T[lc + "p"][:, 0:C], in_ap=T[hc + "p"][:, 0:C], remote_sem=T.sem[arr], local_sem=T.sem[snt], pid=pid, routing_id=rid, dma_engine_mask=mask)
+        count[arr] = count[snt] = 2 * ne
+        W[lc] = [(arr, 2 * ne, {})]
+        gather(0, "lb", 0)
+        for k in range(3):
+            prep(k, "A", "lb", "qB", "dB")
+        gather(1, "lb", 10)
+        prep(0, "B", "lb", "qB", "dB")
+        gather(2, "lb", 8)
+        prep(1, "B", "lb", "qB", "dB")
+        gather(3, "lb", 10)
+        prep(2, "B", "lb", "qB", "dB")
+        gather(4, "lb", 14)
+        gather(5, "lb", 14)
+        gather(6, "lb", 28)
+        gather(7, "lb", 28)
+        for b in range(4):
+            bank = "P%d" % (4 + b)
+            mm(["ebc", lc], [bank], T[bank][:, 0:C], "ebc", 128 * b, lc, 0, C)
+            act([bank], ["dd%d" % b], T.dd[:, b:4 * C:4], T[bank][:, 0:C])
+        offsets("wB", T.a8[:, 0:28], ["a8"])
+        tt(["sc4", "masku"], ["pu"], T.pu[:], T.sc4[:, 3:C:4], T.masku[:], A.mult)
+        scan(["seg4", "pu"], ["pus"], T.pus[:], T.seg4[:, 0:112], T.pu[:])
+        if r == 0:
+            turned("lo", "loP")
+            turned("loq", "loqP")
+
+        def differ(k):
+            if k == 0:
+                tt(["pus", "ag", "ag0"], ["t8"], T.t8[:], T.pus[:, 3:112:4], T.ag[:], A.subtract)
+            else:
+                ts(["t8"], ["dU"], T.dU[:], T.t8[:], 0.0, A.not_equal)
+                act(["tab", "dU"], ["nu"], T.nu[:], T.tab[:, 0:16].indirect(T.dU[:, 0:28]))
+
+        def turn(old):
+            new = "mf%d" % (r % 2)
+            tt(["nu", "loP", old], [new], T[new][:], T.nu[:, 0:C].indirect(T.loP[:, 0:28]), T[old][:], A.mult)
+            return new
+        DD = ["dd%d" % b for b in range(4)]
+        if r < 2:
+            move(T.xt, "xt", T.dd, DD, T.vt, ["vtA"], "A")
+            differ(0)
+            score(T.xt, "xt", "xc", "A")
+            differ(1)
+            move(T.xt, "xt", T.dd, DD, T.vt, ["vtB"], "B")
+            score(T.xt, "xt", "xc", "B")
+            sign("A")
+            halve(T.xt, "xtA", 0, 512, 0)
+            sign("B")
+            halve(T.xt, "xtA", 512, 4 * CA, 1)
+            halve(T.xt, "xtB", 4 * CA, 4 * C, 2)
+            mf = turn(mf)
+        else:
+            differ(0)
+            differ(1)
+            for part, bank, a, b in (("A", "P0", 0, CA), ("B", "P3", CA, C)):
+                move(T.xt, "xt", T.dd, DD, T.vt, ["vt" + part], part)
+                if part == "A":
+                    mf = turn(mf)
+                    scan(["seg16", mf], ["sc"], T.sc[:], T.seg16[:], T[mf][:])
+                    ts(["sc"], ["t3"], T.t3[:], T.sc[:, 15:C:16], 0.0, A.is_lt)
+                    tt(["t3", "dF0"], ["t5"], T.t5[:], T.t3[:], T.dF[:, 0:28], A.mult)
+                    tt(["t5", "qF0"], ["t6"], T.t6[:], T.t5[:], T.qF[:, 0:28], A.add)
+                    cp(["t6"], ["qoU"], T.qoU[:], T.t6[:])
+                    act(["iot", "qoU"], ["qrow"], T.qrow[:], T.iot[:, 0:C].indirect(T.qoU[:, 0:28]), F.Identity, bias=224.0)
+                    dma("y", [(T.qo[:], T.qrow[0:128:16, :])], ["qrow"], ["qo"])
+                quant(["xt" + part], ["xc" + part], "xc", a, b, T.xt, 4 * a)
+                mm(["vq", "xc" + part], [bank], T[bank][:, 0:b - a], "vq", 0, "xc", a, b - a)
+                act([bank], ["y" + part], T.ysb[:, a:b], T[bank][:, 0:b - a])
+                dma("s", [(T.y[:, a:b], T.ysb[:, a:b])], ["y" + part], ["yo" + part])
+                dma("y", [(T.oc[:, 4 * a:4 * b], T.xc[:, a:b].bitcast(dt.uint8))] + [(T.osc[4 * k:4 * k + 4, a:b], T.xcp[32 * k:32 * k + 4, a:b]) for k in range(4)], ["xc" + part], ["oo" + part])
+    for sem in count:
+        if known["g"].get(sem, 0) < count[sem]:
+            g.wait_ge(T.sem[sem], count[sem])

@@ -4,32 +4,33 @@ import comms_topo
 
 STEP = [1, 2, 3]
 C = 448
-CA = 320
+PARTS = [(0, 192), (192, 320), (320, C)]
+HRUNS = [(0, 192), (192, C)]
+K = 2.0 ** 24
 BF, F32, I32, U16, MX, U8 = "bfloat16", "float32", "int32", "uint16", "float8_e4m3fn_x4", "uint8"
 
 SCRATCH = {}
 for _n, _w in (("x0", 1792), ("xt", 1792), ("xh", 1792), ("xg", 1792), ("vt", 1792), ("ht", 1792), ("dd", 1792), ("ut", 512), ("vv", 512),
-               ("wt", 1408), ("eb", 2048), ("zt", 848), ("ident", 128), ("jcol", 128),
-               ("iot", C), ("j16", C), ("j4", C), ("mask16", C), ("mask4", C), ("seg16", C), ("seg4", C), ("masku", 112),
-               ("mf0", C), ("mf1", C), ("mb0", C), ("mb1", C), ("rowq", C), ("rowm", C), ("rowqi", C), ("wA", C), ("wB", C),
-               ("mg", C), ("sc", C), ("sc4", C), ("pu", 112), ("pus", 112), ("nu", C), ("sg", C), ("tab", 16), ("pa", 28), ("ag", 28)):
+               ("wt", 1408), ("eb", 520), ("zt", 512), ("ident", 128), ("jcol", 128), ("R", 8 * C),
+               ("iot", C), ("j4", 16), ("seg16", C), ("seg4", C), ("sa", 32), ("sb", 32), ("sp", 32),
+               ("rowq", C), ("rowm", C), ("rowqi", C), ("rowt", C), ("arow", C), ("brow", C), ("agrow", C), ("df", C), ("nuF", C), ("nuB", C),
+               ("mg", C), ("sc", C), ("sn", C), ("sc4", C), ("sg", C)):
     SCRATCH[_n] = ("sbuf", [128, _w], BF)
 for _n, _w in (("uc", 128), ("uq", 128), ("vq", 128), ("wq", 512), ("xc", C), ("vc", C), ("ebc", 512), ("shc", 352), ("zc", 212),
                ("hc0", C), ("hc1", C), ("hc2", C), ("lc0", C), ("lc1", C), ("lc2", C)):
     SCRATCH[_n] = ("sbuf", [128, _w], MX)
     SCRATCH[_n + "p"] = ("sbuf", [128, _w], U8)
-for _n, _w in (("qU", 28), ("mU", 28), ("loU", 28), ("qiU", 28), ("loqU", 28), ("lf", 224), ("lb", 224), ("l4", 112), ("p16", 28),
-               ("a8", 28), ("loP", 28), ("loqP", 28), ("dU", 28), ("ulist", 8), ("qoU", 28)):
+for _n, _w in (("qU", 28), ("mU", 28), ("loF", 28), ("loB", 28), ("qiU", 28), ("ls", 224), ("l4", 112), ("p16", 28),
+               ("a8r", 28), ("a8", 28), ("ulist", 8), ("qoU", 28), ("rep", 28)):
     SCRATCH[_n] = ("sbuf", [128, _w], U16)
-for _n, _w in (("iwb", 224), ("iw", 28), ("qF", 224), ("dF", 224), ("qB", 224), ("dB", 224), ("t1", 112), ("t2", 112), ("t3", 28), ("t4", 28),
-               ("mF", 28), ("t5", 28), ("t6", 28), ("t7", 28), ("t8", 28), ("t9", 28), ("lo", 28), ("loq", 28), ("dhF", 28), ("qhF", 28), ("dhB", 28), ("qhB", 28), ("cp", 1), ("cp16", 1), ("cphi", 1), ("cq", 4), ("ysb", C), ("qrow", C)):
+for _n, _w in (("iwb", 28), ("iw", 28), ("tabC", 56), ("tC", 56), ("wF", 56), ("wB", 56), ("hiF", 56), ("lwF", 56), ("hiB", 56), ("lwB", 56), ("uu", 56), ("dF", 84), ("dB", 84), ("t3", 28), ("t4", 28),
+               ("hq", 28), ("tq", 28), ("lo", 28), ("dq", 28), ("cq", 20), ("ysb", C), ("qrow", C)):
     SCRATCH[_n] = ("sbuf", [128, _w], F32)
-for _n, _w in (("gqi", 28), ("gmi", 28), ("li", 84), ("pi", 4), ("uli", 16)):
+for _n, _w in (("gqi", 28), ("gmi", 28), ("li", 56), ("pi", 8), ("uli", 16)):
     SCRATCH[_n] = ("sbuf", [128, _w], I32)
-SCRATCH["dl"] = ("dram", [32, 4, 28], U16)
 for _k in range(8):
     SCRATCH["P%d" % _k] = ("psum", [128, 512], F32)
-SEMAPHORES = ["v", "s", "t", "gc"] + ["d%d" % k for k in range(40)] + ["arr%d" % k for k in range(3)] + ["snt%d" % k for k in range(3)]
+SEMAPHORES = ["v", "s", "t", "gc"] + ["d%d" % k for k in range(40)] + ["arr%d" % k for k in range(9)] + ["snt"]
 
 
 def rank_program(g, core, T, topo):
@@ -116,14 +117,24 @@ def rank_program(g, core, T, topo):
     def scan(reads, writes, out, seg, a):
         op("v", reads, writes, lambda: g.vector.tensor_tensor_scan(out, seg, a, 0.0, A.mult, A.add))
 
+    def both(key):
+        return [key + "v", key + "s"]
+
+    def gather(out, o, okey, win, wkeys, lst, l0, lkeys, nv):
+        if nv:
+            cp(wkeys + lkeys, both(okey) if nv == 28 else [okey + "v"], out[:, o:o + 16 * nv], win.indirect(lst[:, l0:l0 + nv]))
+        if nv < 28:
+            act(wkeys + lkeys, both(okey) if nv == 0 else [okey + "s"], out[:, o + 16 * nv:o + C], win.indirect(lst[:, l0 + nv:l0 + 28]))
+
     dma("y", [(T.gqi[:], T.gq[:])], [], ["gqi"])
     dma("y", [(T.gmi[:], T.gm[:])], [], ["gmi"])
-    dma("y", [(T.ut[:], T.u[:])], [], ["ut"])
-    dma("s", [(T.x0[:, 0:4 * CA], T.x[:, 0:4 * CA])], [], ["x0A"])
-    dma("s", [(T.x0[:, 4 * CA:], T.x[:, 4 * CA:])], [], ["x0B"])
-    dma("y", [(T.vv[:], T.v[:])], [], ["vv"])
+    dma("s", [(T.ut[:], T.u[:])], [], ["ut"])
+    for k, (a, b) in enumerate(PARTS):
+        dma("ysy"[k], [(T.x0[:, 4 * a:4 * b], T.x[:, 4 * a:4 * b])], [], ["x0%d" % k])
+    need("y", W["x02"])
     dma("y", [(T.wq[:].bitcast(dt.uint8), T.wc[:])], [], ["wqc"])
     dma("y", [(T.wqp[:], T.ws[:])], [], ["wqp"])
+    dma("y", [(T.vv[:], T.v[:])], [], ["vv"])
 
     def iota(key, out, pat, base, cm, flag=True):
         if flag:
@@ -131,128 +142,156 @@ def rank_program(g, core, T, topo):
         else:
             op("g", [], [key], lambda: g.iota(out, pat, base, cm))
     iota("pi", T.pi[:, 0:1], [[0, 1]], 0, 1, False)
-    iota("uli", T.uli[:, 0:8], [[16, 8]], -16, 0, False)
-    iota("j16", T.j16[:], [[0, 28], [1, 16]], 0, 0)
     iota("jcol", T.jcol[:], [[1, 128]], 0, 0)
+    iota("j4", T.j4[:], [[0, 4], [1, 4]], 0, 0)
     iota("iot", T.iot[:], [[1, C]], -224, 0)
-    iota("iwb", T.iwb[:], [[0, 8], [16, 28]], 0, 0)
-    iota("j4", T.j4[:], [[0, 112], [1, 4]], 0, 0)
-    cplo, c896, cpt, cpp = (T.cq[:, k:k + 1] for k in range(4))
+    iota("iwb", T.iwb[:], [[16, 28]], 0, 0)
+    iota("uli", T.uli[:, 0:8], [[16, 8]], -16, 0, False)
+    cp_, c16, c16n, kap, kaph, kap2, cphi, cphin, k4, c896, cg, cgk, cg7, c8, kin, ctmp, kq = (T.cq[:, k:k + 1] for k in range(17))
+    fill(["z"], T.zt[:], 0.0)
     ts(["pi"], ["pi1"], T.pi[:, 1:2], T.pi[:, 0:1], 15, A.bitwise_and)
+    cp(["pi"], ["cp"], cp_, T.pi[:, 0:1])
+    ts(["pi"], ["pi4"], T.pi[:, 4:5], T.pi[:, 0:1], 4, A.arith_shift_right)
     ts(["pi"], ["pi2"], T.pi[:, 2:3], T.pi[:, 0:1], 2, A.arith_shift_right, 3, A.bitwise_and)
     ts(["pi"], ["pi3"], T.pi[:, 3:4], T.pi[:, 0:1], 3, A.bitwise_and)
+    cp(["pi1"], ["c16"], c16, T.pi[:, 1:2])
+    ts(["pi1"], ["c16n"], c16n, T.pi[:, 1:2], 1.0, A.add)
+    ts(["jcol", "cp"], ["ident"], T.ident[:], T.jcol[:], cp_, A.is_equal)
+    ts(["pi1"], ["kap"], kap, T.pi[:, 1:2], 15.0, A.is_equal, 1 / K, A.max)
+    cp(["pi2"], ["cphi"], cphi, T.pi[:, 2:3])
+    ts(["pi2"], ["cphin"], cphin, T.pi[:, 2:3], 1.0, A.add)
+    ts(["jcol", "c16"], ["sa"], T.sa[:, 0:16], T.jcol[:, 0:16], c16, A.not_equal)
+    ts(["jcol", "c16n"], ["sb"], T.sb[:, 0:16], T.jcol[:, 0:16], c16n, A.is_equal, K, A.mult)
+    ts(["z", "c16"], ["rep"], T.rep[:], T.zt[:, 0:28], c16, A.add)
+    ts(["j4", "cphi"], ["sa4"], T.sa[:, 16:32], T.j4[:], cphi, A.not_equal)
+    ts(["j4", "cphin"], ["sb4"], T.sb[:, 16:32], T.j4[:], cphin, A.is_equal, K, A.mult)
+    fill(["eb"], T.eb[:], 0.0)
+    tt(["sa", "sb", "sa4", "sb4"], ["sp"], T.sp[:], T.sa[:], T.sb[:], A.max)
+    act(["z"], ["wt1"], T.wt[:, C:960], T.zt[:])
+    act(["z"], ["wt0"], T.wt[:, 0:C], T.zt[:, 0:C])
+    act(["z"], ["wt2"], T.wt[:, 960:1408], T.zt[:, 0:C])
+    for t in range(2):
+        act(["ident", "wt1"], ["wi%d" % t], T.wt[:, C + t:960:4], T.ident[:])
+    act(["sp", "rep"], ["seg16"], T.seg16[:], T.sp[:, 0:16].indirect(T.rep[:, 0:28]))
+    quant(["z"], ["zcr"], "zc", 84, 212, T.zt, 0)
+    cp(["ident", "eb"], ["ebi"], T.eb[:, 4:516:4], T.ident[:])
+    ts(["kap"], ["kaph"], kaph, kap, 0.5, A.mult)
+    ts(["kap"], ["kap2"], kap2, kap, -2.0, A.mult)
+    ts(["pi2"], ["kin"], kin, T.pi[:, 2:3], 3.0, A.is_equal, 1 / K, A.max)
+    ts(["pi3"], ["c896"], c896, T.pi[:, 3:4], 896.25, A.add)
+    ts(["pi4"], ["cg7"], cg7, T.pi[:, 4:5], 7.0, A.is_lt)
+    ts(["pi4"], ["ctmp"], ctmp, T.pi[:, 4:5], 7.0, A.is_equal, -224.0, A.mult)
+    ts(["pi4"], ["cg"], cg, T.pi[:, 4:5], 448.0, A.mult, 0.25, A.add)
+    ts(["pi4"], ["c8"], c8, T.pi[:, 4:5], -448.0, A.mult, 7 * 448.0, A.add)
+    ts(["pi1"], ["kq"], kq, T.pi[:, 1:2], 15.0, A.not_equal, 1 / K, A.max)
+    ts(["kin"], ["k4"], k4, kin, 4.0, A.mult)
+    fill(["tabC0"], T.tabC[:, 0:28], 224.25)
+    tt(["cg", "ctmp"], ["cgk"], cgk, cg, ctmp, A.add)
+    ts(["iwb", "c16"], ["iw"], T.iw[:], T.iwb[:], c16, A.add)
     ts(["uli"], ["uli2"], T.uli[:, 8:16], T.uli[:, 0:8], 127, A.bitwise_and)
-    cp(["pi"], ["cp"], T.cp[:], T.pi[:, 0:1])
-    cp(["pi1"], ["cp16"], T.cp16[:], T.pi[:, 1:2])
-    cp(["pi2"], ["cphi"], T.cphi[:], T.pi[:, 2:3])
-    cp(["pi3"], ["cplo"], cplo, T.pi[:, 3:4])
-    cp(["uli2"], ["ulist"], T.ulist[:], T.uli[:, 8:16])
-    ts(["cplo"], ["c896"], c896, cplo, 896.0, A.add)
-    ts(["cplo"], ["cpt"], cpt, cplo, 4.0, A.mult, -224.0, A.add)
-    fill(["zt"], T.zt[:], 0.0)
-    fill(["wt"], T.wt[:], 0.0)
-    ts(["j16", "cp16"], ["mask16"], T.mask16[:], T.j16[:], T.cp16[:], A.is_equal)
-    ts(["j16"], ["seg16"], T.seg16[:], T.j16[:], 0.0, A.is_gt)
-    ts(["jcol", "cp"], ["ident"], T.ident[:], T.jcol[:], T.cp[:], A.is_equal)
-    ts(["jcol"], ["tab"], T.tab[:], T.jcol[:, 0:16], -2.0, A.mult, 1.0, A.add)
-    cp(["ident"], ["wt"], T.wt[:, 448:960:4], T.ident[:])
-    quant(["wt"], ["shc"], "shc", 0, 352, T.wt, 0)
-    quant(["zt"], ["zcr"], "zc", 84, 212, T.zt, 336)
-    ts(["iwb", "cp16"], ["iw"], T.iw[:], T.iwb[:, 0:28], T.cp16[:], A.add)
-    ts(["iwb", "cp16"], ["qF0", "qFr"], T.qF[:], T.iwb[:], T.cp16[:], A.add)
-    fill(["dF0", "dFr"], T.dF[:], 0.0)
+    quant(["wt0", "wt2", "wi0", "wi1"], ["shc"], "shc", 0, 352, T.wt, 0)
+
+    def scatter(a, b):
+        return lambda: cp(["iot", "qU"], ["rowqi"], T.rowqi[:, 0:C].indirect(T.qU[:, a:b]), T.iot[:, 16 * a:16 * b])
+
+    def ebq(b):
+        return lambda: quant(["ebi"], ["ebc%d" % b], "ebc", 128 * b, 128 * b + 128, T.eb, 4 - b)
 
     cp(["gqi"], ["qU"], T.qU[:], T.gqi[:])
-    act(["iot", "qU"], ["rowq"], T.rowq[:], T.iot[:, 0:C].indirect(T.qU[:, 0:28]))
-    cp(["gqi"], ["qF0"], T.qF[:, 0:28], T.gqi[:])
+    cp(["uli2"], ["ulist"], T.ulist[:], T.uli[:, 8:16])
+    ts(["gqi"], ["hq"], T.hq[:], T.gqi[:], 0.5, A.mult, -112.0, A.add)
+    ts(["iw", "cg7", "cgk"], ["tabC1"], T.tabC[:, 28:56], T.iw[:], cg7, A.mult, cgk, A.add)
+    gather(T.rowq, 0, "rowq", T.iot[:, 0:C], ["iot"], T.qU, 0, ["qU"], 14)
     cp(["gmi"], ["mU"], T.mU[:], T.gmi[:])
-    cp(["gmi"], ["mF"], T.mF[:], T.gmi[:])
-    dma("y", [(T.qF[16 * n:128, 28 * n:28 * n + 28], T.qF[0:128 - 16 * n, 0:28]) for n in range(1, 8)], ["qF0"], ["qFr"])
-    tt(["mF", "iw"], ["lo"], T.lo[:], T.mF[:], T.iw[:], A.min)
+    tt(["gmi", "iw"], ["lo"], T.lo[:], T.gmi[:], T.iw[:], A.min)
     quant(["ut"], ["uc"], "uc", 0, 128, T.ut, 0)
-    cp(["lo"], ["loU"], T.loU[:], T.lo[:])
-    tt(["rowq", "mU", "mask16"], ["mg"], T.mg[:], T.rowq[:, 0:C].indirect(T.mU[:, 0:28]), T.mask16[:], A.mult)
-    scan(["seg16", "mg"], ["sc"], T.sc[:], T.seg16[:], T.mg[:])
-    ts(["sc"], ["t6"], T.t6[:], T.sc[:, 15:C:16], 224.0, A.add)
-    tt(["t6", "qF0"], ["dF0"], T.dF[:, 0:28], T.t6[:], T.qF[:, 0:28], A.subtract)
-    dma("y", [(T.dF[16 * n:128, 28 * n:28 * n + 28], T.dF[0:128 - 16 * n, 0:28]) for n in range(1, 8)], ["dF0"], ["dFr"])
-    for a, b in ((0, 848), (848, 1696), (1696, 2048)):
-        act(["zt"], ["eb%d" % a], T.eb[:, a:b], T.zt[:, 0:b - a])
-    for b in range(4):
-        act(["ident", "eb0", "eb848", "eb1696"], ["ebi%d" % b], T.eb[:, 512 * b + b:512 * b + 512:4], T.ident[:])
+    gather(T.rowt, 0, "rowt", T.rowq[:, 0:C], both("rowq"), T.mU, 0, ["mU"], 14)
     cp(["uc", "ulist"], ["uqc"], T.uq[:, 0:128].bitcast(dt.uint32), T.uc[:, 0:128].bitcast(dt.uint32).indirect(T.ulist[:, 0:8]))
-    cp(["uc", "ulist"], ["uqs"], T.uqp[:, 0:128], T.ucp[:, 0:128].indirect(T.ulist[:, 0:8]))
+    act(["uc", "ulist"], ["uqs"], T.uqp[:, 0:128], T.ucp[:, 0:128].indirect(T.ulist[:, 0:8]))
 
-    def score(src, key, c, part):
-        a, b, bank = (0, CA, "P0") if part == "A" else (CA, C, "P3")
-        quant([key + part], [c + part], c, a, b, src, 4 * a)
-        mm(["uqc", "uqs", c + part], [bank], T[bank][:, 0:b - a], "uq", 0, c, a, b - a)
+    def tables(d):
+        w, dg, hi, lw = T["w" + d], T["d" + d], T["hi" + d], T["lw" + d]
+        return [
+            lambda: scan(["seg16"] + both("rowt"), ["sn"], T.sn[:], T.seg16[:], T.rowt[:]),
+            lambda: ts(["sn", "kaph"], ["tq"], T.tq[:], T.sn[:, 15:C:16], kaph, A.mult),
+            lambda: (tt(["tq", "hq"], ["wq" + d], w[:, 0:28], T.tq[:], T.hq[:], A.add),
+                     tt(["tq", "hq"], ["wd" + d], w[:, 28:56], T.tq[:], T.hq[:], A.subtract)),
+            lambda: (ts(["wq" + d, "wd" + d], ["li"], T.li[:], w[:], 1 / 16, A.mult),
+                     ts(["wd" + d, "kap"], ["dh" + d], dg[:, 56:84], w[:, 28:56], kap, A.mult)),
+            lambda: ts(["li"], ["hi" + d], hi[:], T.li[:], 16.0, A.mult),
+            lambda: (tt(["hi" + d, "wq" + d, "wd" + d], ["lw" + d], lw[:], w[:], hi[:], A.subtract),
+                     ts(["hi" + d, "kap"], ["dhi" + d], dg[:, 0:28], hi[:, 28:56], kap, A.mult)),
+            lambda: ts(["lw" + d, "kap"], ["dlo" + d], dg[:, 28:56], lw[:, 28:56], kap, A.mult),
+        ]
 
-    def sign(part):
-        a, b, bank = (0, CA, "P0") if part == "A" else (CA, C, "P3")
-        act([bank], ["sg" + part], T.sg[:, a:b], T[bank][:, 0:b - a], F.Sign, bias=-(2.0 ** -93))
+    def score(src, key, c, k):
+        a, b = PARTS[k]
+        quant([key + str(k)], [c + str(k)], c, a, b, src, 4 * a)
+        mm(["uqc", "uqs", c + str(k)], ["P%d" % k], T["P%d" % k][:, 0:b - a], "uq", 0, c, a, b - a)
 
-    def halve(src, key, a, b, piece):
-        act([key], ["xh%d" % piece], T.xh[:, a:b], src[:, a:b], F.Copy, scale=0.5)
+    def sign(k):
+        a, b = PARTS[k]
+        act(["P%d" % k], ["sg%d" % k], T.sg[:, a:b], T["P%d" % k][:, 0:b - a], F.Sign, bias=-(2.0 ** -93))
 
-    XH = ["xh0", "xh1", "xh2"]
-    score(T.x0, "x0", "xc", "A")
-    score(T.x0, "x0", "xc", "B")
-    sign("A")
-    sign("B")
-    quant(["vv"], ["vq"], "vq", 0, 128, T.vv, 0)
-    ts(["dF0"], ["dhF"], T.dhF[:], T.dF[:, 0:28], 0.5, A.mult)
-    tt(["dhF", "qF0"], ["qhF"], T.qhF[:], T.dhF[:], T.qF[:, 0:28], A.add)
-    quant(["ebi0", "ebi1", "ebi2", "ebi3"], ["ebc"], "ebc", 0, 512, T.eb, 0)
-    halve(T.x0, "x0A", 0, 512, 0)
-    halve(T.x0, "x0A", 512, 4 * CA, 1)
-    halve(T.x0, "x0B", 4 * CA, 4 * C, 2)
-    tt(["cpt", "cphi"], ["cpp"], cpp, cpt, T.cphi[:], A.add)
+    def halve(src, key, k):
+        a, b = PARTS[k]
+        act([key + str(k)], ["xh%d" % k], T.xh[:, 4 * a:4 * b], src[:, 4 * a:4 * b], F.Copy, scale=0.5)
 
-    def late_constants():
-        ts(["j4", "cphi"], ["mask4"], T.mask4[:], T.j4[:], T.cphi[:], A.is_equal)
-        ts(["j4"], ["seg4"], T.seg4[:], T.j4[:], 0.0, A.is_gt)
-        ts(["j4", "cplo"], ["masku"], T.masku[:], T.j4[:, 0:112], cplo, A.is_equal)
-        ts(["iwb", "cpp"], ["ag0", "ag"], T.ag[:], T.iwb[:, 0:28], cpp, A.add)
+    def copy_half(ks):
+        a, b = PARTS[ks[0]][0], PARTS[ks[-1]][1]
+        dma("y", [(T.xg[:, 4 * a:4 * b], T.xh[:, 4 * a:4 * b])], ["xh%d" % k for k in ks], ["xg%d" % k for k in ks])
 
-    def turned(src, dst):
-        cp([src], ["li"], T.li[:, 0:28], T[src][:])
-        ts(["li"], ["li1"], T.li[:, 28:56], T.li[:, 0:28], 3, A.bitwise_and)
-        ts(["li"], ["li2"], T.li[:, 56:84], T.li[:, 0:28], 2, A.arith_shift_right, 3, A.bitwise_and)
-        tt(["li1", "li2"], ["t9"], T.t9[:], T.li[:, 28:56], T.li[:, 56:84], A.subtract)
-        ts(["t9"], ["t5"], T.t5[:], T.t9[:], 3.0, A.mult)
-        tt(["t5", src], ["t6"], T.t6[:], T.t5[:], T[src][:], A.add)
-        cp(["t6"], [dst], T[dst][:], T.t6[:])
+    tf = tables("F")
+    tf[0]()
+    gather(T.rowm, 0, "rowm", T.iot[:, 0:C], ["iot"], T.mU, 0, ["mU"], 0)
+    cp(["lo"], ["loF"], T.loF[:], T.lo[:])
+    scatter(0, 4)()
+    tf[1]()
+    scatter(4, 8)()
+    tf[2]()
+    score(T.x0, "x0", "xc", 0)
+    tf[3]()
+    score(T.x0, "x0", "xc", 1)
+    tf[4]()
+    halve(T.x0, "x0", 0)
+    score(T.x0, "x0", "xc", 2)
+    tf[5]()
+    for k in range(3):
+        sign(k)
+    scatter(8, 12)()
+    tf[6]()
 
-    def back_tables_1():
-        cp(["iot", "qU"], ["rowqi"], T.rowqi[:, 0:C].indirect(T.qU[:, 0:28]), T.iot[:])
+    def back_tables():
+        tb = tables("B")
+        return [
+            lambda: scan(["seg16", "rowqi"], ["sn"], T.sn[:], T.seg16[:], T.rowqi[:]),
+            lambda: (ts(["sn", "kap"], ["qiU"], T.qiU[:], T.sn[:, 15:C:16], kap, A.mult, 224.25, A.add),
+                     ts(["sn", "kaph"], ["hq"], T.hq[:], T.sn[:, 15:C:16], kaph, A.mult)),
+            lambda: gather(T.rowt, 0, "rowt", T.rowm[:, 0:C], both("rowm"), T.qiU, 0, ["qiU"], 0),
+            tb[0], tb[1],
+            lambda: (tt(["tq", "hq"], ["lo"], T.lo[:], T.tq[:], T.hq[:], A.min), tb[2]()),
+            lambda: (ts(["lo"], ["loB"], T.loB[:], T.lo[:], 2.0, A.mult, 224.25, A.add), tb[3]()),
+        ] + tb[4:]
 
-    def back_tables_2():
-        tt(["rowqi", "mask16"], ["mg"], T.mg[:], T.rowqi[:], T.mask16[:], A.mult)
-        scan(["seg16", "mg"], ["sc"], T.sc[:], T.seg16[:], T.mg[:])
-        ts(["sc"], ["qiU"], T.qiU[:], T.sc[:, 15:C:16], 224.0, A.add)
-        ts(["sc"], ["qB0"], T.qB[:, 0:28], T.sc[:, 15:C:16], 224.0, A.add)
-        dma("y", [(T.qB[0:128 - 16 * n, 28 * n:28 * n + 28], T.qB[16 * n:128, 0:28]) for n in range(1, 8)], ["qB0"], ["qBr"])
-        tt(["rowm", "qiU", "mask16"], ["mg"], T.mg[:], T.rowm[:, 0:C].indirect(T.qiU[:, 0:28]), T.mask16[:], A.mult)
-        scan(["seg16", "mg"], ["sc"], T.sc[:], T.seg16[:], T.mg[:])
-        ts(["sc"], ["t7"], T.t7[:], T.sc[:, 15:C:16], 224.0, A.add)
-        tt(["t7", "qB0"], ["dB0"], T.dB[:, 0:28], T.t7[:], T.qB[:, 0:28], A.subtract)
-        dma("y", [(T.dB[0:128 - 16 * n, 28 * n:28 * n + 28], T.dB[16 * n:128, 0:28]) for n in range(1, 8)], ["dB0"], ["dBr"])
-        tt(["t7", "qB0"], ["loq"], T.loq[:], T.t7[:], T.qB[:, 0:28], A.min)
-        ts(["dB0"], ["dhB"], T.dhB[:], T.dB[:, 0:28], 0.5, A.mult)
-        cp(["loq"], ["loqU"], T.loqU[:], T.loq[:])
-        tt(["dhB", "qB0"], ["qhB"], T.qhB[:], T.dhB[:], T.qB[:, 0:28], A.add)
-
-    def spread(lo, mask, lst, q, d, way):
-        tt(["sgA", "sgB", lo, mask], ["mg"], T.mg[:], T.sg[:, 0:C].indirect(T[lo][:, 0:28]), T[mask][:], A.mult)
-        scan(["seg16", "mg"], ["sc"], T.sc[:], T.seg16[:], T.mg[:])
-        dh, qh = ("dhF", "qhF") if lst == "lf" else ("dhB", "qhB")
-        ts(["sc"], ["zt"], T.zt[:, 336:448:4], T.sc[:, 15:C:16], 0.0, A.is_gt)
-        tt(["sc", dh], ["t3"], T.t3[:], T.sc[:, 15:C:16], T[dh][:], A.mult)
-        quant(["zt"], ["zc"], "zc", 0, 128, T.zt, 0)
-        tt(["t3", qh], ["t4"], T.t4[:], T.t3[:], T[qh][:], A.add)
-        cp(["t4"], [lst + "o"], T[lst][:, 0:28], T.t4[:])
-        for bank, ns in (("P1", (1, 2, 3)), ("P2", (4, 5, 6, 7))):
+    def chain(d, way, shares, vgap, sgap):
+        def gap(name):
+            for f in vgap.get(name, []) + sgap.get(name, []):
+                f()
+        dg, w = T["d" + d], T["w" + d]
+        gather(T.mg, 0, "mg", T.sg[:, 0:C], ["sg0", "sg1", "sg2"], T["lo" + d], 0, ["lo" + d], shares[0])
+        gap("signs")
+        scan(["seg16"] + both("mg"), ["sc"], T.sc[:], T.seg16[:], T.mg[:])
+        gap("scan")
+        s = T.sc[:, 15:C:16]
+        tt(["sc", "dh" + d], ["t3"], T.t3[:], s, dg[:, 56:84], A.mult)
+        tt(["sc", "dhi" + d], ["u0"], T.uu[:, 0:28], s, dg[:, 0:28], A.mult)
+        tt(["sc", "dlo" + d], ["u1"], T.uu[:, 28:56], s, dg[:, 28:56], A.mult)
+        tt(["t3", "wq" + d], ["t4"], T.t4[:], T.t3[:], w[:, 0:28], A.add)
+        tt(["u0", "hi" + d], ["z0", "z"], T.zt[:, 336:C:4], T.uu[:, 0:28], T["hi" + d][:, 0:28], A.add)
+        tt(["u1", "lw" + d], ["z1"], T.zt[:, 337:C:4], T.uu[:, 28:56], T["lw" + d][:, 0:28], A.add)
+        ts(["t4"], ["ls0"], T.ls[:, 0:28], T.t4[:], 224.25, A.add)
+        quant(["z0", "z1"], ["zc"], "zc", 0, 128, T.zt, 0)
+        for bank, ns in (("P0", (1,)), ("P1", (2, 3, 4, 5)), ("P2", (6, 7))):
             need("t", deps(["zc", "zcr", "shc"], [bank]))
             for n in ns:
                 s0, z0 = 112 + way * 16 * n, 84 - 28 * (n - ns[0])
@@ -260,174 +299,183 @@ def rank_program(g, core, T, topo):
             count["t"] = count.get("t", 0) + 1
             i.then_inc(T.sem["t"], 1)
             done(("t", count["t"], dict(known["t"])), ["zc", "zcr", "shc"], [bank])
+        gap("own")
+        gather(T.R, 0, "R0", T.iot[:, 0:C], ["iot"], T.ls, 0, ["ls0"], shares[1])
+        ts(["P0"], ["ls1"], T.ls[:, 28:56], T.P0[:, 0:28], 224.25, A.add)
+        gap(0)
+        for n in range(1, 8):
+            lk = "ls%d" % (1 if n == 1 else 2 if n < 6 else 6)
+            if d == "F" and n == 7:
+                gather(T.arow, 0, "arow", T.R[:, 0:7 * C], [k for i in range(7) for k in both("R%d" % i)], T.ls, 196, [lk], shares[8])
+            else:
+                gather(T.R, n * C, "R%d" % n, T.R[:, (n - 1) * C:n * C], both("R%d" % (n - 1)), T.ls, 28 * n, [lk], shares[1 + n])
+            if n == 1:
+                ts(["P1"], ["ls2"], T.ls[:, 56:168], T.P1[:, 0:112], 224.25, A.add)
+            if n == 2 and d == "B":
+                ts(["P2"], ["ls6"], T.ls[:, 168:224], T.P2[:, 0:56], 224.25, A.add)
+            if n == 3 and d == "F":
+                tt(["P2", "tabC0", "tabC1"], ["tC"], T.tC[:], T.P2[:, 0:56], T.tabC[:], A.add)
+            if n == 4 and d == "F":
+                cp(["tC"], ["ls6"], T.ls[:, 168:224], T.tC[:])
+            gap(n)
+        row = "arow"
+        if d == "B":
+            gather(T.brow, 0, "brow", T.R[:, 0:8 * C], [k for i in range(8) for k in both("R%d" % i)], T.a8, 0, ["a8"], shares[9])
+            gap(8)
+            row = "brow"
+        scan(["seg4"] + both(row), ["sc4"], T.sc4[:], T.seg4[:], T[row][:])
+        gap("scan4")
+        ts(["sc4", "k4", "c896"], ["l4"], T.l4[:], T.sc4[:, 3:C:4], k4, A.mult, c896, A.add)
+        gap("l4")
 
-    def prep(k, part, lst, q, d):
-        bank, a, n = ("P1", 28, 84) if part == "A" else ("P2", 112, 112)
-        if k == 0:
-            tt([bank, d + "r"], ["t1"], T.t1[:, 0:n], T[bank][:, 0:n], T[d][:, a:a + n], A.mult)
-        if k == 1:
-            tt(["t1", q + "r"], ["t2"], T.t2[:, 0:n], T.t1[:, 0:n], T[q][:, a:a + n], A.add)
-        if k == 2:
-            cp(["t2"], [lst + part], T[lst][:, a:a + n], T.t2[:, 0:n])
+    def move(out, okey, win, wkeys, base, bkey, k):
+        a, b = PARTS[k]
+        tt(wkeys + ["l4", bkey + str(k)], [okey + str(k)], out[:, 4 * a:4 * b], win[:, 0:4 * C].indirect(T.l4[:, a // 4:b // 4]), base[:, 4 * a:4 * b], A.add)
 
-    def gather(i, lst, nv):
-        src = "iot" if i == 0 else ("wB", "wA")[i % 2]
-        dst = ("wA", "wB")[i % 2]
-        key = ["iot"] if i == 0 else [src + "v", src + "s"]
-        lk = lst + ("o" if i == 0 else "A" if i < 4 else "B")
-        if nv:
-            cp(key + [lk], [dst + "v"] + ([dst + "s"] if nv == 28 else []), T[dst][:, 0:16 * nv], T[src][:, 0:C].indirect(T[lst][:, 28 * i:28 * i + nv]))
-        if nv < 28:
-            act(key + [lk], [dst + "s"] + ([dst + "v"] if nv == 0 else []), T[dst][:, 16 * nv:C], T[src][:, 0:C].indirect(T[lst][:, 28 * i + nv:28 * i + 28]))
+    def turn_row(d):
+        act(["df0", "df1", "lo" + d, "kap", "kap2"], ["nu" + d], T["nu" + d][:], T.df[:, 0:C].indirect(T["lo" + d][:, 0:28]), F.Identity, bias=kap, scale=kap2)
 
-    def offsets(src, off, offkeys):
-        tt([src + "v", src + "s", "mask4"] + offkeys, ["mg"], T.mg[:], T[src][:, 0:C].indirect(off), T.mask4[:], A.mult)
-        scan(["seg4", "mg"], ["sc4"], T.sc4[:], T.seg4[:], T.mg[:])
-        ts(["sc4", "c896"], ["l4"], T.l4[:], T.sc4[:, 3:C:4], 4.0, A.mult, c896, A.add)
+    def turn_scan(d):
+        scan(["seg16", "nu" + d], ["sn"], T.sn[:], T.seg16[:], T["nu" + d][:])
 
-    def move(out, okey, win, wkeys, base, bkeys, part):
-        a, b = (0, CA) if part == "A" else (CA, C)
-        tt(wkeys + ["l4"] + bkeys, [okey + part], out[:, 4 * a:4 * b], win[:, 0:4 * C].indirect(T.l4[:, a // 4:b // 4]), base[:, 4 * a:4 * b], A.add)
+    def turn(d):
+        for k, name in enumerate(("dhi", "dlo", "dh")):
+            v = T["d" + d][:, 28 * k:28 * k + 28]
+            tt(["sn"], [name + d], v, v, T.sn[:, 15:C:16], A.mult)
 
-    mf, mb = "mask16", "mask16"
+    def differ(k):
+        tt(both("brow") + ["agrow", "ag0"], ["df%d" % k], T.df[:, 224 * k:224 * k + 224], T.brow[:, 224 * k:224 * k + 224], T.agrow[:, 224 * k:224 * k + 224], A.not_equal)
+
+    XH = ["xh0", "xh1", "xh2"]
+    DD = ["dd%d%d" % (h, b) for h in range(len(HRUNS)) for b in range(4)]
+    even = [14, 12] + [14] * 8
     for r in range(3):
         dst = T.cores[rank ^ STEP[r]]
         hc, lc = "hc%d" % r, "lc%d" % r
-        dma("y", [(T.xg[:], T.xh[:])], XH, ["xg"])
-        spread("loU", mf, "lf", "qF", "dF", -1)
-        gather(0, "lf", 0 if r == 0 else 4)
-        for k in range(3):
-            prep(k, "A", "lf", "qF", "dF")
+        src, skey = (T.x0, "x0") if r == 0 else (T.xt, "xt")
         if r == 0:
-            for k in range(3):
-                prep(k, "B", "lf", "qF", "dF")
-            for k in range(1, 7):
-                gather(k, "lf", 0)
-                if k == 2:
-                    act(["iwb", "cp16"], ["qB0", "qBr"], T.qB[:], T.iwb[:], F.Identity, bias=T.cp16[:])
-                    act(["wt"], ["dB0", "dBr"], T.dB[:], T.wt[:, 0:224])
-                    act(["iot", "mU"], ["rowm"], T.rowm[:], T.iot[:, 0:C].indirect(T.mU[:, 0:28]))
-            late_constants()
-            back_tables_1()
-            back_tables_2()
+            bt = back_tables()
+            vgap = {"signs": [scatter(12, 16)], "scan": [scatter(16, 20)], "own": [scatter(20, 24)], 0: [scatter(24, 28)], 1: [bt[0]], 2: [bt[1]], 3: [bt[2]],
+                    4: [bt[3]], 5: [bt[4]], 6: [bt[5]], 7: [bt[6]], "scan4": [bt[7]], "l4": [bt[8]]}
+            sgap = {"signs": [lambda: halve(src, skey, 1), lambda: halve(src, skey, 2), lambda: copy_half([0, 1, 2])],
+                    5: [lambda: act(["sp", "rep"], ["seg4"], T.seg4[:], T.sp[:, 16:32].indirect(T.rep[:, 0:28]))]}
+            shares = [14, 12, 14, 14, 14, 26, 14, 26, 14]
+            dma("y", [(T.agrow[0:16, :], T.iot[0:16, :])], ["iot"], ["ag0"])
         else:
-            gather(1, "lf", 10)
-            prep(0, "B", "lf", "qF", "dF")
-            gather(2, "lf", 8)
-            prep(1, "B", "lf", "qF", "dF")
-            gather(3, "lf", 10)
-            prep(2, "B", "lf", "qF", "dF")
-            gather(4, "lf", 0)
-            nxt = "mb%d" % (r % 2)
-            tt(["nu", "loqP", mb], [nxt], T[nxt][:], T.nu[:, 0:C].indirect(T.loqP[:, 0:28]), T[mb][:], A.mult)
-            mb = nxt
-            gather(5, "lf", 14)
-            gather(6, "lf", 14)
-        offsets("wA", T.lf[:, 196:224], ["lfB"])
-        move(T.vt, "vt", T.xh, XH, T.xg, ["xg"], "A")
-        score(T.vt, "vt", "vc", "A")
-        sign("A")
+            vgap = {3: [lambda: turn_scan("B")], 5: [lambda: turn("B")]}
+            sgap = {"signs": [lambda: halve(src, skey, 2), lambda: copy_half([2])]}
+            shares = even
+        chain("F", -1, shares, vgap, sgap)
+        dma("y", [(T.agrow[16:128, :], T.arow[0:112, :])], both("arow"), ["agrow"])
 
-        def layer(b, part):
-            a, e = (0, CA) if part == "A" else (CA, C)
+        def layer(h):
+            a, e = HRUNS[h]
+            for b in range(4):
+                bank = "P%d" % (4 + b)
+                mm(["wqc", "wqp"] + ["vc%d" % k for k in range(3) if a <= PARTS[k][0] < e], [bank], T[bank][:, 0:e - a], "wq", 128 * b, "vc", a, e - a)
+
+        def layer_out(h, b):
+            a, e = HRUNS[h]
             bank = "P%d" % (4 + b)
-            mm(["wqc", "wqp", "vc" + part], [bank], T[bank][:, 0:e - a], "wq", 128 * b, "vc", a, e - a)
-            act([bank], ["ht%d%s" % (b, part)], T.ht[:, 4 * a + b:4 * e:4], T[bank][:, 0:e - a], F.Copy, scale=0.03125)
-        layer(0, "A")
-        move(T.vt, "vt", T.xh, XH, T.xg, ["xg"], "B")
-        mm(["wqc", "wqp", "vcA"], ["P5"], T.P5[:, 0:CA], "wq", 128, "vc", 0, CA)
-        score(T.vt, "vt", "vc", "B")
-        sign("B")
-        act(["P5"], ["ht1A"], T.ht[:, 1:4 * CA:4], T.P5[:, 0:CA], F.Copy, scale=0.03125)
-        layer(2, "A")
-        layer(3, "A")
-        for b in range(4):
-            layer(b, "B")
-        tt(["sc4", "masku"], ["pu"], T.pu[:], T.sc4[:, 3:C:4], T.masku[:], A.mult)
-        scan(["seg4", "pu"], ["pus"], T.pus[:], T.seg4[:, 0:112], T.pu[:])
-        ts(["pus"], ["p16"], T.p16[:], T.pus[:, 3:112:4], 224.0, A.add)
-        cp(["pus"], ["pa"], T.pa[:], T.pus[:, 3:112:4])
-        dma("y", [(T.dl[k:32:4, :, :], T.p16[k:128:4, :]) for k in range(4)], ["p16"], ["dl"])
-        dma("y", [(T.ag[16:128, :], T.pa[0:112, :])], ["pa"], ["ag"])
-        dma("y", [(T.a8[16 * k:16 * k + 16, :], T.dl[28:32, :, :]) for k in range(8)], ["dl"], ["a8"])
-        spread("loqU", mb, "lb", "qB", "dB", 1)
-        quant(["ht%d%s" % (b, k) for b in range(4) for k in "AB"], [hc], hc, 0, C, T.ht, 0)
-        need("g", W[hc])
-        rid, pid, _ = topo.addr(dst)
-        mask, ne = topo.mask(core, dst), len(topo.engines(core, dst))
-        arr, snt = "arr%d" % r, "snt%d" % r
-        g.remote_dma(out_ap=T[lc][:, 0:C].bitcast(dt.uint8), in_ap=T[hc][:, 0:C].bitcast(dt.uint8), remote_sem=T.sem[arr], local_sem=T.sem[snt], pid=pid, routing_id=rid, dma_engine_mask=mask)
-        g.remote_dma(out_ap=T[lc + "p"][:, 0:C], in_ap=T[hc + "p"][:, 0:C], remote_sem=T.sem[arr], local_sem=T.sem[snt], pid=pid, routing_id=rid, dma_engine_mask=mask)
-        count[arr] = count[snt] = 2 * ne
-        W[lc] = [(arr, 2 * ne, {})]
-        gather(0, "lb", 0)
-        for k in range(3):
-            prep(k, "A", "lb", "qB", "dB")
-        gather(1, "lb", 10)
-        prep(0, "B", "lb", "qB", "dB")
-        gather(2, "lb", 8)
-        prep(1, "B", "lb", "qB", "dB")
-        gather(3, "lb", 10)
-        prep(2, "B", "lb", "qB", "dB")
-        gather(4, "lb", 14)
-        gather(5, "lb", 14)
-        gather(6, "lb", 28)
-        gather(7, "lb", 28)
-        for b in range(4):
+            act([bank], ["ht%d%d" % (h, b)], T.ht[:, 4 * a + b:4 * e:4], T[bank][:, 0:e - a], F.Copy, scale=0.03125)
+
+        def send(h):
+            a, e = HRUNS[h]
+            quant(["ht%d%d" % (h, b) for b in range(4)], [hc + str(h)], hc, a, e, T.ht, 4 * a)
+            need("g", W[hc + str(h)])
+            rid, pid, _ = topo.addr(dst)
+            mask, ne = topo.mask(core, dst), len(topo.engines(core, dst))
+            arr = "arr%d" % (3 * r + h)
+            g.remote_dma(out_ap=T[lc][:, a:e].bitcast(dt.uint8), in_ap=T[hc][:, a:e].bitcast(dt.uint8), remote_sem=T.sem[arr], local_sem=T.sem["snt"], pid=pid, routing_id=rid, dma_engine_mask=mask)
+            g.remote_dma(out_ap=T[lc + "p"][:, a:e], in_ap=T[hc + "p"][:, a:e], remote_sem=T.sem[arr], local_sem=T.sem["snt"], pid=pid, routing_id=rid, dma_engine_mask=mask)
+            count[arr] = 2 * ne
+            count["snt"] = count.get("snt", 0) + 2 * ne
+            W[lc + str(h)] = [(arr, 2 * ne, {})]
+
+        def unpack(h):
+            a, e = HRUNS[h]
+            for b in range(4):
+                bank = "P%d" % (4 + b)
+                mm(["ebc%d" % b, lc + str(h)], [bank], T[bank][:, 0:e - a], "ebc", 128 * b, lc, a, e - a)
+
+        def unpack_out(h, b):
+            a, e = HRUNS[h]
             bank = "P%d" % (4 + b)
-            mm(["ebc", lc], [bank], T[bank][:, 0:C], "ebc", 128 * b, lc, 0, C)
-            act([bank], ["dd%d" % b], T.dd[:, b:4 * C:4], T[bank][:, 0:C])
-        offsets("wB", T.a8[:, 0:28], ["a8"])
-        tt(["sc4", "masku"], ["pu"], T.pu[:], T.sc4[:, 3:C:4], T.masku[:], A.mult)
-        scan(["seg4", "pu"], ["pus"], T.pus[:], T.seg4[:, 0:112], T.pu[:])
+            act([bank], ["dd%d%d" % (h, b)], T.dd[:, 4 * a + b:4 * e:4], T[bank][:, 0:e - a])
+
+        move(T.vt, "vt", T.xh, XH, T.xg, "xg", 0)
         if r == 0:
-            turned("lo", "loP")
-            turned("loq", "loqP")
-
-        def differ(k):
-            if k == 0:
-                tt(["pus", "ag", "ag0"], ["t8"], T.t8[:], T.pus[:, 3:112:4], T.ag[:], A.subtract)
-            else:
-                ts(["t8"], ["dU"], T.dU[:], T.t8[:], 0.0, A.not_equal)
-                act(["tab", "dU"], ["nu"], T.nu[:], T.tab[:, 0:16].indirect(T.dU[:, 0:28]))
-
-        def turn(old):
-            new = "mf%d" % (r % 2)
-            tt(["nu", "loP", old], [new], T[new][:], T.nu[:, 0:C].indirect(T.loP[:, 0:28]), T[old][:], A.mult)
-            return new
-        DD = ["dd%d" % b for b in range(4)]
+            bt[9]()
+        move(T.vt, "vt", T.xh, XH, T.xg, "xg", 1)
+        score(T.vt, "vt", "vc", 0)
+        layer(0)
+        sign(0)
+        for b in range(4):
+            layer_out(0, b)
+        move(T.vt, "vt", T.xh, XH, T.xg, "xg", 2)
+        score(T.vt, "vt", "vc", 1)
+        score(T.vt, "vt", "vc", 2)
+        layer(1)
+        sign(1)
+        sign(2)
+        scan(["seg16"] + both("arow"), ["sn"], T.sn[:], T.seg16[:], T.arow[:])
+        send(0)
+        ts(["sn", "kap"], ["p16"], T.p16[:], T.sn[:, 15:C:16], kap, A.mult, 224.25, A.add)
+        dma("y", [(T.a8r[16 * k:16 * k + 16, :], T.p16[112:128, :]) for k in range(8)], ["p16"], ["a8r"])
+        vgap = {"own": [lambda: send(1)], 6: [lambda: ts(["a8r", "c8"], ["a8"], T.a8[:], T.a8r[:], c8, A.add)],
+                "scan4": [lambda: differ(0)], "l4": [lambda: differ(1)]}
+        if r == 0:
+            vgap["signs"] = [ebq(0)]
+            vgap["scan"] = [ebq(1)]
+            vgap[0] = [ebq(2)]
+            vgap[1] = [ebq(3)]
+        if r == 1:
+            vgap[3] = [lambda: quant(["vv"], ["vq"], "vq", 0, 128, T.vv, 0)]
+        if r == 2:
+            vgap[3] = [lambda: ts(["dhF", "kq"], ["dq"], T.dq[:], T.dF[:, 56:84], -K, A.mult, kq, A.mult)]
+        sgap = {"signs": [lambda b=b: layer_out(1, b) for b in range(4)],
+                3: [lambda: unpack(0), lambda: unpack_out(0, 0)], 4: [lambda: unpack_out(0, 1)], 5: [lambda: unpack_out(0, 2)], 6: [lambda: unpack_out(0, 3), lambda: unpack(1)],
+                7: [lambda: unpack_out(1, 0)], 8: [lambda b=b: unpack_out(1, b) for b in (1, 2, 3)]}
+        chain("B", 1, [14, 10] + [14] * 8, vgap, sgap)
+        turn_row("F")
         if r < 2:
-            move(T.xt, "xt", T.dd, DD, T.vt, ["vtA"], "A")
-            differ(0)
-            score(T.xt, "xt", "xc", "A")
-            differ(1)
-            move(T.xt, "xt", T.dd, DD, T.vt, ["vtB"], "B")
-            score(T.xt, "xt", "xc", "B")
-            sign("A")
-            halve(T.xt, "xtA", 0, 512, 0)
-            sign("B")
-            halve(T.xt, "xtA", 512, 4 * CA, 1)
-            halve(T.xt, "xtB", 4 * CA, 4 * C, 2)
-            mf = turn(mf)
+            turn_row("B")
+            move(T.xt, "xt", T.dd, DD, T.vt, "vt", 0)
+            halve(T.xt, "xt", 0)
+            move(T.xt, "xt", T.dd, DD, T.vt, "vt", 1)
+            score(T.xt, "xt", "xc", 0)
+            halve(T.xt, "xt", 1)
+            copy_half([0, 1])
+            sign(0)
+            move(T.xt, "xt", T.dd, DD, T.vt, "vt", 2)
+            score(T.xt, "xt", "xc", 1)
+            score(T.xt, "xt", "xc", 2)
+            sign(1)
+            sign(2)
+            turn_scan("F")
+            turn("F")
         else:
-            differ(0)
-            differ(1)
-            for part, bank, a, b in (("A", "P0", 0, CA), ("B", "P3", CA, C)):
-                move(T.xt, "xt", T.dd, DD, T.vt, ["vt" + part], part)
-                if part == "A":
-                    mf = turn(mf)
-                    scan(["seg16", mf], ["sc"], T.sc[:], T.seg16[:], T[mf][:])
-                    ts(["sc"], ["t3"], T.t3[:], T.sc[:, 15:C:16], 0.0, A.is_lt)
-                    tt(["t3", "dF0"], ["t5"], T.t5[:], T.t3[:], T.dF[:, 0:28], A.mult)
-                    tt(["t5", "qF0"], ["t6"], T.t6[:], T.t5[:], T.qF[:, 0:28], A.add)
-                    cp(["t6"], ["qoU"], T.qoU[:], T.t6[:])
-                    act(["iot", "qoU"], ["qrow"], T.qrow[:], T.iot[:, 0:C].indirect(T.qoU[:, 0:28]), F.Identity, bias=224.0)
-                    dma("y", [(T.qo[:], T.qrow[0:128:16, :])], ["qrow"], ["qo"])
-                quant(["xt" + part], ["xc" + part], "xc", a, b, T.xt, 4 * a)
-                mm(["vq", "xc" + part], [bank], T[bank][:, 0:b - a], "vq", 0, "xc", a, b - a)
-                act([bank], ["y" + part], T.ysb[:, a:b], T[bank][:, 0:b - a])
-                dma("s", [(T.y[:, a:b], T.ysb[:, a:b])], ["y" + part], ["yo" + part])
-                dma("y", [(T.oc[:, 4 * a:4 * b], T.xc[:, a:b].bitcast(dt.uint8))] + [(T.osc[4 * k:4 * k + 4, a:b], T.xcp[32 * k:32 * k + 4, a:b]) for k in range(4)], ["xc" + part], ["oo" + part])
+            def out(k):
+                a, b = PARTS[k]
+                bank = "P%d" % k
+                quant(["xt%d" % k], ["xc%d" % k], "xc", a, b, T.xt, 4 * a)
+                dma("y", [(T.oc[:, 4 * a:4 * b], T.xc[:, a:b].bitcast(dt.uint8))], ["xc%d" % k], ["oc%d" % k])
+                mm(["vq", "xc%d" % k], [bank], T[bank][:, 0:b - a], "vq", 0, "xc", a, b - a)
+                act([bank], ["y%d" % k], T.ysb[:, a:b], T[bank][:, 0:b - a])
+                dma("s", [(T.y[:, a:b], T.ysb[:, a:b])], ["y%d" % k], ["yo%d" % k])
+            move(T.xt, "xt", T.dd, DD, T.vt, "vt", 0)
+            turn_scan("F")
+            move(T.xt, "xt", T.dd, DD, T.vt, "vt", 1)
+            tt(["sn", "dq"], ["t3"], T.t3[:], T.sn[:, 15:C:16], T.dq[:], A.mult)
+            out(0)
+            tt(["t3", "wqF"], ["t4"], T.t4[:], T.t3[:], T.wF[:, 0:28], A.add)
+            move(T.xt, "xt", T.dd, DD, T.vt, "vt", 2)
+            ts(["t4"], ["qoU"], T.qoU[:], T.t4[:], 224.25, A.add)
+            out(1)
+            out(2)
+            ts(["iot", "qoU"], ["qrow"], T.qrow[:], T.iot[:, 0:C].indirect(T.qoU[:, 0:28]), 224.0, A.add)
+            dma("y", [(T.osc[4 * k:4 * k + 4, :], T.xcp[32 * k:32 * k + 4, 0:C]) for k in range(4)], ["xc0", "xc1", "xc2"], ["osc"])
+            dma("y", [(T.qo[:], T.qrow[0:128:16, :])], ["qrow"], ["qo"])
     for sem in count:
         if known["g"].get(sem, 0) < count[sem]:
             g.wait_ge(T.sem[sem], count[sem])

@@ -4,17 +4,19 @@ import comms_topo
 
 STEP = [1, 2, 3]
 C = 448
-PARTS = [(0, 192), (192, 320), (320, C)]
-HRUNS = [(0, 192), (192, C)]
+PARTS = [(0, 128), (128, 320), (320, C)]
+HRUNS = [(0, 128), (128, C)]
+CUT = 192
 K = 2.0 ** 24
+M = 1.5 * 2.0 ** 27
 BF, F32, I32, U16, MX, U8 = "bfloat16", "float32", "int32", "uint16", "float8_e4m3fn_x4", "uint8"
 
 SCRATCH = {}
-for _n, _w in (("x0", 1792), ("xt", 1792), ("xh", 1792), ("xg", 1792), ("vt", 1792), ("ht", 1792), ("dd", 1792), ("ut", 512), ("vv", 512),
+for _n, _w in (("x0", 1792), ("xt", 1792), ("xh", 1792), ("xg", 1792), ("vt", 1792), ("ht", 1792), ("dd", 1792), ("tg", 1792), ("ut", 512), ("vv", 512),
                ("wt", 1408), ("eb", 520), ("zt", 512), ("ident", 128), ("jcol", 128), ("R", 8 * C),
                ("iot", C), ("j4", 16), ("seg16", C), ("seg4", C), ("sa", 32), ("sb", 32), ("sp", 32),
                ("rowq", C), ("rowm", C), ("rowqi", C), ("rowt", C), ("arow", C), ("brow", C), ("agrow", C), ("df", C), ("nuF", C), ("nuB", C),
-               ("mg", C), ("sc", C), ("sn", C), ("sc4", C), ("sg", C)):
+               ("mg", C), ("sc", C), ("sn", C), ("sm", C), ("sc4", C), ("sg", C)):
     SCRATCH[_n] = ("sbuf", [128, _w], BF)
 for _n, _w in (("uc", 128), ("uq", 128), ("vq", 128), ("wq", 512), ("xc", C), ("vc", C), ("ebc", 512), ("shc", 352), ("zc", 212),
                ("hc0", C), ("hc1", C), ("hc2", C), ("lc0", C), ("lc1", C), ("lc2", C)):
@@ -23,10 +25,11 @@ for _n, _w in (("uc", 128), ("uq", 128), ("vq", 128), ("wq", 512), ("xc", C), ("
 for _n, _w in (("qU", 28), ("mU", 28), ("loF", 28), ("loB", 28), ("qiU", 28), ("ls", 224), ("l4", 112), ("p16", 28),
                ("a8r", 28), ("a8", 28), ("ulist", 8), ("qoU", 28), ("rep", 28)):
     SCRATCH[_n] = ("sbuf", [128, _w], U16)
-for _n, _w in (("iwb", 28), ("iw", 28), ("tabC", 56), ("tC", 56), ("wF", 56), ("wB", 56), ("hiF", 56), ("lwF", 56), ("hiB", 56), ("lwB", 56), ("uu", 56), ("dF", 84), ("dB", 84), ("t3", 28), ("t4", 28),
-               ("hq", 28), ("tq", 28), ("lo", 28), ("dq", 28), ("cq", 20), ("ysb", C), ("qrow", C)):
+for _n, _w in (("iwb", 28), ("iw", 28), ("tabC", 56), ("tC", 56), ("wF", 28), ("wB", 28), ("hiF", 28), ("lwF", 28), ("hiB", 28), ("lwB", 28),
+               ("uu", 56), ("dF", 84), ("dB", 84), ("t3", 28), ("t4", 28),
+               ("hq", 56), ("tq", 56), ("lo", 28), ("dq", 28), ("cq", 20), ("ysb", C), ("qrow", C)):
     SCRATCH[_n] = ("sbuf", [128, _w], F32)
-for _n, _w in (("gqi", 28), ("gmi", 28), ("li", 56), ("pi", 8), ("uli", 16)):
+for _n, _w in (("gqi", 28), ("gmi", 28), ("pi", 8), ("uli", 16)):
     SCRATCH[_n] = ("sbuf", [128, _w], I32)
 for _k in range(8):
     SCRATCH["P%d" % _k] = ("psum", [128, 512], F32)
@@ -117,6 +120,9 @@ def rank_program(g, core, T, topo):
     def scan(reads, writes, out, seg, a):
         op("v", reads, writes, lambda: g.vector.tensor_tensor_scan(out, seg, a, 0.0, A.mult, A.add))
 
+    def cols(key, a, b):
+        return ["%s:%d" % (key, k) for k in range(a // 32, (b + 31) // 32)]
+
     def both(key):
         return [key + "v", key + "s"]
 
@@ -127,11 +133,11 @@ def rank_program(g, core, T, topo):
             act(wkeys + lkeys, both(okey) if nv == 0 else [okey + "s"], out[:, o + 16 * nv:o + C], win.indirect(lst[:, l0 + nv:l0 + 28]))
 
     dma("y", [(T.gqi[:], T.gq[:])], [], ["gqi"])
-    dma("y", [(T.gmi[:], T.gm[:])], [], ["gmi"])
-    dma("s", [(T.ut[:], T.u[:])], [], ["ut"])
+    dma("s", [(T.gmi[:], T.gm[:])], [], ["gmi"])
+    dma("y", [(T.ut[:], T.u[:])], [], ["ut"])
     for k, (a, b) in enumerate(PARTS):
-        dma("ysy"[k], [(T.x0[:, 4 * a:4 * b], T.x[:, 4 * a:4 * b])], [], ["x0%d" % k])
-    need("y", W["x02"])
+        dma("sys"[k], [(T.x0[:, 4 * a:4 * b], T.x[:, 4 * a:4 * b])], [], cols("x0", a, b))
+    need("y", W[cols("x0", C - 1, C)[0]])
     dma("y", [(T.wq[:].bitcast(dt.uint8), T.wc[:])], [], ["wqc"])
     dma("y", [(T.wqp[:], T.ws[:])], [], ["wqp"])
     dma("y", [(T.vv[:], T.v[:])], [], ["vv"])
@@ -147,7 +153,7 @@ def rank_program(g, core, T, topo):
     iota("iot", T.iot[:], [[1, C]], -224, 0)
     iota("iwb", T.iwb[:], [[16, 28]], 0, 0)
     iota("uli", T.uli[:, 0:8], [[16, 8]], -16, 0, False)
-    cp_, c16, c16n, kap, kaph, kap2, cphi, cphin, k4, c896, cg, cgk, cg7, c8, kin, ctmp, kq = (T.cq[:, k:k + 1] for k in range(17))
+    cp_, c16, c16n, kap, kaph, kap2, cphi, cphin, k4, c896, cg, cgk, cg7, c8, kin, ctmp, kq, km = (T.cq[:, k:k + 1] for k in range(18))
     fill(["z"], T.zt[:], 0.0)
     ts(["pi"], ["pi1"], T.pi[:, 1:2], T.pi[:, 0:1], 15, A.bitwise_and)
     cp(["pi"], ["cp"], cp_, T.pi[:, 0:1])
@@ -177,6 +183,7 @@ def rank_program(g, core, T, topo):
     cp(["ident", "eb"], ["ebi"], T.eb[:, 4:516:4], T.ident[:])
     ts(["kap"], ["kaph"], kaph, kap, 0.5, A.mult)
     ts(["kap"], ["kap2"], kap2, kap, -2.0, A.mult)
+    ts(["kap"], ["km"], km, kap, M, A.mult)
     ts(["pi2"], ["kin"], kin, T.pi[:, 2:3], 3.0, A.is_equal, 1 / K, A.max)
     ts(["pi3"], ["c896"], c896, T.pi[:, 3:4], 896.25, A.add)
     ts(["pi4"], ["cg7"], cg7, T.pi[:, 4:5], 7.0, A.is_lt)
@@ -198,80 +205,80 @@ def rank_program(g, core, T, topo):
         return lambda: quant(["ebi"], ["ebc%d" % b], "ebc", 128 * b, 128 * b + 128, T.eb, 4 - b)
 
     cp(["gqi"], ["qU"], T.qU[:], T.gqi[:])
-    cp(["uli2"], ["ulist"], T.ulist[:], T.uli[:, 8:16])
-    ts(["gqi"], ["hq"], T.hq[:], T.gqi[:], 0.5, A.mult, -112.0, A.add)
-    ts(["iw", "cg7", "cgk"], ["tabC1"], T.tabC[:, 28:56], T.iw[:], cg7, A.mult, cgk, A.add)
-    gather(T.rowq, 0, "rowq", T.iot[:, 0:C], ["iot"], T.qU, 0, ["qU"], 14)
     cp(["gmi"], ["mU"], T.mU[:], T.gmi[:])
+    cp(["uli2"], ["ulist"], T.ulist[:], T.uli[:, 8:16])
+    ts(["gqi"], ["hq"], T.hq[:, 0:28], T.gqi[:], 0.5, A.mult, -112.0, A.add)
+    gather(T.rowq, 0, "rowq", T.iot[:, 0:C], ["iot"], T.qU, 0, ["qU"], 14)
+    ts(["gqi", "kaph"], ["hk"], T.hq[:, 28:56], T.gqi[:], -224.0, A.add, kaph, A.mult)
     tt(["gmi", "iw"], ["lo"], T.lo[:], T.gmi[:], T.iw[:], A.min)
-    quant(["ut"], ["uc"], "uc", 0, 128, T.ut, 0)
+    ts(["iw", "cg7", "cgk"], ["tabC1"], T.tabC[:, 28:56], T.iw[:], cg7, A.mult, cgk, A.add)
     gather(T.rowt, 0, "rowt", T.rowq[:, 0:C], both("rowq"), T.mU, 0, ["mU"], 14)
-    cp(["uc", "ulist"], ["uqc"], T.uq[:, 0:128].bitcast(dt.uint32), T.uc[:, 0:128].bitcast(dt.uint32).indirect(T.ulist[:, 0:8]))
-    act(["uc", "ulist"], ["uqs"], T.uqp[:, 0:128], T.ucp[:, 0:128].indirect(T.ulist[:, 0:8]))
+    quant(["ut"], ["uc"], "uc", 0, 128, T.ut, 0)
+    cp(["lo"], ["loF"], T.loF[:], T.lo[:])
 
     def tables(d):
         w, dg, hi, lw = T["w" + d], T["d" + d], T["hi" + d], T["lw" + d]
         return [
             lambda: scan(["seg16"] + both("rowt"), ["sn"], T.sn[:], T.seg16[:], T.rowt[:]),
-            lambda: ts(["sn", "kaph"], ["tq"], T.tq[:], T.sn[:, 15:C:16], kaph, A.mult),
-            lambda: (tt(["tq", "hq"], ["wq" + d], w[:, 0:28], T.tq[:], T.hq[:], A.add),
-                     tt(["tq", "hq"], ["wd" + d], w[:, 28:56], T.tq[:], T.hq[:], A.subtract)),
-            lambda: (ts(["wq" + d, "wd" + d], ["li"], T.li[:], w[:], 1 / 16, A.mult),
-                     ts(["wd" + d, "kap"], ["dh" + d], dg[:, 56:84], w[:, 28:56], kap, A.mult)),
-            lambda: ts(["li"], ["hi" + d], hi[:], T.li[:], 16.0, A.mult),
-            lambda: (tt(["hi" + d, "wq" + d, "wd" + d], ["lw" + d], lw[:], w[:], hi[:], A.subtract),
-                     ts(["hi" + d, "kap"], ["dhi" + d], dg[:, 0:28], hi[:, 28:56], kap, A.mult)),
-            lambda: ts(["lw" + d, "kap"], ["dlo" + d], dg[:, 28:56], lw[:, 28:56], kap, A.mult),
+            lambda: (ts(["sn", "kaph"], ["tq"], T.tq[:, 0:28], T.sn[:, 15:C:16], kaph, A.mult),
+                     ts(["sn", "kaph", "kap"], ["tk"], T.tq[:, 28:56], T.sn[:, 15:C:16], kaph, A.mult, kap, A.mult)),
+            lambda: (tt(["tq", "hq"], ["wq" + d], w[:], T.tq[:, 0:28], T.hq[:, 0:28], A.add),
+                     tt(["tk", "hk"], ["dh" + d], dg[:, 56:84], T.tq[:, 28:56], T.hq[:, 28:56], A.subtract)),
+            lambda: (ts(["wq" + d], ["hi" + d], hi[:], w[:], M, A.add, -M, A.add),
+                     ts(["dh" + d, "km"], ["dhi" + d], dg[:, 0:28], dg[:, 56:84], km, A.add, km, A.subtract)),
+            lambda: (tt(["hi" + d, "wq" + d], ["lw" + d], lw[:], w[:], hi[:], A.subtract),
+                     tt(["dhi" + d, "dh" + d], ["dlo" + d], dg[:, 28:56], dg[:, 56:84], dg[:, 0:28], A.subtract)),
         ]
 
     def score(src, key, c, k):
         a, b = PARTS[k]
-        quant([key + str(k)], [c + str(k)], c, a, b, src, 4 * a)
+        quant(cols(key, a, b), [c + str(k)], c, a, b, src, 4 * a)
         mm(["uqc", "uqs", c + str(k)], ["P%d" % k], T["P%d" % k][:, 0:b - a], "uq", 0, c, a, b - a)
 
     def sign(k):
         a, b = PARTS[k]
         act(["P%d" % k], ["sg%d" % k], T.sg[:, a:b], T["P%d" % k][:, 0:b - a], F.Sign, bias=-(2.0 ** -93))
 
-    def halve(src, key, k):
-        a, b = PARTS[k]
-        act([key + str(k)], ["xh%d" % k], T.xh[:, 4 * a:4 * b], src[:, 4 * a:4 * b], F.Copy, scale=0.5)
+    def halve(src, key, a, b):
+        act(cols(key, a, b), cols("xh", a, b), T.xh[:, 4 * a:4 * b], src[:, 4 * a:4 * b], F.Copy, scale=0.5)
 
-    def copy_half(ks):
-        a, b = PARTS[ks[0]][0], PARTS[ks[-1]][1]
-        dma("y", [(T.xg[:, 4 * a:4 * b], T.xh[:, 4 * a:4 * b])], ["xh%d" % k for k in ks], ["xg%d" % k for k in ks])
+    def copy_half():
+        dma("y", [(T.xg[:, 0:4 * CUT], T.xh[:, 0:4 * CUT])], cols("xh", 0, CUT), cols("xg", 0, CUT))
 
     tf = tables("F")
     tf[0]()
+    cp(["uc", "ulist"], ["uqc"], T.uq[:, 0:128].bitcast(dt.uint32), T.uc[:, 0:128].bitcast(dt.uint32).indirect(T.ulist[:, 0:8]))
+    act(["uc", "ulist"], ["uqs"], T.uqp[:, 0:128], T.ucp[:, 0:128].indirect(T.ulist[:, 0:8]))
     gather(T.rowm, 0, "rowm", T.iot[:, 0:C], ["iot"], T.mU, 0, ["mU"], 0)
-    cp(["lo"], ["loF"], T.loF[:], T.lo[:])
-    scatter(0, 4)()
+    act(["sp", "rep"], ["seg4"], T.seg4[:], T.sp[:, 16:32].indirect(T.rep[:, 0:28]))
     tf[1]()
-    scatter(4, 8)()
+    scatter(0, 4)()
     tf[2]()
-    score(T.x0, "x0", "xc", 0)
+    scatter(4, 8)()
     tf[3]()
-    score(T.x0, "x0", "xc", 1)
+    score(T.x0, "x0", "xc", 0)
     tf[4]()
-    halve(T.x0, "x0", 0)
+    halve(T.x0, "x0", 0, 128)
+    score(T.x0, "x0", "xc", 1)
     score(T.x0, "x0", "xc", 2)
-    tf[5]()
     for k in range(3):
         sign(k)
     scatter(8, 12)()
-    tf[6]()
+    scatter(12, 16)()
 
     def back_tables():
         tb = tables("B")
         return [
             lambda: scan(["seg16", "rowqi"], ["sn"], T.sn[:], T.seg16[:], T.rowqi[:]),
             lambda: (ts(["sn", "kap"], ["qiU"], T.qiU[:], T.sn[:, 15:C:16], kap, A.mult, 224.25, A.add),
-                     ts(["sn", "kaph"], ["hq"], T.hq[:], T.sn[:, 15:C:16], kaph, A.mult)),
+                     ts(["sn", "kaph"], ["hq"], T.hq[:, 0:28], T.sn[:, 15:C:16], kaph, A.mult),
+                     ts(["sn", "kaph", "kap"], ["hk"], T.hq[:, 28:56], T.sn[:, 15:C:16], kaph, A.mult, kap, A.mult)),
             lambda: gather(T.rowt, 0, "rowt", T.rowm[:, 0:C], both("rowm"), T.qiU, 0, ["qiU"], 0),
             tb[0], tb[1],
-            lambda: (tt(["tq", "hq"], ["lo"], T.lo[:], T.tq[:], T.hq[:], A.min), tb[2]()),
+            lambda: (tt(["tq", "hq"], ["lo"], T.lo[:], T.tq[:, 0:28], T.hq[:, 0:28], A.min), tb[2]()),
             lambda: (ts(["lo"], ["loB"], T.loB[:], T.lo[:], 2.0, A.mult, 224.25, A.add), tb[3]()),
-        ] + tb[4:]
+            tb[4],
+        ]
 
     def chain(d, way, shares, vgap, sgap):
         def gap(name):
@@ -286,12 +293,12 @@ def rank_program(g, core, T, topo):
         tt(["sc", "dh" + d], ["t3"], T.t3[:], s, dg[:, 56:84], A.mult)
         tt(["sc", "dhi" + d], ["u0"], T.uu[:, 0:28], s, dg[:, 0:28], A.mult)
         tt(["sc", "dlo" + d], ["u1"], T.uu[:, 28:56], s, dg[:, 28:56], A.mult)
-        tt(["t3", "wq" + d], ["t4"], T.t4[:], T.t3[:], w[:, 0:28], A.add)
-        tt(["u0", "hi" + d], ["z0", "z"], T.zt[:, 336:C:4], T.uu[:, 0:28], T["hi" + d][:, 0:28], A.add)
-        tt(["u1", "lw" + d], ["z1"], T.zt[:, 337:C:4], T.uu[:, 28:56], T["lw" + d][:, 0:28], A.add)
+        tt(["t3", "wq" + d], ["t4"], T.t4[:], T.t3[:], w[:], A.add)
+        tt(["u0", "hi" + d], ["z0", "z"], T.zt[:, 336:C:4], T.uu[:, 0:28], T["hi" + d][:], A.add)
+        tt(["u1", "lw" + d], ["z1"], T.zt[:, 337:C:4], T.uu[:, 28:56], T["lw" + d][:], A.add)
         ts(["t4"], ["ls0"], T.ls[:, 0:28], T.t4[:], 224.25, A.add)
         quant(["z0", "z1"], ["zc"], "zc", 0, 128, T.zt, 0)
-        for bank, ns in (("P0", (1,)), ("P1", (2, 3, 4, 5)), ("P2", (6, 7))):
+        for bank, ns in (("P0", (1,)), ("P3", (2,)), ("P1", (3, 4, 5)), ("P2", (6, 7))):
             need("t", deps(["zc", "zcr", "shc"], [bank]))
             for n in ns:
                 s0, z0 = 112 + way * 16 * n, 84 - 28 * (n - ns[0])
@@ -302,20 +309,21 @@ def rank_program(g, core, T, topo):
         gap("own")
         gather(T.R, 0, "R0", T.iot[:, 0:C], ["iot"], T.ls, 0, ["ls0"], shares[1])
         ts(["P0"], ["ls1"], T.ls[:, 28:56], T.P0[:, 0:28], 224.25, A.add)
+        ts(["P3"], ["ls2"], T.ls[:, 56:84], T.P3[:, 0:28], 224.25, A.add)
         gap(0)
         for n in range(1, 8):
-            lk = "ls%d" % (1 if n == 1 else 2 if n < 6 else 6)
+            lk = "ls%d" % (n if n < 3 else 3 if n < 6 else 6)
             if d == "F" and n == 7:
                 gather(T.arow, 0, "arow", T.R[:, 0:7 * C], [k for i in range(7) for k in both("R%d" % i)], T.ls, 196, [lk], shares[8])
             else:
                 gather(T.R, n * C, "R%d" % n, T.R[:, (n - 1) * C:n * C], both("R%d" % (n - 1)), T.ls, 28 * n, [lk], shares[1 + n])
             if n == 1:
-                ts(["P1"], ["ls2"], T.ls[:, 56:168], T.P1[:, 0:112], 224.25, A.add)
+                ts(["P1"], ["ls3"], T.ls[:, 84:168], T.P1[:, 0:84], 224.25, A.add)
             if n == 2 and d == "B":
                 ts(["P2"], ["ls6"], T.ls[:, 168:224], T.P2[:, 0:56], 224.25, A.add)
-            if n == 3 and d == "F":
+            if n == 2 and d == "F":
                 tt(["P2", "tabC0", "tabC1"], ["tC"], T.tC[:], T.P2[:, 0:56], T.tabC[:], A.add)
-            if n == 4 and d == "F":
+            if n == 3 and d == "F":
                 cp(["tC"], ["ls6"], T.ls[:, 168:224], T.tC[:])
             gap(n)
         row = "arow"
@@ -328,9 +336,14 @@ def rank_program(g, core, T, topo):
         ts(["sc4", "k4", "c896"], ["l4"], T.l4[:], T.sc4[:, 3:C:4], k4, A.mult, c896, A.add)
         gap("l4")
 
-    def move(out, okey, win, wkeys, base, bkey, k):
-        a, b = PARTS[k]
-        tt(wkeys + ["l4", bkey + str(k)], [okey + str(k)], out[:, 4 * a:4 * b], win[:, 0:4 * C].indirect(T.l4[:, a // 4:b // 4]), base[:, 4 * a:4 * b], A.add)
+    def move(out, okey, win, wkeys, base, bkey, a, b):
+        tt(wkeys + ["l4"] + cols(bkey, a, b), cols(okey, a, b), out[:, 4 * a:4 * b], win[:, 0:4 * C].indirect(T.l4[:, a // 4:b // 4]), base[:, 4 * a:4 * b], A.add)
+
+    def fetch(win, wkeys, a, b):
+        act(wkeys + ["l4"], cols("tg", a, b), T.tg[:, 4 * a:4 * b], win[:, 0:4 * C].indirect(T.l4[:, a // 4:b // 4]))
+
+    def add(out, okey, base, bkey, a, b):
+        tt(cols("tg", a, b) + cols(bkey, a, b), cols(okey, a, b), out[:, 4 * a:4 * b], T.tg[:, 4 * a:4 * b], base[:, 4 * a:4 * b], A.add)
 
     def turn_row(d):
         act(["df0", "df1", "lo" + d, "kap", "kap2"], ["nu" + d], T["nu" + d][:], T.df[:, 0:C].indirect(T["lo" + d][:, 0:28]), F.Identity, bias=kap, scale=kap2)
@@ -346,25 +359,25 @@ def rank_program(g, core, T, topo):
     def differ(k):
         tt(both("brow") + ["agrow", "ag0"], ["df%d" % k], T.df[:, 224 * k:224 * k + 224], T.brow[:, 224 * k:224 * k + 224], T.agrow[:, 224 * k:224 * k + 224], A.not_equal)
 
-    XH = ["xh0", "xh1", "xh2"]
+    XH = cols("xh", 0, C)
     DD = ["dd%d%d" % (h, b) for h in range(len(HRUNS)) for b in range(4)]
-    even = [14, 12] + [14] * 8
     for r in range(3):
         dst = T.cores[rank ^ STEP[r]]
         hc, lc = "hc%d" % r, "lc%d" % r
         src, skey = (T.x0, "x0") if r == 0 else (T.xt, "xt")
         if r == 0:
             bt = back_tables()
-            vgap = {"signs": [scatter(12, 16)], "scan": [scatter(16, 20)], "own": [scatter(20, 24)], 0: [scatter(24, 28)], 1: [bt[0]], 2: [bt[1]], 3: [bt[2]],
-                    4: [bt[3]], 5: [bt[4]], 6: [bt[5]], 7: [bt[6]], "scan4": [bt[7]], "l4": [bt[8]]}
-            sgap = {"signs": [lambda: halve(src, skey, 1), lambda: halve(src, skey, 2), lambda: copy_half([0, 1, 2])],
-                    5: [lambda: act(["sp", "rep"], ["seg4"], T.seg4[:], T.sp[:, 16:32].indirect(T.rep[:, 0:28]))]}
-            shares = [14, 12, 14, 14, 14, 26, 14, 26, 14]
+            vgap = {"signs": [scatter(16, 20)], "scan": [scatter(20, 24)], "own": [scatter(24, 28)], 0: [bt[0]], 1: [bt[1]], 2: [bt[2]],
+                    4: [bt[3]], 5: [bt[4]], 6: [bt[5]], 7: [bt[6]], "scan4": [bt[7]]}
+            sgap = {"signs": [lambda: halve(src, skey, 128, CUT), copy_half, lambda: halve(src, skey, CUT, C)]}
+            shares = [14, 10, 14, 14, 26, 14, 14, 14, 14]
             dma("y", [(T.agrow[0:16, :], T.iot[0:16, :])], ["iot"], ["ag0"])
         else:
-            vgap = {3: [lambda: turn_scan("B")], 5: [lambda: turn("B")]}
-            sgap = {"signs": [lambda: halve(src, skey, 2), lambda: copy_half([2])]}
-            shares = even
+            vgap = {}
+            sgap = {"signs": [lambda: halve(src, skey, 0, CUT), copy_half, lambda: halve(src, skey, CUT, 352)],
+                    1: [lambda: halve(src, skey, 352, 384)], 2: [lambda: halve(src, skey, 384, 416)], 3: [lambda: halve(src, skey, 416, C)],
+                    7: [lambda: turn_row("B")]}
+            shares = [14, 12] + [14] * 7
         chain("F", -1, shares, vgap, sgap)
         dma("y", [(T.agrow[16:128, :], T.arow[0:112, :])], both("arow"), ["agrow"])
 
@@ -403,29 +416,36 @@ def rank_program(g, core, T, topo):
             bank = "P%d" % (4 + b)
             act([bank], ["dd%d%d" % (h, b)], T.dd[:, 4 * a + b:4 * e:4], T[bank][:, 0:e - a])
 
-        move(T.vt, "vt", T.xh, XH, T.xg, "xg", 0)
-        if r == 0:
-            bt[9]()
-        move(T.vt, "vt", T.xh, XH, T.xg, "xg", 1)
+        move(T.vt, "vt", T.xh, XH, T.xg, "xg", 0, 128)
+        fetch(T.xh, XH, CUT, 320)
+        fetch(T.xh, XH, 320, C)
+        move(T.vt, "vt", T.xh, XH, T.xg, "xg", 128, CUT)
         score(T.vt, "vt", "vc", 0)
         layer(0)
         sign(0)
         for b in range(4):
             layer_out(0, b)
-        move(T.vt, "vt", T.xh, XH, T.xg, "xg", 2)
+        add(T.vt, "vt", T.xh, "xh", CUT, 320)
+        add(T.vt, "vt", T.xh, "xh", 320, C)
         score(T.vt, "vt", "vc", 1)
         score(T.vt, "vt", "vc", 2)
         layer(1)
         sign(1)
         sign(2)
-        scan(["seg16"] + both("arow"), ["sn"], T.sn[:], T.seg16[:], T.arow[:])
         send(0)
-        ts(["sn", "kap"], ["p16"], T.p16[:], T.sn[:, 15:C:16], kap, A.mult, 224.25, A.add)
-        dma("y", [(T.a8r[16 * k:16 * k + 16, :], T.p16[112:128, :]) for k in range(8)], ["p16"], ["a8r"])
-        vgap = {"own": [lambda: send(1)], 6: [lambda: ts(["a8r", "c8"], ["a8"], T.a8[:], T.a8r[:], c8, A.add)],
+        if r:
+            turn_scan("B")
+        scan(["seg16"] + both("arow"), ["sm"], T.sm[:], T.seg16[:], T.arow[:])
+        if r:
+            turn("B")
+
+        def spread_a8():
+            ts(["sm", "kap"], ["p16"], T.p16[:], T.sm[:, 15:C:16], kap, A.mult, 224.25, A.add)
+            dma("y", [(T.a8r[16 * k:16 * k + 16, :], T.p16[112:128, :]) for k in range(8)], ["p16"], ["a8r"])
+        vgap = {"signs": [spread_a8], "own": [lambda: send(1)], 6: [lambda: ts(["a8r", "c8"], ["a8"], T.a8[:], T.a8r[:], c8, A.add)],
                 "scan4": [lambda: differ(0)], "l4": [lambda: differ(1)]}
         if r == 0:
-            vgap["signs"] = [ebq(0)]
+            vgap["signs"] += [ebq(0)]
             vgap["scan"] = [ebq(1)]
             vgap[0] = [ebq(2)]
             vgap[1] = [ebq(3)]
@@ -436,18 +456,16 @@ def rank_program(g, core, T, topo):
         sgap = {"signs": [lambda b=b: layer_out(1, b) for b in range(4)],
                 3: [lambda: unpack(0), lambda: unpack_out(0, 0)], 4: [lambda: unpack_out(0, 1)], 5: [lambda: unpack_out(0, 2)], 6: [lambda: unpack_out(0, 3), lambda: unpack(1)],
                 7: [lambda: unpack_out(1, 0)], 8: [lambda b=b: unpack_out(1, b) for b in (1, 2, 3)]}
-        chain("B", 1, [14, 10] + [14] * 8, vgap, sgap)
-        turn_row("F")
+        chain("B", 1, [14, 8, 14, 14, 14, 14, 14, 14, 14, 16], vgap, sgap)
         if r < 2:
-            turn_row("B")
-            move(T.xt, "xt", T.dd, DD, T.vt, "vt", 0)
-            halve(T.xt, "xt", 0)
-            move(T.xt, "xt", T.dd, DD, T.vt, "vt", 1)
+            fetch(T.dd, DD, CUT, 320)
+            fetch(T.dd, DD, 320, C)
+            turn_row("F")
+            move(T.xt, "xt", T.dd, DD, T.vt, "vt", 0, CUT)
+            add(T.xt, "xt", T.vt, "vt", CUT, 320)
             score(T.xt, "xt", "xc", 0)
-            halve(T.xt, "xt", 1)
-            copy_half([0, 1])
             sign(0)
-            move(T.xt, "xt", T.dd, DD, T.vt, "vt", 2)
+            add(T.xt, "xt", T.vt, "vt", 320, C)
             score(T.xt, "xt", "xc", 1)
             score(T.xt, "xt", "xc", 2)
             sign(1)
@@ -456,25 +474,26 @@ def rank_program(g, core, T, topo):
             turn("F")
         else:
             def out(k):
-                a, b = PARTS[k]
+                a, b = ((0, 224), (224, C))[k]
                 bank = "P%d" % k
-                quant(["xt%d" % k], ["xc%d" % k], "xc", a, b, T.xt, 4 * a)
+                quant(cols("xt", a, b), ["xc%d" % k], "xc", a, b, T.xt, 4 * a)
                 dma("y", [(T.oc[:, 4 * a:4 * b], T.xc[:, a:b].bitcast(dt.uint8))], ["xc%d" % k], ["oc%d" % k])
                 mm(["vq", "xc%d" % k], [bank], T[bank][:, 0:b - a], "vq", 0, "xc", a, b - a)
                 act([bank], ["y%d" % k], T.ysb[:, a:b], T[bank][:, 0:b - a])
                 dma("s", [(T.y[:, a:b], T.ysb[:, a:b])], ["y%d" % k], ["yo%d" % k])
-            move(T.xt, "xt", T.dd, DD, T.vt, "vt", 0)
+            turn_row("F")
+            fetch(T.dd, DD, 288, C)
+            move(T.xt, "xt", T.dd, DD, T.vt, "vt", 0, 224)
             turn_scan("F")
-            move(T.xt, "xt", T.dd, DD, T.vt, "vt", 1)
-            tt(["sn", "dq"], ["t3"], T.t3[:], T.sn[:, 15:C:16], T.dq[:], A.mult)
             out(0)
-            tt(["t3", "wqF"], ["t4"], T.t4[:], T.t3[:], T.wF[:, 0:28], A.add)
-            move(T.xt, "xt", T.dd, DD, T.vt, "vt", 2)
+            tt(["sn", "dq"], ["t3"], T.t3[:], T.sn[:, 15:C:16], T.dq[:], A.mult)
+            move(T.xt, "xt", T.dd, DD, T.vt, "vt", 224, 288)
+            tt(["t3", "wqF"], ["t4"], T.t4[:], T.t3[:], T.wF[:], A.add)
+            add(T.xt, "xt", T.vt, "vt", 288, C)
             ts(["t4"], ["qoU"], T.qoU[:], T.t4[:], 224.25, A.add)
             out(1)
-            out(2)
             ts(["iot", "qoU"], ["qrow"], T.qrow[:], T.iot[:, 0:C].indirect(T.qoU[:, 0:28]), 224.0, A.add)
-            dma("y", [(T.osc[4 * k:4 * k + 4, :], T.xcp[32 * k:32 * k + 4, 0:C]) for k in range(4)], ["xc0", "xc1", "xc2"], ["osc"])
+            dma("y", [(T.osc[4 * k:4 * k + 4, :], T.xcp[32 * k:32 * k + 4, 0:C]) for k in range(4)], ["xc0", "xc1"], ["osc"])
             dma("y", [(T.qo[:], T.qrow[0:128:16, :])], ["qrow"], ["qo"])
     for sem in count:
         if known["g"].get(sem, 0) < count[sem]:

@@ -4,7 +4,8 @@ import comms_topo
 
 STEP = [1, 2, 3]
 C = 448
-PARTS = [(0, 128), (128, 320), (320, C)]
+PARTS = [(0, 192), (192, 320), (320, C)]
+VPARTS = [(0, 128), (128, 320), (320, C)]
 HRUNS = [(0, 128), (128, C)]
 CUT = 192
 K = 2.0 ** 24
@@ -13,8 +14,8 @@ BF, F32, I32, U16, MX, U8 = "bfloat16", "float32", "int32", "uint16", "float8_e4
 
 SCRATCH = {}
 for _n, _w in (("x0", 1792), ("xt", 1792), ("xh", 1792), ("xg", 1792), ("vt", 1792), ("ht", 1792), ("dd", 1792), ("tg", 1792), ("ut", 512), ("vv", 512),
-               ("wt", 1408), ("eb", 520), ("zt", 512), ("ident", 128), ("jcol", 128), ("R", 8 * C),
-               ("iot", C), ("j4", 16), ("seg16", C), ("seg4", C), ("sa", 32), ("sb", 32), ("sp", 32),
+               ("wt", 1408), ("eb", 520), ("zt", 512), ("ident", 128), ("R", 5 * C), ("iot", 5 * C),
+               ("j16", 16), ("j4", 16), ("seg16", C), ("seg4", C), ("sa", 32), ("sb", 32), ("sp", 32),
                ("rowq", C), ("rowm", C), ("rowqi", C), ("rowt", C), ("arow", C), ("brow", C), ("agrow", C), ("df", C), ("nuF", C), ("nuB", C),
                ("mg", C), ("sc", C), ("sn", C), ("sm", C), ("sc4", C), ("sg", C)):
     SCRATCH[_n] = ("sbuf", [128, _w], BF)
@@ -23,11 +24,11 @@ for _n, _w in (("uc", 128), ("uq", 128), ("vq", 128), ("wq", 512), ("xc", C), ("
     SCRATCH[_n] = ("sbuf", [128, _w], MX)
     SCRATCH[_n + "p"] = ("sbuf", [128, _w], U8)
 for _n, _w in (("qU", 28), ("mU", 28), ("loF", 28), ("loB", 28), ("qiU", 28), ("ls", 224), ("l4", 112), ("p16", 28),
-               ("a8r", 28), ("a8", 28), ("ulist", 8), ("qoU", 28), ("rep", 28)):
+               ("a8r", 28), ("a8", 28), ("ulist", 8), ("qoU", 28), ("rep", 28), ("lf", 28)):
     SCRATCH[_n] = ("sbuf", [128, _w], U16)
-for _n, _w in (("iwb", 28), ("iw", 28), ("tabC", 56), ("tC", 56), ("wF", 28), ("wB", 28), ("hiF", 28), ("lwF", 28), ("hiB", 28), ("lwB", 28),
+for _n, _w in (("iwb", 28), ("iw", 28), ("tabC", 28), ("tC", 28), ("wF", 28), ("wB", 28), ("hiF", 28), ("lwF", 28), ("hiB", 28), ("lwB", 28),
                ("uu", 56), ("dF", 84), ("dB", 84), ("t3", 28), ("t4", 28),
-               ("hq", 56), ("tq", 56), ("lo", 28), ("dq", 28), ("cq", 20), ("ysb", C), ("qrow", C)):
+               ("hq", 56), ("tq", 56), ("lo", 28), ("dq", 28), ("cq", 32), ("ysb", C), ("qrow", C)):
     SCRATCH[_n] = ("sbuf", [128, _w], F32)
 for _n, _w in (("gqi", 28), ("gmi", 28), ("pi", 8), ("uli", 16)):
     SCRATCH[_n] = ("sbuf", [128, _w], I32)
@@ -120,6 +121,12 @@ def rank_program(g, core, T, topo):
     def scan(reads, writes, out, seg, a):
         op("v", reads, writes, lambda: g.vector.tensor_tensor_scan(out, seg, a, 0.0, A.mult, A.add))
 
+    def iota(key, out, pat, base, cm, flag=True):
+        if flag:
+            op("g", [], [key], lambda: g.iota(out, pat, base, cm, allow_small_or_imprecise_dtypes=True))
+        else:
+            op("g", [], [key], lambda: g.iota(out, pat, base, cm))
+
     def cols(key, a, b):
         return ["%s:%d" % (key, k) for k in range(a // 32, (b + 31) // 32)]
 
@@ -132,6 +139,19 @@ def rank_program(g, core, T, topo):
         if nv < 28:
             act(wkeys + lkeys, both(okey) if nv == 0 else [okey + "s"], out[:, o + 16 * nv:o + C], win.indirect(lst[:, l0 + nv:l0 + 28]))
 
+    place = {}
+
+    def col(name):
+        k = place.setdefault(name, len(place))
+        return T.cq[:, k:k + 1]
+
+    def icol(name):
+        k = ("pi", "p16", "p4", "p1", "grp").index(name)
+        return T.pi[:, k:k + 1]
+
+    def const(name, src, s1, o1, s2=None, o2=None):
+        ts([src], [name], col(name), icol(src) if src in ("pi", "p16", "p4", "p1", "grp") else col(src), s1, o1, s2, o2)
+
     dma("y", [(T.gqi[:], T.gq[:])], [], ["gqi"])
     dma("s", [(T.gmi[:], T.gm[:])], [], ["gmi"])
     dma("y", [(T.ut[:], T.u[:])], [], ["ut"])
@@ -142,102 +162,14 @@ def rank_program(g, core, T, topo):
     dma("y", [(T.wqp[:], T.ws[:])], [], ["wqp"])
     dma("y", [(T.vv[:], T.v[:])], [], ["vv"])
 
-    def iota(key, out, pat, base, cm, flag=True):
-        if flag:
-            op("g", [], [key], lambda: g.iota(out, pat, base, cm, allow_small_or_imprecise_dtypes=True))
-        else:
-            op("g", [], [key], lambda: g.iota(out, pat, base, cm))
-    iota("pi", T.pi[:, 0:1], [[0, 1]], 0, 1, False)
-    iota("jcol", T.jcol[:], [[1, 128]], 0, 0)
-    iota("j4", T.j4[:], [[0, 4], [1, 4]], 0, 0)
-    iota("iot", T.iot[:], [[1, C]], -224, 0)
-    iota("iwb", T.iwb[:], [[16, 28]], 0, 0)
-    iota("uli", T.uli[:, 0:8], [[16, 8]], -16, 0, False)
-    cp_, c16, c16n, kap, kaph, kap2, cphi, cphin, k4, c896, cg, cgk, cg7, c8, kin, ctmp, kq, km = (T.cq[:, k:k + 1] for k in range(18))
-    fill(["z"], T.zt[:], 0.0)
-    ts(["pi"], ["pi1"], T.pi[:, 1:2], T.pi[:, 0:1], 15, A.bitwise_and)
-    cp(["pi"], ["cp"], cp_, T.pi[:, 0:1])
-    ts(["pi"], ["pi4"], T.pi[:, 4:5], T.pi[:, 0:1], 4, A.arith_shift_right)
-    ts(["pi"], ["pi2"], T.pi[:, 2:3], T.pi[:, 0:1], 2, A.arith_shift_right, 3, A.bitwise_and)
-    ts(["pi"], ["pi3"], T.pi[:, 3:4], T.pi[:, 0:1], 3, A.bitwise_and)
-    cp(["pi1"], ["c16"], c16, T.pi[:, 1:2])
-    ts(["pi1"], ["c16n"], c16n, T.pi[:, 1:2], 1.0, A.add)
-    ts(["jcol", "cp"], ["ident"], T.ident[:], T.jcol[:], cp_, A.is_equal)
-    ts(["pi1"], ["kap"], kap, T.pi[:, 1:2], 15.0, A.is_equal, 1 / K, A.max)
-    cp(["pi2"], ["cphi"], cphi, T.pi[:, 2:3])
-    ts(["pi2"], ["cphin"], cphin, T.pi[:, 2:3], 1.0, A.add)
-    ts(["jcol", "c16"], ["sa"], T.sa[:, 0:16], T.jcol[:, 0:16], c16, A.not_equal)
-    ts(["jcol", "c16n"], ["sb"], T.sb[:, 0:16], T.jcol[:, 0:16], c16n, A.is_equal, K, A.mult)
-    ts(["z", "c16"], ["rep"], T.rep[:], T.zt[:, 0:28], c16, A.add)
-    ts(["j4", "cphi"], ["sa4"], T.sa[:, 16:32], T.j4[:], cphi, A.not_equal)
-    ts(["j4", "cphin"], ["sb4"], T.sb[:, 16:32], T.j4[:], cphin, A.is_equal, K, A.mult)
-    fill(["eb"], T.eb[:], 0.0)
-    tt(["sa", "sb", "sa4", "sb4"], ["sp"], T.sp[:], T.sa[:], T.sb[:], A.max)
-    act(["z"], ["wt1"], T.wt[:, C:960], T.zt[:])
-    act(["z"], ["wt0"], T.wt[:, 0:C], T.zt[:, 0:C])
-    act(["z"], ["wt2"], T.wt[:, 960:1408], T.zt[:, 0:C])
-    for t in range(2):
-        act(["ident", "wt1"], ["wi%d" % t], T.wt[:, C + t:960:4], T.ident[:])
-    act(["sp", "rep"], ["seg16"], T.seg16[:], T.sp[:, 0:16].indirect(T.rep[:, 0:28]))
-    quant(["z"], ["zcr"], "zc", 84, 212, T.zt, 0)
-    cp(["ident", "eb"], ["ebi"], T.eb[:, 4:516:4], T.ident[:])
-    ts(["kap"], ["kaph"], kaph, kap, 0.5, A.mult)
-    ts(["kap"], ["kap2"], kap2, kap, -2.0, A.mult)
-    ts(["kap"], ["km"], km, kap, M, A.mult)
-    ts(["pi2"], ["kin"], kin, T.pi[:, 2:3], 3.0, A.is_equal, 1 / K, A.max)
-    ts(["pi3"], ["c896"], c896, T.pi[:, 3:4], 896.25, A.add)
-    ts(["pi4"], ["cg7"], cg7, T.pi[:, 4:5], 7.0, A.is_lt)
-    ts(["pi4"], ["ctmp"], ctmp, T.pi[:, 4:5], 7.0, A.is_equal, -224.0, A.mult)
-    ts(["pi4"], ["cg"], cg, T.pi[:, 4:5], 448.0, A.mult, 0.25, A.add)
-    ts(["pi4"], ["c8"], c8, T.pi[:, 4:5], -448.0, A.mult, 7 * 448.0, A.add)
-    ts(["pi1"], ["kq"], kq, T.pi[:, 1:2], 15.0, A.not_equal, 1 / K, A.max)
-    ts(["kin"], ["k4"], k4, kin, 4.0, A.mult)
-    fill(["tabC0"], T.tabC[:, 0:28], 224.25)
-    tt(["cg", "ctmp"], ["cgk"], cgk, cg, ctmp, A.add)
-    ts(["iwb", "c16"], ["iw"], T.iw[:], T.iwb[:], c16, A.add)
-    ts(["uli"], ["uli2"], T.uli[:, 8:16], T.uli[:, 0:8], 127, A.bitwise_and)
-    quant(["wt0", "wt2", "wi0", "wi1"], ["shc"], "shc", 0, 352, T.wt, 0)
-
-    def scatter(a, b):
-        return lambda: cp(["iot", "qU"], ["rowqi"], T.rowqi[:, 0:C].indirect(T.qU[:, a:b]), T.iot[:, 16 * a:16 * b])
-
-    def ebq(b):
-        return lambda: quant(["ebi"], ["ebc%d" % b], "ebc", 128 * b, 128 * b + 128, T.eb, 4 - b)
-
-    cp(["gqi"], ["qU"], T.qU[:], T.gqi[:])
-    cp(["gmi"], ["mU"], T.mU[:], T.gmi[:])
-    cp(["uli2"], ["ulist"], T.ulist[:], T.uli[:, 8:16])
-    ts(["gqi"], ["hq"], T.hq[:, 0:28], T.gqi[:], 0.5, A.mult, -112.0, A.add)
-    gather(T.rowq, 0, "rowq", T.iot[:, 0:C], ["iot"], T.qU, 0, ["qU"], 14)
-    ts(["gqi", "kaph"], ["hk"], T.hq[:, 28:56], T.gqi[:], -224.0, A.add, kaph, A.mult)
-    tt(["gmi", "iw"], ["lo"], T.lo[:], T.gmi[:], T.iw[:], A.min)
-    ts(["iw", "cg7", "cgk"], ["tabC1"], T.tabC[:, 28:56], T.iw[:], cg7, A.mult, cgk, A.add)
-    gather(T.rowt, 0, "rowt", T.rowq[:, 0:C], both("rowq"), T.mU, 0, ["mU"], 14)
-    quant(["ut"], ["uc"], "uc", 0, 128, T.ut, 0)
-    cp(["lo"], ["loF"], T.loF[:], T.lo[:])
-
-    def tables(d):
-        w, dg, hi, lw = T["w" + d], T["d" + d], T["hi" + d], T["lw" + d]
-        return [
-            lambda: scan(["seg16"] + both("rowt"), ["sn"], T.sn[:], T.seg16[:], T.rowt[:]),
-            lambda: (ts(["sn", "kaph"], ["tq"], T.tq[:, 0:28], T.sn[:, 15:C:16], kaph, A.mult),
-                     ts(["sn", "kaph", "kap"], ["tk"], T.tq[:, 28:56], T.sn[:, 15:C:16], kaph, A.mult, kap, A.mult)),
-            lambda: (tt(["tq", "hq"], ["wq" + d], w[:], T.tq[:, 0:28], T.hq[:, 0:28], A.add),
-                     tt(["tk", "hk"], ["dh" + d], dg[:, 56:84], T.tq[:, 28:56], T.hq[:, 28:56], A.subtract)),
-            lambda: (ts(["wq" + d], ["hi" + d], hi[:], w[:], M, A.add, -M, A.add),
-                     ts(["dh" + d, "km"], ["dhi" + d], dg[:, 0:28], dg[:, 56:84], km, A.add, km, A.subtract)),
-            lambda: (tt(["hi" + d, "wq" + d], ["lw" + d], lw[:], w[:], hi[:], A.subtract),
-                     tt(["dhi" + d, "dh" + d], ["dlo" + d], dg[:, 28:56], dg[:, 56:84], dg[:, 0:28], A.subtract)),
-        ]
-
     def score(src, key, c, k):
-        a, b = PARTS[k]
+        a, b = (VPARTS if c == "vc" else PARTS)[k]
         quant(cols(key, a, b), [c + str(k)], c, a, b, src, 4 * a)
         mm(["uqc", "uqs", c + str(k)], ["P%d" % k], T["P%d" % k][:, 0:b - a], "uq", 0, c, a, b - a)
 
-    def sign(k):
-        a, b = PARTS[k]
-        act(["P%d" % k], ["sg%d" % k], T.sg[:, a:b], T["P%d" % k][:, 0:b - a], F.Sign, bias=-(2.0 ** -93))
+    def sign(k, f=act, parts=PARTS):
+        a, b = parts[k]
+        f(["P%d" % k], ["sg%d" % k], T.sg[:, a:b], T["P%d" % k][:, 0:b - a])
 
     def halve(src, key, a, b):
         act(cols(key, a, b), cols("xh", a, b), T.xh[:, 4 * a:4 * b], src[:, 4 * a:4 * b], F.Copy, scale=0.5)
@@ -245,34 +177,40 @@ def rank_program(g, core, T, topo):
     def copy_half():
         dma("y", [(T.xg[:, 0:4 * CUT], T.xh[:, 0:4 * CUT])], cols("xh", 0, CUT), cols("xg", 0, CUT))
 
-    tf = tables("F")
-    tf[0]()
-    cp(["uc", "ulist"], ["uqc"], T.uq[:, 0:128].bitcast(dt.uint32), T.uc[:, 0:128].bitcast(dt.uint32).indirect(T.ulist[:, 0:8]))
-    act(["uc", "ulist"], ["uqs"], T.uqp[:, 0:128], T.ucp[:, 0:128].indirect(T.ulist[:, 0:8]))
-    gather(T.rowm, 0, "rowm", T.iot[:, 0:C], ["iot"], T.mU, 0, ["mU"], 0)
-    act(["sp", "rep"], ["seg4"], T.seg4[:], T.sp[:, 16:32].indirect(T.rep[:, 0:28]))
-    tf[1]()
-    scatter(0, 4)()
-    tf[2]()
-    scatter(4, 8)()
-    tf[3]()
-    score(T.x0, "x0", "xc", 0)
-    tf[4]()
-    halve(T.x0, "x0", 0, 128)
-    score(T.x0, "x0", "xc", 1)
-    score(T.x0, "x0", "xc", 2)
-    for k in range(3):
-        sign(k)
-    scatter(8, 12)()
-    scatter(12, 16)()
+    def scatter(a, b):
+        return lambda: cp(["iot", "qU"], ["rowqi"], T.rowqi[:, 0:C].indirect(T.qU[:, a:b]), T.iot[:, 16 * a:16 * b])
+
+    def ebq(b):
+        return lambda: quant(["ebi"], ["ebc%d" % b], "ebc", 128 * b, 128 * b + 128, T.eb, 4 - b)
+
+    def halves(reads, key, out, a, s1, o1, s2, o2):
+        ts(reads, [key + "a"], out(0, 14), a(0, 14), s1[0], o1, s2[0], o2)
+        ts(reads, [key + "b"], out(14, 28), a(14, 28), s1[1], o1, s2[1], o2)
+
+    def tables(d):
+        w, dg, hi, lw = T["w" + d], T["d" + d], T["hi" + d], T["lw" + d]
+        return [
+            lambda: scan(["seg16"] + both("rowt"), ["sn"], T.sn[:], T.seg16[:], T.rowt[:]),
+            lambda: (ts(["sn", "kaph"], ["tq"], T.tq[:, 0:28], T.sn[:, 15:C:16], col("kaph"), A.mult),
+                     halves(["sn", "kaph", "kap"], "tk", lambda a, b: T.tq[:, 28 + a:28 + b], lambda a, b: T.sn[:, 16 * a + 15:16 * b:16],
+                            (col("kap"), col("kaph")), A.mult, (col("kap"), col("kap")), A.mult)),
+            lambda: (tt(["tq", "hq"], ["wq" + d], w[:], T.tq[:, 0:28], T.hq[:, 0:28], A.add),
+                     tt(["tka", "tkb", "hka", "hkb"], ["dh" + d], dg[:, 56:84], T.tq[:, 28:56], T.hq[:, 28:56], A.subtract)),
+            lambda: (ts(["wq" + d], ["hi" + d], hi[:], w[:], M, A.add, -M, A.add),
+                     halves(["dh" + d, "km", "km2"], "dhi" + d, lambda a, b: dg[:, a:b], lambda a, b: dg[:, 56 + a:56 + b],
+                            (col("km2"), col("km")), A.add, (col("km2"), col("km")), A.subtract)),
+            lambda: (tt(["hi" + d, "wq" + d], ["lw" + d], lw[:], w[:], hi[:], A.subtract),
+                     tt(["dhi%sa" % d, "dhi%sb" % d, "dh" + d], ["dlo" + d, "dhi" + d], dg[:, 28:56], dg[:, 56:84], dg[:, 0:28], A.subtract)),
+        ]
 
     def back_tables():
         tb = tables("B")
         return [
             lambda: scan(["seg16", "rowqi"], ["sn"], T.sn[:], T.seg16[:], T.rowqi[:]),
-            lambda: (ts(["sn", "kap"], ["qiU"], T.qiU[:], T.sn[:, 15:C:16], kap, A.mult, 224.25, A.add),
-                     ts(["sn", "kaph"], ["hq"], T.hq[:, 0:28], T.sn[:, 15:C:16], kaph, A.mult),
-                     ts(["sn", "kaph", "kap"], ["hk"], T.hq[:, 28:56], T.sn[:, 15:C:16], kaph, A.mult, kap, A.mult)),
+            lambda: (ts(["sn", "kap"], ["qiU"], T.qiU[:], T.sn[:, 15:C:16], col("kap"), A.mult, 224.25, A.add),
+                     ts(["sn", "kaph"], ["hq"], T.hq[:, 0:28], T.sn[:, 15:C:16], col("kaph"), A.mult),
+                     halves(["sn", "kaph", "kap"], "hk", lambda a, b: T.hq[:, 28 + a:28 + b], lambda a, b: T.sn[:, 16 * a + 15:16 * b:16],
+                            (col("kap"), col("kaph")), A.mult, (col("kap"), col("kap")), A.mult)),
             lambda: gather(T.rowt, 0, "rowt", T.rowm[:, 0:C], both("rowm"), T.qiU, 0, ["qiU"], 0),
             tb[0], tb[1],
             lambda: (tt(["tq", "hq"], ["lo"], T.lo[:], T.tq[:, 0:28], T.hq[:, 0:28], A.min), tb[2]()),
@@ -280,60 +218,161 @@ def rank_program(g, core, T, topo):
             tb[4],
         ]
 
+    iota("pi", icol("pi"), [[0, 1]], 0, 1, False)
+    iota("j16", T.j16[:], [[1, 16]], 0, 0)
+    iota("iot", T.iot[:, 0:C], [[1, C]], -224, 0)
+    iota("iwb", T.iwb[:], [[16, 28]], 0, 0)
+    iota("uli", T.uli[:, 0:8], [[16, 8]], -16, 0, False)
+    iota("j4", T.j4[:], [[0, 4], [1, 4]], 0, 0)
+    fill(["z"], T.zt[:], 0.0)
+    ts(["pi"], ["p16"], icol("p16"), icol("pi"), 15, A.bitwise_and)
+    const("cp", "pi", 0.0, A.add)
+    ts(["pi"], ["p4"], icol("p4"), icol("pi"), 2, A.arith_shift_right, 3, A.bitwise_and)
+    ts(["pi"], ["p1"], icol("p1"), icol("pi"), 3, A.bitwise_and)
+    ts(["pi"], ["grp"], icol("grp"), icol("pi"), 4, A.arith_shift_right)
+    const("c16", "p16", 0.0, A.add)
+    const("c16n", "p16", 1.0, A.add)
+    const("kap", "p16", 15.0, A.is_equal, 1 / K, A.max)
+    const("c4", "p4", 0.0, A.add)
+    const("c4n", "p4", 1.0, A.add)
+    ts(["j16", "c16"], ["sa"], T.sa[:, 0:16], T.j16[:], col("c16"), A.not_equal)
+    ts(["j16", "c16n"], ["sb"], T.sb[:, 0:16], T.j16[:], col("c16n"), A.is_equal, K, A.mult)
+    ts(["z", "c16"], ["rep"], T.rep[:], T.zt[:, 0:28], col("c16"), A.add)
+    const("kaph", "kap", 0.5, A.mult)
+    const("km", "kap", M, A.mult)
+    const("km2", "kap", 2 * M, A.mult)
+    tt(["sa", "sb"], ["sp"], T.sp[:, 0:16], T.sa[:, 0:16], T.sb[:, 0:16], A.max)
+    act(["z"], ["wt1"], T.wt[:, C:960], T.zt[:])
+    act(["z"], ["wt0"], T.wt[:, 0:C], T.zt[:, 0:C])
+    act(["sp", "rep"], ["seg16"], T.seg16[:], T.sp[:, 0:16].indirect(T.rep[:, 0:28]))
+    quant(["z"], ["zcr"], "zc", 84, 212, T.zt, 0)
+    ts(["iot", "cp"], ["ident"], T.ident[:], T.iot[:, 224:352], col("cp"), A.is_equal)
+    cp(["gqi"], ["qU"], T.qU[:], T.gqi[:])
+    cp(["gmi"], ["mU"], T.mU[:], T.gmi[:])
+    ts(["gqi"], ["hq"], T.hq[:, 0:28], T.gqi[:], 0.5, A.mult, -112.0, A.add)
+    halves(["gqi", "kaph", "kap"], "hk", lambda a, b: T.hq[:, 28 + a:28 + b], lambda a, b: T.gqi[:, a:b], (-224.0, -224.0), A.add, (col("kap"), col("kaph")), A.mult)
+    gather(T.rowq, 0, "rowq", T.iot[:, 0:C], ["iot"], T.qU, 0, ["qU"], 14)
+    act(["z"], ["wt2"], T.wt[:, 960:1408], T.zt[:, 0:C])
+    ts(["uli"], ["uli2"], T.uli[:, 8:16], T.uli[:, 0:8], 127, A.bitwise_and)
+    ts(["iwb", "c16"], ["iw"], T.iw[:], T.iwb[:], col("c16"), A.add)
+    quant(["ut"], ["uc"], "uc", 0, 128, T.ut, 0)
+    cp(["uli2"], ["ulist"], T.ulist[:], T.uli[:, 8:16])
+    gather(T.rowt, 0, "rowt", T.rowq[:, 0:C], both("rowq"), T.mU, 0, ["mU"], 16)
+    act(["uc", "ulist"], ["uqs"], T.uqp[:, 0:128], T.ucp[:, 0:128].indirect(T.ulist[:, 0:8]))
+    for t in range(2):
+        act(["ident", "wt1"], ["wi%d" % t], T.wt[:, C + t:960:4], T.ident[:])
+    cp(["uc", "ulist"], ["uqc"], T.uq[:, 0:128].bitcast(dt.uint32), T.uc[:, 0:128].bitcast(dt.uint32).indirect(T.ulist[:, 0:8]))
+    tf = tables("F")
+    tf[0]()
+    tt(["gmi", "iw"], ["lo"], T.lo[:], T.gmi[:], T.iw[:], A.min)
+    ts(["j4", "c4"], ["sa4"], T.sa[:, 16:32], T.j4[:], col("c4"), A.not_equal)
+    ts(["j4", "c4n"], ["sb4"], T.sb[:, 16:32], T.j4[:], col("c4n"), A.is_equal, K, A.mult)
+    tf[1]()
+    score(T.x0, "x0", "xc", 0)
+    tf[2]()
+    cp(["lo"], ["loF"], T.loF[:], T.lo[:])
+    score(T.x0, "x0", "xc", 1)
+    tt(["sa4", "sb4"], ["sp4"], T.sp[:, 16:32], T.sa[:, 16:32], T.sb[:, 16:32], A.max)
+    score(T.x0, "x0", "xc", 2)
+    tf[3]()
+    halve(T.x0, "x0", 0, 128)
+    sign(0)
+    sign(1)
+    quant(["wt0", "wt2", "wi0", "wi1"], ["shc"], "shc", 0, 352, T.wt, 0)
+    sign(2, cp)
+    tf[4]()
+
+    def late_constants():
+        return [
+            lambda: (const("cg7", "grp", 7.0, A.is_lt), const("c7", "grp", 7.0, A.is_equal, -224.0, A.mult), const("cg", "grp", 4.0, A.max, 448.0, A.mult),
+                     const("cfa", "grp", 4.0, A.min, 448.0, A.mult)),
+            lambda: (ts(["cg", "c7"], ["cgk"], col("cgk"), col("cg"), col("c7"), A.add, 0.25 - 4 * C, A.add), const("cfF", "cfa", 224.25, A.add),
+                     const("kin", "p4", 3.0, A.is_equal, 1 / K, A.max), const("c896", "p1", 896.25, A.add)),
+            lambda: (ts(["iw", "cg7", "cgk"], ["tabC"], T.tabC[:], T.iw[:], col("cg7"), A.mult, col("cgk"), A.add), const("k4", "kin", 4.0, A.mult)),
+            lambda: (const("c8a", "grp", 3.0, A.min, -448.0, A.mult), const("cfb", "grp", 3.0, A.max, -448.0, A.mult), const("kap2", "kap", -2.0, A.mult),
+                     const("kq", "p16", 15.0, A.not_equal, 1 / K, A.max)),
+            lambda: (const("c8", "c8a", 3.0 * C, A.add), const("cfB", "cfb", 224.25 + 7 * C, A.add)),
+        ]
+
     def chain(d, way, shares, vgap, sgap):
         def gap(name):
             for f in vgap.get(name, []) + sgap.get(name, []):
                 f()
         dg, w = T["d" + d], T["w" + d]
-        gather(T.mg, 0, "mg", T.sg[:, 0:C], ["sg0", "sg1", "sg2"], T["lo" + d], 0, ["lo" + d], shares[0])
+        keys = ["sg0", "sg1", "sg2", "lo" + d]
+        ts(keys, ["mgv"], T.mg[:, 0:224], T.sg[:, 0:C].indirect(T["lo" + d][:, 0:14]), 0.0, A.is_gt, -0.5, A.add)
+        act(keys, ["mgs"], T.mg[:, 224:C], T.sg[:, 0:C].indirect(T["lo" + d][:, 14:28]), F.Sign, bias=-(2.0 ** -93))
         gap("signs")
         scan(["seg16"] + both("mg"), ["sc"], T.sc[:], T.seg16[:], T.mg[:])
         gap("scan")
         s = T.sc[:, 15:C:16]
-        tt(["sc", "dh" + d], ["t3"], T.t3[:], s, dg[:, 56:84], A.mult)
         tt(["sc", "dhi" + d], ["u0"], T.uu[:, 0:28], s, dg[:, 0:28], A.mult)
         tt(["sc", "dlo" + d], ["u1"], T.uu[:, 28:56], s, dg[:, 28:56], A.mult)
-        tt(["t3", "wq" + d], ["t4"], T.t4[:], T.t3[:], w[:], A.add)
+        tt(["sc", "dh" + d], ["t3"], T.t3[:], s, dg[:, 56:84], A.mult)
+        gap("times")
         tt(["u0", "hi" + d], ["z0", "z"], T.zt[:, 336:C:4], T.uu[:, 0:28], T["hi" + d][:], A.add)
         tt(["u1", "lw" + d], ["z1"], T.zt[:, 337:C:4], T.uu[:, 28:56], T["lw" + d][:], A.add)
-        ts(["t4"], ["ls0"], T.ls[:, 0:28], T.t4[:], 224.25, A.add)
+        tt(["t3", "wq" + d], ["t4"], T.t4[:], T.t3[:], w[:], A.add)
+        gap("plus")
         quant(["z0", "z1"], ["zc"], "zc", 0, 128, T.zt, 0)
-        for bank, ns in (("P0", (1,)), ("P3", (2,)), ("P1", (3, 4, 5)), ("P2", (6, 7))):
+        ts(["t4"], ["ls0"], T.ls[:, 0:28], T.t4[:], 224.25, A.add)
+        for bank, ns in (("P0", (5,)), ("P3", (1,)), ("P1", (6, 2, 3, 4)), ("P2", (7,))):
             need("t", deps(["zc", "zcr", "shc"], [bank]))
-            for n in ns:
-                s0, z0 = 112 + way * 16 * n, 84 - 28 * (n - ns[0])
+            for k, n in enumerate(ns):
+                s0, z0 = 112 + way * 16 * n, 84 - 28 * k
                 i = g.tensor.matmul_mx(T[bank][:, 0:128], T.shc[:, s0:s0 + 128], T.shcp[:, s0:s0 + 128], T.zc[:, z0:z0 + 128], T.zcp[:, z0:z0 + 128], n == ns[0], n == ns[-1])
             count["t"] = count.get("t", 0) + 1
             i.then_inc(T.sem["t"], 1)
             done(("t", count["t"], dict(known["t"])), ["zc", "zcr", "shc"], [bank])
-        gap("own")
-        gather(T.R, 0, "R0", T.iot[:, 0:C], ["iot"], T.ls, 0, ["ls0"], shares[1])
-        ts(["P0"], ["ls1"], T.ls[:, 28:56], T.P0[:, 0:28], 224.25, A.add)
-        ts(["P3"], ["ls2"], T.ls[:, 56:84], T.P3[:, 0:28], 224.25, A.add)
-        gap(0)
-        for n in range(1, 8):
-            lk = "ls%d" % (n if n < 3 else 3 if n < 6 else 6)
-            if d == "F" and n == 7:
-                gather(T.arow, 0, "arow", T.R[:, 0:7 * C], [k for i in range(7) for k in both("R%d" % i)], T.ls, 196, [lk], shares[8])
-            else:
-                gather(T.R, n * C, "R%d" % n, T.R[:, (n - 1) * C:n * C], both("R%d" % (n - 1)), T.ls, 28 * n, [lk], shares[1 + n])
-            if n == 1:
-                ts(["P1"], ["ls3"], T.ls[:, 84:168], T.P1[:, 0:84], 224.25, A.add)
-            if n == 2 and d == "B":
-                ts(["P2"], ["ls6"], T.ls[:, 168:224], T.P2[:, 0:56], 224.25, A.add)
-            if n == 2 and d == "F":
-                tt(["P2", "tabC0", "tabC1"], ["tC"], T.tC[:], T.P2[:, 0:56], T.tabC[:], A.add)
-            if n == 3 and d == "F":
-                cp(["tC"], ["ls6"], T.ls[:, 168:224], T.tC[:])
-            gap(n)
-        row = "arow"
-        if d == "B":
-            gather(T.brow, 0, "brow", T.R[:, 0:8 * C], [k for i in range(8) for k in both("R%d" % i)], T.a8, 0, ["a8"], shares[9])
-            gap(8)
-            row = "brow"
+        gap("list")
+
+        def left(n):
+            gather(T.R, n * C, "L%d" % n, T.R[:, (n - 1) * C:n * C], both("L%d" % (n - 1)), T.ls, (56, 112, 140, 168)[n - 1], ["ls1" if n == 1 else "lsB"], shares.get("L%d" % n, 14))
+            gap("L%d" % n)
+
+        def right(n, whole=False):
+            lst, l0, lk = ((T.ls, 28, "lsA"), (T.ls, 84, "lsB"), (T.ls, 196, "lsC"), (T.a8, 0, "a8"))[n]
+            a = 0 if whole else n
+            gather(T.iot, (n + 1) * C, "Q%d" % n, T.iot[:, a * C:(n + 1) * C], ["iot"] + [k for i in range(max(a - 1, 0), n) for k in both("Q%d" % i)], lst, l0, [lk], shares.get("Q%d" % n, 14))
+            if n == 0:
+                ts(["P1"], ["lsB"], T.ls[:, 84:196], T.P1[:, 0:112], 224.25, A.add)
+            if n == 1 and d == "F":
+                cp(["tC"], ["lsC"], T.ls[:, 196:224], T.tC[:])
+            gap("Q%d" % n)
+
+        def wrap(n):
+            scan(["seg16"] + both("Q%d" % n), ["sc"], T.sc[:], T.seg16[:], T.iot[:, (n + 1) * C:(n + 2) * C])
+            gap("wrap")
+
+        gather(T.R, 0, "L0", T.iot[:, 0:C], ["iot"], T.ls, 0, ["ls0"], shares.get("L0", 8))
+        ts(["P0"], ["lsA"], T.ls[:, 28:56], T.P0[:, 0:28], 224.25, A.add)
+        ts(["P3"], ["ls1"], T.ls[:, 56:84], T.P3[:, 0:28], 224.25, A.add)
+        gap("L0")
+        right(0)
+        left(1)
+        if d == "F":
+            tt(["P2", "tabC"], ["tC"], T.tC[:], T.P2[:, 0:28], T.tabC[:], A.add)
+        else:
+            ts(["P2"], ["lsC"], T.ls[:, 196:224], T.P2[:, 0:28], 224.25, A.add)
+        right(1)
+        left(2)
+        right(2, d == "F")
+        left(3)
+        if d == "F":
+            wrap(2)
+            left(4)
+        else:
+            right(3, True)
+            left(4)
+            wrap(3)
+        ts(["sc", "kap", "cf" + d], ["lf"], T.lf[:], T.sc[:, 15:C:16], col("kap"), A.mult, col("cf" + d), A.add)
+        gap("fin")
+        row = "arow" if d == "F" else "brow"
+        gather(T[row], 0, row, T.R[:, 0:5 * C], [k for i in range(5) for k in both("L%d" % i)], T.lf, 0, ["lf"], shares.get("last", 14))
+        gap("last")
         scan(["seg4"] + both(row), ["sc4"], T.sc4[:], T.seg4[:], T[row][:])
         gap("scan4")
-        ts(["sc4", "k4", "c896"], ["l4"], T.l4[:], T.sc4[:, 3:C:4], k4, A.mult, c896, A.add)
+        ts(["sc4", "k4", "c896"], ["l4"], T.l4[:], T.sc4[:, 3:C:4], col("k4"), A.mult, col("c896"), A.add)
         gap("l4")
 
     def move(out, okey, win, wkeys, base, bkey, a, b):
@@ -346,7 +385,7 @@ def rank_program(g, core, T, topo):
         tt(cols("tg", a, b) + cols(bkey, a, b), cols(okey, a, b), out[:, 4 * a:4 * b], T.tg[:, 4 * a:4 * b], base[:, 4 * a:4 * b], A.add)
 
     def turn_row(d):
-        act(["df0", "df1", "lo" + d, "kap", "kap2"], ["nu" + d], T["nu" + d][:], T.df[:, 0:C].indirect(T["lo" + d][:, 0:28]), F.Identity, bias=kap, scale=kap2)
+        act(["df0", "df1", "lo" + d, "kap", "kap2"], ["nu" + d], T["nu" + d][:], T.df[:, 0:C].indirect(T["lo" + d][:, 0:28]), F.Identity, bias=col("kap"), scale=col("kap2"))
 
     def turn_scan(d):
         scan(["seg16", "nu" + d], ["sn"], T.sn[:], T.seg16[:], T["nu" + d][:])
@@ -366,18 +405,20 @@ def rank_program(g, core, T, topo):
         hc, lc = "hc%d" % r, "lc%d" % r
         src, skey = (T.x0, "x0") if r == 0 else (T.xt, "xt")
         if r == 0:
-            bt = back_tables()
-            vgap = {"signs": [scatter(16, 20)], "scan": [scatter(20, 24)], "own": [scatter(24, 28)], 0: [bt[0]], 1: [bt[1]], 2: [bt[2]],
-                    4: [bt[3]], 5: [bt[4]], 6: [bt[5]], 7: [bt[6]], "scan4": [bt[7]]}
-            sgap = {"signs": [lambda: halve(src, skey, 128, CUT), copy_half, lambda: halve(src, skey, CUT, C)]}
-            shares = [14, 10, 14, 14, 26, 14, 14, 14, 14]
-            dma("y", [(T.agrow[0:16, :], T.iot[0:16, :])], ["iot"], ["ag0"])
+            bt, late = back_tables(), late_constants()
+            vgap = {"signs": [scatter(0, 4)], "scan": [scatter(4, 8)], "times": [late[0]], "plus": [late[1]], "list": [late[2], scatter(8, 12)], "L0": [scatter(12, 14)],
+                    "Q0": [scatter(14, 18)], "Q1": [scatter(18, 22)], "L2": [scatter(22, 28)], "L3": [bt[0]], "wrap": [bt[1]],
+                    "last": [bt[2], late[3]], "scan4": [late[4], lambda: fill(["eb"], T.eb[:], 0.0)]}
+            sgap = {"signs": [lambda: halve(src, skey, 128, CUT), copy_half, lambda: halve(src, skey, CUT, C),
+                              lambda: act(["sp4", "rep"], ["seg4"], T.seg4[:], T.sp[:, 16:32].indirect(T.rep[:, 0:28]))],
+                    "L4": [lambda: gather(T.rowm, 0, "rowm", T.iot[:, 0:C], ["iot"], T.mU, 0, ["mU"], 0)]}
+            shares = {"L0": 8, "Q0": 8, "L1": 10, "Q1": 8, "L2": 8, "Q2": 10, "L3": 10, "L4": 20, "last": 20}
+            dma("y", [(T.agrow[0:16, :], T.iot[0:16, 0:C])], ["iot"], ["ag0"])
         else:
-            vgap = {}
-            sgap = {"signs": [lambda: halve(src, skey, 0, CUT), copy_half, lambda: halve(src, skey, CUT, 352)],
-                    1: [lambda: halve(src, skey, 352, 384)], 2: [lambda: halve(src, skey, 384, 416)], 3: [lambda: halve(src, skey, 416, C)],
-                    7: [lambda: turn_row("B")]}
-            shares = [14, 12] + [14] * 7
+            vgap = {"signs": [lambda: turn("F")]}
+            sgap = {"signs": [lambda: halve(src, skey, 0, CUT), copy_half, lambda: halve(src, skey, CUT, C)],
+                    "last": [lambda: turn_row("B")]}
+            shares = {"Q0": 12, "L4": 12}
         chain("F", -1, shares, vgap, sgap)
         dma("y", [(T.agrow[16:128, :], T.arow[0:112, :])], both("arow"), ["agrow"])
 
@@ -385,7 +426,7 @@ def rank_program(g, core, T, topo):
             a, e = HRUNS[h]
             for b in range(4):
                 bank = "P%d" % (4 + b)
-                mm(["wqc", "wqp"] + ["vc%d" % k for k in range(3) if a <= PARTS[k][0] < e], [bank], T[bank][:, 0:e - a], "wq", 128 * b, "vc", a, e - a)
+                mm(["wqc", "wqp"] + ["vc%d" % k for k in range(3) if a <= VPARTS[k][0] < e], [bank], T[bank][:, 0:e - a], "wq", 128 * b, "vc", a, e - a)
 
         def layer_out(h, b):
             a, e = HRUNS[h]
@@ -408,55 +449,64 @@ def rank_program(g, core, T, topo):
         def unpack(h):
             a, e = HRUNS[h]
             for b in range(4):
-                bank = "P%d" % (4 + b)
+                bank = "P%d" % (4 - 4 * h + b)
                 mm(["ebc%d" % b, lc + str(h)], [bank], T[bank][:, 0:e - a], "ebc", 128 * b, lc, a, e - a)
 
-        def unpack_out(h, b):
+        def unpack_out(h, b, f=act):
             a, e = HRUNS[h]
-            bank = "P%d" % (4 + b)
-            act([bank], ["dd%d%d" % (h, b)], T.dd[:, 4 * a + b:4 * e:4], T[bank][:, 0:e - a])
+            bank = "P%d" % (4 - 4 * h + b)
+            f([bank], ["dd%d%d" % (h, b)], T.dd[:, 4 * a + b:4 * e:4], T[bank][:, 0:e - a])
 
+        first = (lambda k: bt[k]()) if r == 0 else (lambda k: None)
         move(T.vt, "vt", T.xh, XH, T.xg, "xg", 0, 128)
         fetch(T.xh, XH, CUT, 320)
         fetch(T.xh, XH, 320, C)
+        first(3)
         move(T.vt, "vt", T.xh, XH, T.xg, "xg", 128, CUT)
+        first(4)
         score(T.vt, "vt", "vc", 0)
         layer(0)
-        sign(0)
+        sign(0, act, VPARTS)
         for b in range(4):
             layer_out(0, b)
         add(T.vt, "vt", T.xh, "xh", CUT, 320)
+        first(5)
         add(T.vt, "vt", T.xh, "xh", 320, C)
         score(T.vt, "vt", "vc", 1)
         score(T.vt, "vt", "vc", 2)
         layer(1)
-        sign(1)
-        sign(2)
+        sign(1, act, VPARTS)
+        first(6)
         send(0)
-        if r:
-            turn_scan("B")
         scan(["seg16"] + both("arow"), ["sm"], T.sm[:], T.seg16[:], T.arow[:])
         if r:
-            turn("B")
+            turn_scan("B")
+        sign(2, cp, VPARTS)
+        first(7)
 
         def spread_a8():
-            ts(["sm", "kap"], ["p16"], T.p16[:], T.sm[:, 15:C:16], kap, A.mult, 224.25, A.add)
+            ts(["sm", "kap"], ["p16"], T.p16[:], T.sm[:, 15:C:16], col("kap"), A.mult, 224.25, A.add)
             dma("y", [(T.a8r[16 * k:16 * k + 16, :], T.p16[112:128, :]) for k in range(8)], ["p16"], ["a8r"])
-        vgap = {"signs": [spread_a8], "own": [lambda: send(1)], 6: [lambda: ts(["a8r", "c8"], ["a8"], T.a8[:], T.a8r[:], c8, A.add)],
+        vgap = {"signs": [spread_a8], "list": [lambda: send(1)], "L2": [lambda: ts(["a8r", "c8"], ["a8"], T.a8[:], T.a8r[:], col("c8"), A.add)],
+                "wrap": [lambda: unpack_out(1, 0, cp)], "fin": [lambda: unpack_out(1, 1, cp)],
                 "scan4": [lambda: differ(0)], "l4": [lambda: differ(1)]}
         if r == 0:
-            vgap["signs"] += [ebq(0)]
-            vgap["scan"] = [ebq(1)]
-            vgap[0] = [ebq(2)]
-            vgap[1] = [ebq(3)]
+            vgap["signs"] += [lambda: cp(["ident", "eb"], ["ebi"], T.eb[:, 4:516:4], T.ident[:])]
+            vgap["scan"] = [ebq(0)]
+            vgap["times"] = [ebq(1)]
+            vgap["plus"] = [ebq(2)]
+            vgap["L0"] = [ebq(3)]
+        else:
+            vgap["signs"] += [lambda: turn("B")]
         if r == 1:
-            vgap[3] = [lambda: quant(["vv"], ["vq"], "vq", 0, 128, T.vv, 0)]
+            vgap["scan"] = [lambda: quant(["vv"], ["vq"], "vq", 0, 128, T.vv, 0)]
         if r == 2:
-            vgap[3] = [lambda: ts(["dhF", "kq"], ["dq"], T.dq[:], T.dF[:, 56:84], -K, A.mult, kq, A.mult)]
+            vgap["scan"] = [lambda: ts(["dhF", "kq"], ["dq"], T.dq[:, 0:14], T.dF[:, 56:70], -K / 2, A.mult, col("kq"), A.mult),
+                            lambda: ts(["dhF", "kq"], ["dq1"], T.dq[:, 14:28], T.dF[:, 70:84], -K, A.mult, col("kq"), A.mult)]
         sgap = {"signs": [lambda b=b: layer_out(1, b) for b in range(4)],
-                3: [lambda: unpack(0), lambda: unpack_out(0, 0)], 4: [lambda: unpack_out(0, 1)], 5: [lambda: unpack_out(0, 2)], 6: [lambda: unpack_out(0, 3), lambda: unpack(1)],
-                7: [lambda: unpack_out(1, 0)], 8: [lambda b=b: unpack_out(1, b) for b in (1, 2, 3)]}
-        chain("B", 1, [14, 8, 14, 14, 14, 14, 14, 14, 14, 16], vgap, sgap)
+                "L2": [lambda: unpack(0), lambda: unpack(1)], "L4": [lambda b=b: unpack_out(0, b) for b in range(4)],
+                "last": [lambda b=b: unpack_out(1, b) for b in (2, 3)]}
+        chain("B", 1, {"L0": 4, "Q0": 12, "L4": 10}, vgap, sgap)
         if r < 2:
             fetch(T.dd, DD, CUT, 320)
             fetch(T.dd, DD, 320, C)
@@ -469,32 +519,43 @@ def rank_program(g, core, T, topo):
             score(T.xt, "xt", "xc", 1)
             score(T.xt, "xt", "xc", 2)
             sign(1)
-            sign(2)
             turn_scan("F")
-            turn("F")
+            sign(2, cp)
         else:
-            def out(k):
-                a, b = ((0, 224), (224, C))[k]
-                bank = "P%d" % k
+            def product(k):
+                a, b = PARTS[k]
                 quant(cols("xt", a, b), ["xc%d" % k], "xc", a, b, T.xt, 4 * a)
-                dma("y", [(T.oc[:, 4 * a:4 * b], T.xc[:, a:b].bitcast(dt.uint8))], ["xc%d" % k], ["oc%d" % k])
-                mm(["vq", "xc%d" % k], [bank], T[bank][:, 0:b - a], "vq", 0, "xc", a, b - a)
-                act([bank], ["y%d" % k], T.ysb[:, a:b], T[bank][:, 0:b - a])
-                dma("s", [(T.y[:, a:b], T.ysb[:, a:b])], ["y%d" % k], ["yo%d" % k])
+                mm(["vq", "xc%d" % k], ["P%d" % k], T["P%d" % k][:, 0:b - a], "vq", 0, "xc", a, b - a)
+
+            def result(k, f):
+                a, b = PARTS[k]
+                f(["P%d" % k], ["y%d" % k], T.ysb[:, a:b], T["P%d" % k][:, 0:b - a])
+
+            def codes_out(a, b, keys):
+                dma("y", [(T.oc[:, 4 * a:4 * b], T.xc[:, a:b].bitcast(dt.uint8))], keys, ["oc%d" % a])
             turn_row("F")
             fetch(T.dd, DD, 288, C)
-            move(T.xt, "xt", T.dd, DD, T.vt, "vt", 0, 224)
+            move(T.xt, "xt", T.dd, DD, T.vt, "vt", 0, CUT)
             turn_scan("F")
-            out(0)
-            tt(["sn", "dq"], ["t3"], T.t3[:], T.sn[:, 15:C:16], T.dq[:], A.mult)
-            move(T.xt, "xt", T.dd, DD, T.vt, "vt", 224, 288)
+            product(0)
+            codes_out(0, CUT, ["xc0"])
+            result(0, act)
+            dma("s", [(T.y[:, 0:CUT], T.ysb[:, 0:CUT])], ["y0"], ["yo0"])
+            tt(["sn", "dq", "dq1"], ["t3"], T.t3[:], T.sn[:, 15:C:16], T.dq[:], A.mult)
+            move(T.xt, "xt", T.dd, DD, T.vt, "vt", CUT, 288)
             tt(["t3", "wqF"], ["t4"], T.t4[:], T.t3[:], T.wF[:], A.add)
-            add(T.xt, "xt", T.vt, "vt", 288, C)
+            add(T.xt, "xt", T.vt, "vt", 288, 320)
+            add(T.xt, "xt", T.vt, "vt", 320, C)
             ts(["t4"], ["qoU"], T.qoU[:], T.t4[:], 224.25, A.add)
-            out(1)
-            ts(["iot", "qoU"], ["qrow"], T.qrow[:], T.iot[:, 0:C].indirect(T.qoU[:, 0:28]), 224.0, A.add)
-            dma("y", [(T.osc[4 * k:4 * k + 4, :], T.xcp[32 * k:32 * k + 4, 0:C]) for k in range(4)], ["xc0", "xc1"], ["osc"])
-            dma("y", [(T.qo[:], T.qrow[0:128:16, :])], ["qrow"], ["qo"])
+            product(1)
+            product(2)
+            act(["iot", "qoU"], ["qrow"], T.qrow[:], T.iot[:, 0:C].indirect(T.qoU[:, 0:28]), F.Identity, bias=224.0)
+            dma("s", [(T.qo[:], T.qrow[0:128:16, :])], ["qrow"], ["qo"])
+            codes_out(CUT, C, ["xc1", "xc2"])
+            result(1, cp)
+            result(2, cp)
+            dma("y", [(T.osc[4 * k:4 * k + 4, :], T.xcp[32 * k:32 * k + 4, 0:C]) for k in range(4)], ["xc0", "xc1", "xc2"], ["osc"])
+            dma("y", [(T.y[:, CUT:C], T.ysb[:, CUT:C])], ["y1", "y2"], ["yo1"])
     for sem in count:
         if known["g"].get(sem, 0) < count[sem]:
             g.wait_ge(T.sem[sem], count[sem])

@@ -5,36 +5,38 @@ import comms_topo
 STEP = [1, 2, 3]
 C = 448
 PARTS = [(0, 192), (192, 320), (320, C)]
-VPARTS = [(0, 128), (128, 320), (320, C)]
-HRUNS = [(0, 128), (128, C)]
-CUT = 192
+EARLY, NV = 12, 20
+HRUNS = [(0, 192), (192, C)]
+CUT = HEAD = 224
+SHARES = {"F0": {"L0": 4, "Q0": 8, "L2": 10, "Q2": 10, "L4": 12, "last": 20}, "F": {"L0": 10, "Q0": 12, "L1": 12, "L4": 12},
+          "B0": {"L0": 4, "Q0": 12, "L1": 12, "L4": 10}, "B": {"L0": 6, "Q0": 12, "L1": 12, "L4": 8}}
 K = 2.0 ** 24
 M = 1.5 * 2.0 ** 27
 BF, F32, I32, U16, MX, U8 = "bfloat16", "float32", "int32", "uint16", "float8_e4m3fn_x4", "uint8"
 
 SCRATCH = {}
 for _n, _w in (("x0", 1792), ("xt", 1792), ("xh", 1792), ("xg", 1792), ("vt", 1792), ("ht", 1792), ("dd", 1792), ("tg", 1792), ("ut", 512), ("vv", 512),
-               ("wt", 1408), ("eb", 520), ("zt", 512), ("ident", 128), ("R", 5 * C), ("iot", 5 * C),
+               ("wt", 1408), ("eb", 520), ("zt", 520), ("R", 5 * C), ("iot", 5 * C),
                ("j16", 16), ("j4", 16), ("seg16", C), ("seg4", C), ("sa", 32), ("sb", 32), ("sp", 32),
-               ("rowq", C), ("rowm", C), ("rowqi", C), ("rowt", C), ("arow", C), ("brow", C), ("agrow", C), ("df", C), ("nuF", C), ("nuB", C),
-               ("mg", C), ("sc", C), ("sn", C), ("sm", C), ("sc4", C), ("sg", C)):
+               ("rowq", C), ("rowqs", C), ("rowqi", C), ("rowt", C), ("arow", C), ("brow", C), ("agrow", C), ("df", C), ("nu", C), ("nrow", C),
+               ("mg", C), ("s3", 1360), ("sc", C), ("sn", C), ("sm", C), ("sc4", C), ("sg", C)):
     SCRATCH[_n] = ("sbuf", [128, _w], BF)
-for _n, _w in (("uc", 128), ("uq", 128), ("vq", 128), ("wq", 512), ("xc", C), ("vc", C), ("ebc", 512), ("shc", 352), ("zc", 212),
+for _n, _w in (("uc", 128), ("uq", 128), ("vq", 128), ("wq", 512), ("xc", C), ("vc", C), ("ebc", 512), ("shc", 352), ("zc", 256),
                ("hc0", C), ("hc1", C), ("hc2", C), ("lc0", C), ("lc1", C), ("lc2", C)):
     SCRATCH[_n] = ("sbuf", [128, _w], MX)
     SCRATCH[_n + "p"] = ("sbuf", [128, _w], U8)
-for _n, _w in (("qU", 28), ("mU", 28), ("loF", 28), ("loB", 28), ("qiU", 28), ("ls", 224), ("l4", 112), ("p16", 28),
-               ("a8r", 28), ("a8", 28), ("ulist", 8), ("qoU", 28), ("rep", 28), ("lf", 28)):
+for _n, _w in (("qU", 28), ("mU", 28), ("loU", 28), ("ls0", 28), ("ls", 224), ("l4", 112), ("a8w", 28), ("n8w", 28), ("a8r", 28),
+               ("ulist", 8), ("qoU", 28), ("rep", 28), ("lf", 28)):
     SCRATCH[_n] = ("sbuf", [128, _w], U16)
-for _n, _w in (("iwb", 28), ("iw", 28), ("tabC", 28), ("tC", 28), ("wF", 28), ("wB", 28), ("hiF", 28), ("lwF", 28), ("hiB", 28), ("lwB", 28),
-               ("uu", 56), ("dF", 84), ("dB", 84), ("t3", 28), ("t4", 28),
-               ("hq", 56), ("tq", 56), ("lo", 28), ("dq", 28), ("cq", 32), ("ysb", C), ("qrow", C)):
+for _n, _w in (("iwb", 28), ("iw", 28), ("tabC", 28), ("tC", 28), ("wB", 28),
+               ("ds", 28), ("tO", 56), ("tbF", 252), ("tbB", 252), ("t4", 84),
+               ("hq", 56), ("tq", 56), ("lo", 28), ("dq", 84), ("cq", 40), ("ysb", C), ("qrow", C)):
     SCRATCH[_n] = ("sbuf", [128, _w], F32)
 for _n, _w in (("gqi", 28), ("gmi", 28), ("pi", 8), ("uli", 16)):
     SCRATCH[_n] = ("sbuf", [128, _w], I32)
 for _k in range(8):
     SCRATCH["P%d" % _k] = ("psum", [128, 512], F32)
-SEMAPHORES = ["v", "s", "t", "gc"] + ["d%d" % k for k in range(40)] + ["arr%d" % k for k in range(9)] + ["snt"]
+SEMAPHORES = ["v", "s", "t", "gc"] + ["d%d" % k for k in range(60)] + ["arr%d" % k for k in range(9)] + ["snt"]
 
 
 def rank_program(g, core, T, topo):
@@ -141,9 +143,9 @@ def rank_program(g, core, T, topo):
 
     place = {}
 
-    def col(name):
+    def col(name, a=0):
         k = place.setdefault(name, len(place))
-        return T.cq[:, k:k + 1]
+        return T.cq[a:128, k:k + 1]
 
     def icol(name):
         k = ("pi", "p16", "p4", "p1", "grp").index(name)
@@ -163,13 +165,19 @@ def rank_program(g, core, T, topo):
     dma("y", [(T.vv[:], T.v[:])], [], ["vv"])
 
     def score(src, key, c, k):
-        a, b = (VPARTS if c == "vc" else PARTS)[k]
+        a, b = PARTS[k]
         quant(cols(key, a, b), [c + str(k)], c, a, b, src, 4 * a)
         mm(["uqc", "uqs", c + str(k)], ["P%d" % k], T["P%d" % k][:, 0:b - a], "uq", 0, c, a, b - a)
 
-    def sign(k, f=act, parts=PARTS):
-        a, b = parts[k]
+    def sign(k, f=act):
+        a, b = PARTS[k]
         f(["P%d" % k], ["sg%d" % k], T.sg[:, a:b], T["P%d" % k][:, 0:b - a])
+
+    def early_signs():
+        ts(["sg0", "loU"], ["mge"], T.mg[:, 0:16 * EARLY], T.sg[:, 0:16 * EARLY].indirect(T.loU[:, 0:EARLY]), 0.0, A.is_gt, -0.5, A.add)
+
+    def early_scan():
+        scan(["seg16", "mge"], ["s3e"], T.s3[:, 0:48 * EARLY:3], T.seg16[:, 0:16 * EARLY], T.mg[:, 0:16 * EARLY])
 
     def halve(src, key, a, b):
         act(cols(key, a, b), cols("xh", a, b), T.xh[:, 4 * a:4 * b], src[:, 4 * a:4 * b], F.Copy, scale=0.5)
@@ -184,49 +192,56 @@ def rank_program(g, core, T, topo):
         return lambda: quant(["ebi"], ["ebc%d" % b], "ebc", 128 * b, 128 * b + 128, T.eb, 4 - b)
 
     def halves(reads, key, out, a, s1, o1, s2, o2):
-        ts(reads, [key + "a"], out(0, 14), a(0, 14), s1[0], o1, s2[0], o2)
-        ts(reads, [key + "b"], out(14, 28), a(14, 28), s1[1], o1, s2[1], o2)
+        ts(reads, [key + "a"], out(0, NV), a(0, NV), s1[0], o1, s2[0], o2)
+        ts(reads, [key + "b"], out(NV, 28), a(NV, 28), s1[1], o1, s2[1], o2)
+
+    def tab(d, k, e, a=0, b=28):
+        return T["tb" + d][:, 84 * k + 3 * a + e:84 * k + 3 * b:3]
 
     def tables(d):
-        w, dg, hi, lw = T["w" + d], T["d" + d], T["hi" + d], T["lw" + d]
+        w, hi, lw = tab(d, 2, 2) if d == "F" else T.wB[:], tab(d, 0, 2), tab(d, 1, 2)
+        dh, dk = ((lambda a, b: tab(d, 2, 1, a, b)), "dhF") if d == "F" else ((lambda a, b: T.ds[:, a:b]), "ds")
         return [
             lambda: scan(["seg16"] + both("rowt"), ["sn"], T.sn[:], T.seg16[:], T.rowt[:]),
             lambda: (ts(["sn", "kaph"], ["tq"], T.tq[:, 0:28], T.sn[:, 15:C:16], col("kaph"), A.mult),
                      halves(["sn", "kaph", "kap"], "tk", lambda a, b: T.tq[:, 28 + a:28 + b], lambda a, b: T.sn[:, 16 * a + 15:16 * b:16],
                             (col("kap"), col("kaph")), A.mult, (col("kap"), col("kap")), A.mult)),
-            lambda: (tt(["tq", "hq"], ["wq" + d], w[:], T.tq[:, 0:28], T.hq[:, 0:28], A.add),
-                     tt(["tka", "tkb", "hka", "hkb"], ["dh" + d], dg[:, 56:84], T.tq[:, 28:56], T.hq[:, 28:56], A.subtract)),
-            lambda: (ts(["wq" + d], ["hi" + d], hi[:], w[:], M, A.add, -M, A.add),
-                     halves(["dh" + d, "km", "km2"], "dhi" + d, lambda a, b: dg[:, a:b], lambda a, b: dg[:, 56 + a:56 + b],
-                            (col("km2"), col("km")), A.add, (col("km2"), col("km")), A.subtract)),
-            lambda: (tt(["hi" + d, "wq" + d], ["lw" + d], lw[:], w[:], hi[:], A.subtract),
-                     tt(["dhi%sa" % d, "dhi%sb" % d, "dh" + d], ["dlo" + d, "dhi" + d], dg[:, 28:56], dg[:, 56:84], dg[:, 0:28], A.subtract)),
+            lambda: (tt(["tq", "hq"], ["wq" + d], w, T.tq[:, 0:28], T.hq[:, 0:28], A.add),
+                     tt(["tka", "tkb", "hka", "hkb"], [dk], dh(0, 28), T.tq[:, 28:56], T.hq[:, 28:56], A.subtract)),
+            lambda: (ts(["wq" + d], ["hi" + d], hi, w, M, A.add, -M, A.add),
+                     halves([dk, "km", "km2"], "dhi" + d, lambda a, b: tab(d, 0, 1, a, b), dh, (col("km2"), col("km")), A.add, (col("km2"), col("km")), A.subtract)),
+            lambda: (tt(["hi" + d, "wq" + d], ["lw" + d], lw, w, hi, A.subtract),
+                     tt(["dhi%sa" % d, "dhi%sb" % d, dk], ["dlo" + d, "dhi" + d], tab(d, 1, 1), dh(0, 28), tab(d, 0, 1), A.subtract)),
         ]
 
     def back_tables():
         tb = tables("B")
         return [
-            lambda: scan(["seg16", "rowqi"], ["sn"], T.sn[:], T.seg16[:], T.rowqi[:]),
-            lambda: (ts(["sn", "kap"], ["qiU"], T.qiU[:], T.sn[:, 15:C:16], col("kap"), A.mult, 224.25, A.add),
-                     ts(["sn", "kaph"], ["hq"], T.hq[:, 0:28], T.sn[:, 15:C:16], col("kaph"), A.mult),
+            lambda: dma("y", [(T.rowqs[16:128, :], T.rowqi[0:112, :]), (T.rowqs[0:16, :], T.rowqi[112:128, :])], ["rowqi"], ["rowqs"]),
+            lambda: gather(T.rowt, 0, "rowt", T.rowqs[:, 0:C], ["rowqs"], T.mU, 0, ["mU"], 0),
+            lambda: scan(["seg16", "rowqs"], ["sn"], T.sn[:], T.seg16[:], T.rowqs[:]),
+            lambda: (ts(["sn", "kaph"], ["hq"], T.hq[:, 0:28], T.sn[:, 15:C:16], col("kaph"), A.mult),
                      halves(["sn", "kaph", "kap"], "hk", lambda a, b: T.hq[:, 28 + a:28 + b], lambda a, b: T.sn[:, 16 * a + 15:16 * b:16],
                             (col("kap"), col("kaph")), A.mult, (col("kap"), col("kap")), A.mult)),
-            lambda: gather(T.rowt, 0, "rowt", T.rowm[:, 0:C], both("rowm"), T.qiU, 0, ["qiU"], 0),
-            tb[0], tb[1],
-            lambda: (tt(["tq", "hq"], ["lo"], T.lo[:], T.tq[:, 0:28], T.hq[:, 0:28], A.min), tb[2]()),
-            lambda: (ts(["lo"], ["loB"], T.loB[:], T.lo[:], 2.0, A.mult, 224.25, A.add), tb[3]()),
-            tb[4],
+        ] + tb + [
+            lambda: (tt(["gmi", "iw"], ["tO0"], T.tO[:, 0:28], T.gmi[:], T.iw[:], A.add),
+                     tt(["gmi", "iw"], ["tO1"], T.tO[:, 28:56], T.gmi[:], T.iw[:], A.subtract)),
+            lambda: (ts(["tO0"], ["wO"], tab("B", 2, 2), T.tO[:, 0:28], 0.5, A.mult, -224.0, A.add),
+                     ts(["tO1", "kap"], ["dhB0"], tab("B", 2, 1, 0, NV), T.tO[:, 28:28 + NV], col("kap"), A.mult),
+                     ts(["tO1", "kaph"], ["dhB"], tab("B", 2, 1, NV, 28), T.tO[:, 28 + NV:56], col("kaph"), A.mult)),
         ]
 
     iota("pi", icol("pi"), [[0, 1]], 0, 1, False)
     iota("j16", T.j16[:], [[1, 16]], 0, 0)
+    iota("j4", T.j4[:], [[0, 4], [1, 4]], 0, 0)
     iota("iot", T.iot[:, 0:C], [[1, C]], -224, 0)
     iota("iwb", T.iwb[:], [[16, 28]], 0, 0)
-    iota("uli", T.uli[:, 0:8], [[16, 8]], -16, 0, False)
-    iota("j4", T.j4[:], [[0, 4], [1, 4]], 0, 0)
+    iota("uli", T.uli[:, 1:8], [[16, 7]], 0, 0, False)
+    iota("uli0", T.uli[:, 0:1], [[0, 1]], 112, 0, False)
     fill(["z"], T.zt[:], 0.0)
+    op("g", ["z"], ["wi"], lambda: g.affine_select(T.wt[:, C:960], T.zt[:, 0:512], [[1, 128], [0, 4]], A.not_equal, 1.0, 0, -1))
+    op("g", ["z"], ["ebi"], lambda: g.affine_select(T.eb[:], T.zt[:], [[1, 520]], A.not_equal, 1.0, -4, -4))
     ts(["pi"], ["p16"], icol("p16"), icol("pi"), 15, A.bitwise_and)
-    const("cp", "pi", 0.0, A.add)
     ts(["pi"], ["p4"], icol("p4"), icol("pi"), 2, A.arith_shift_right, 3, A.bitwise_and)
     ts(["pi"], ["p1"], icol("p1"), icol("pi"), 3, A.bitwise_and)
     ts(["pi"], ["grp"], icol("grp"), icol("pi"), 4, A.arith_shift_right)
@@ -238,165 +253,201 @@ def rank_program(g, core, T, topo):
     ts(["j16", "c16"], ["sa"], T.sa[:, 0:16], T.j16[:], col("c16"), A.not_equal)
     ts(["j16", "c16n"], ["sb"], T.sb[:, 0:16], T.j16[:], col("c16n"), A.is_equal, K, A.mult)
     ts(["z", "c16"], ["rep"], T.rep[:], T.zt[:, 0:28], col("c16"), A.add)
+    const("c896", "p1", 896.25, A.add)
+    const("cg", "grp", 0.0, A.add)
     const("kaph", "kap", 0.5, A.mult)
-    const("km", "kap", M, A.mult)
-    const("km2", "kap", 2 * M, A.mult)
     tt(["sa", "sb"], ["sp"], T.sp[:, 0:16], T.sa[:, 0:16], T.sb[:, 0:16], A.max)
-    act(["z"], ["wt1"], T.wt[:, C:960], T.zt[:])
     act(["z"], ["wt0"], T.wt[:, 0:C], T.zt[:, 0:C])
+    act(["z"], ["wt2"], T.wt[:, 960:1408], T.zt[:, 0:C])
+    for d in "FB":
+        act(["z"], ["t0" + d], T["tb" + d][:, 0:252:3], T.zt[:, 0:84])
     act(["sp", "rep"], ["seg16"], T.seg16[:], T.sp[:, 0:16].indirect(T.rep[:, 0:28]))
-    quant(["z"], ["zcr"], "zc", 84, 212, T.zt, 0)
-    ts(["iot", "cp"], ["ident"], T.ident[:], T.iot[:, 224:352], col("cp"), A.is_equal)
+    quant(["z"], ["zcr", "zc"], "zc", 0, 128, T.zt, 0)
+    quant(["z"], ["zcs"], "zc", 128, 256, T.zt, 0)
+    fill(["s30"], T.s3[:, 29:1360:48], 0.0)
+    fill(["s31"], T.s3[:, 13:1360:48], 1.0)
+    ts(["j4", "c4"], ["sa4"], T.sa[:, 16:32], T.j4[:], col("c4"), A.not_equal)
+    ts(["j4", "c4n"], ["sb4"], T.sb[:, 16:32], T.j4[:], col("c4n"), A.is_equal, K, A.mult)
+    ts(["iwb", "c16"], ["iw"], T.iw[:], T.iwb[:], col("c16"), A.add)
     cp(["gqi"], ["qU"], T.qU[:], T.gqi[:])
     cp(["gmi"], ["mU"], T.mU[:], T.gmi[:])
+    tt(["sa4", "sb4"], ["sp4"], T.sp[:, 16:32], T.sa[:, 16:32], T.sb[:, 16:32], A.max)
     ts(["gqi"], ["hq"], T.hq[:, 0:28], T.gqi[:], 0.5, A.mult, -112.0, A.add)
     halves(["gqi", "kaph", "kap"], "hk", lambda a, b: T.hq[:, 28 + a:28 + b], lambda a, b: T.gqi[:, a:b], (-224.0, -224.0), A.add, (col("kap"), col("kaph")), A.mult)
     gather(T.rowq, 0, "rowq", T.iot[:, 0:C], ["iot"], T.qU, 0, ["qU"], 14)
-    act(["z"], ["wt2"], T.wt[:, 960:1408], T.zt[:, 0:C])
-    ts(["uli"], ["uli2"], T.uli[:, 8:16], T.uli[:, 0:8], 127, A.bitwise_and)
-    ts(["iwb", "c16"], ["iw"], T.iw[:], T.iwb[:], col("c16"), A.add)
+    tt(["gmi", "iw"], ["lo"], T.lo[:], T.gmi[:], T.iw[:], A.min)
+    cp(["uli", "uli0"], ["ulist"], T.ulist[:], T.uli[:, 0:8])
+    gather(T.rowt, 0, "rowt", T.rowq[:, 0:C], both("rowq"), T.mU, 0, ["mU"], 14)
     quant(["ut"], ["uc"], "uc", 0, 128, T.ut, 0)
-    cp(["uli2"], ["ulist"], T.ulist[:], T.uli[:, 8:16])
-    gather(T.rowt, 0, "rowt", T.rowq[:, 0:C], both("rowq"), T.mU, 0, ["mU"], 16)
-    act(["uc", "ulist"], ["uqs"], T.uqp[:, 0:128], T.ucp[:, 0:128].indirect(T.ulist[:, 0:8]))
-    for t in range(2):
-        act(["ident", "wt1"], ["wi%d" % t], T.wt[:, C + t:960:4], T.ident[:])
-    cp(["uc", "ulist"], ["uqc"], T.uq[:, 0:128].bitcast(dt.uint32), T.uc[:, 0:128].bitcast(dt.uint32).indirect(T.ulist[:, 0:8]))
+    cp(["lo"], ["loU"], T.loU[:], T.lo[:])
     tf = tables("F")
     tf[0]()
-    tt(["gmi", "iw"], ["lo"], T.lo[:], T.gmi[:], T.iw[:], A.min)
-    ts(["j4", "c4"], ["sa4"], T.sa[:, 16:32], T.j4[:], col("c4"), A.not_equal)
-    ts(["j4", "c4n"], ["sb4"], T.sb[:, 16:32], T.j4[:], col("c4n"), A.is_equal, K, A.mult)
-    tf[1]()
+    act(["uc", "ulist"], ["uqs"], T.uqp[:, 0:128], T.ucp[:, 0:128].indirect(T.ulist[:, 0:8]))
+    cp(["uc", "ulist"], ["uqc"], T.uq[:, 0:128].bitcast(dt.uint32), T.uc[:, 0:128].bitcast(dt.uint32).indirect(T.ulist[:, 0:8]))
     score(T.x0, "x0", "xc", 0)
-    tf[2]()
-    cp(["lo"], ["loF"], T.loF[:], T.lo[:])
+    tf[1]()
+
+    def aconst(name, src, f, scale, bias, more=()):
+        act([src] + list(more), [name], col(name), col(src), f, scale=scale, bias=bias)
+    aconst("km", "kap", F.Identity, M, 0.0)
+    aconst("km2", "kap", F.Identity, 2 * M, 0.0)
+    aconst("r4", "cg", F.Relu, 448.0, 0.25 - 4 * C)
+    aconst("r6", "cg", F.Relu, 1.0, -6.0)
+    aconst("rF", "cg", F.Relu, -448.0, 4.0 * C)
+    aconst("r2", "c4", F.Relu, 1.0, -2.0)
+    aconst("cg7", "r6", F.Identity, -1.0, 1.0)
+    aconst("cgk", "r6", F.Identity, -224.0, col("r4"), ["r4"])
+    aconst("cfF", "rF", F.Identity, -1.0, 224.25 + 4 * C)
+    aconst("k4", "r2", F.Identity, 4.0, 4 / K)
+    act(["iw", "cg7", "cgk"], ["tabC"], T.tabC[:], T.iw[:], F.Identity, scale=col("cg7"), bias=col("cgk"))
+
+    def back_constants():
+        aconst("rB", "cg", F.Relu, 448.0, -3.0 * C)
+        aconst("c8", "cg", F.Relu, -448.0, 3.0 * C)
+        aconst("kap2", "kap", F.Identity, -2.0, 0.0)
+        aconst("r14", "c16", F.Relu, 1.0, -14.0)
+        aconst("cfB", "rB", F.Identity, -1.0, 224.25 + 4 * C)
+        aconst("kq", "r14", F.Identity, 1 / K - 1, 1.0)
     score(T.x0, "x0", "xc", 1)
-    tt(["sa4", "sb4"], ["sp4"], T.sp[:, 16:32], T.sa[:, 16:32], T.sb[:, 16:32], A.max)
+    tf[2]()
     score(T.x0, "x0", "xc", 2)
-    tf[3]()
-    halve(T.x0, "x0", 0, 128)
     sign(0)
     sign(1)
-    quant(["wt0", "wt2", "wi0", "wi1"], ["shc"], "shc", 0, 352, T.wt, 0)
-    sign(2, cp)
+    tf[3]()
+    quant(["wt0", "wt2", "wi"], ["shc"], "shc", 0, 352, T.wt, 0)
+    early_signs()
+    sign(2)
     tf[4]()
+    scatter(0, 4)()
+    early_scan()
 
-    def late_constants():
-        return [
-            lambda: (const("cg7", "grp", 7.0, A.is_lt), const("c7", "grp", 7.0, A.is_equal, -224.0, A.mult), const("cg", "grp", 4.0, A.max, 448.0, A.mult),
-                     const("cfa", "grp", 4.0, A.min, 448.0, A.mult)),
-            lambda: (ts(["cg", "c7"], ["cgk"], col("cgk"), col("cg"), col("c7"), A.add, 0.25 - 4 * C, A.add), const("cfF", "cfa", 224.25, A.add),
-                     const("kin", "p4", 3.0, A.is_equal, 1 / K, A.max), const("c896", "p1", 896.25, A.add)),
-            lambda: (ts(["iw", "cg7", "cgk"], ["tabC"], T.tabC[:], T.iw[:], col("cg7"), A.mult, col("cgk"), A.add), const("k4", "kin", 4.0, A.mult)),
-            lambda: (const("c8a", "grp", 3.0, A.min, -448.0, A.mult), const("cfb", "grp", 3.0, A.max, -448.0, A.mult), const("kap2", "kap", -2.0, A.mult),
-                     const("kq", "p16", 15.0, A.not_equal, 1 / K, A.max)),
-            lambda: (const("c8", "c8a", 3.0 * C, A.add), const("cfB", "cfb", 224.25 + 7 * C, A.add)),
-        ]
+    SC = ["sc"]
 
     def chain(d, way, shares, vgap, sgap):
         def gap(name):
             for f in vgap.get(name, []) + sgap.get(name, []):
                 f()
-        dg, w = T["d" + d], T["w" + d]
-        keys = ["sg0", "sg1", "sg2", "lo" + d]
-        ts(keys, ["mgv"], T.mg[:, 0:224], T.sg[:, 0:C].indirect(T["lo" + d][:, 0:14]), 0.0, A.is_gt, -0.5, A.add)
-        act(keys, ["mgs"], T.mg[:, 224:C], T.sg[:, 0:C].indirect(T["lo" + d][:, 14:28]), F.Sign, bias=-(2.0 ** -93))
+        wk = "wqF" if d == "F" else "wO"
+        ts(["sg0", "sg1", "loU"], ["mgv"], T.mg[:, 16 * EARLY:16 * NV], T.sg[:, 0:16 * NV].indirect(T.loU[:, EARLY:NV]), 0.0, A.is_gt, -0.5, A.add)
+        act(["sg0", "sg1", "sg2", "loU"], ["mgs"], T.mg[:, 16 * NV:C], T.sg[:, 0:C].indirect(T.loU[:, NV:28]), F.Sign, bias=-(2.0 ** -93))
         gap("signs")
-        scan(["seg16"] + both("mg"), ["sc"], T.sc[:], T.seg16[:], T.mg[:])
+        scan(["seg16", "mgv"], ["s3m"], T.s3[:, 48 * EARLY:48 * NV:3], T.seg16[:, 16 * EARLY:16 * NV], T.mg[:, 16 * EARLY:16 * NV])
+        scan(["seg16", "mgs"], ["s3l"], T.s3[:, 48 * NV:3 * C:3], T.seg16[:, 16 * NV:C], T.mg[:, 16 * NV:C])
         gap("scan")
-        s = T.sc[:, 15:C:16]
-        tt(["sc", "dhi" + d], ["u0"], T.uu[:, 0:28], s, dg[:, 0:28], A.mult)
-        tt(["sc", "dlo" + d], ["u1"], T.uu[:, 28:56], s, dg[:, 28:56], A.mult)
-        tt(["sc", "dh" + d], ["t3"], T.t3[:], s, dg[:, 56:84], A.mult)
+        made = ((0, ["dhi" + d, "hi" + d], ["z0", "z"], T.zt[:, 0:336:4]), (1, ["dlo" + d, "lw" + d], ["z1"], T.zt[:, 1:336:4]),
+                (2, ["dh" + d, wk] + ["dhB0"] * (d == "B"), ["t4"], T.t4[:]))
+        for k, keys, okeys, out in made:
+            op("v", ["s3e", "s3m", "s3l", "s30", "s31", "t0" + d] + keys, okeys,
+               lambda: g.vector.tensor_tensor_scan(out, T["tb" + d][:, 84 * k:84 * k + 84], T.s3[:, 29:1358:16], 0.0, A.add, A.mult))
         gap("times")
-        tt(["u0", "hi" + d], ["z0", "z"], T.zt[:, 336:C:4], T.uu[:, 0:28], T["hi" + d][:], A.add)
-        tt(["u1", "lw" + d], ["z1"], T.zt[:, 337:C:4], T.uu[:, 28:56], T["lw" + d][:], A.add)
-        tt(["t3", "wq" + d], ["t4"], T.t4[:], T.t3[:], w[:], A.add)
-        gap("plus")
-        quant(["z0", "z1"], ["zc"], "zc", 0, 128, T.zt, 0)
-        ts(["t4"], ["ls0"], T.ls[:, 0:28], T.t4[:], 224.25, A.add)
-        for bank, ns in (("P0", (5,)), ("P3", (1,)), ("P1", (6, 2, 3, 4)), ("P2", (7,))):
-            need("t", deps(["zc", "zcr", "shc"], [bank]))
+        quant(["z0", "z1"], ["zc"], "zc", 84, 212, T.zt, 0)
+        ts(["t4"], ["ls0"], T.ls0[:], T.t4[:, 2:84:3], 224.25, A.add)
+        for bank, ns in (("P0", (5,)), ("P3", (1,)), ("P1", (6, 2)), ("P2", (3, 4)), ("P4", (7,))):
+            need("t", deps(["zc", "zcr", "zcs", "shc"], [bank]))
             for k, n in enumerate(ns):
-                s0, z0 = 112 + way * 16 * n, 84 - 28 * k
-                i = g.tensor.matmul_mx(T[bank][:, 0:128], T.shc[:, s0:s0 + 128], T.shcp[:, s0:s0 + 128], T.zc[:, z0:z0 + 128], T.zcp[:, z0:z0 + 128], n == ns[0], n == ns[-1])
+                s0, z0, e = 112 + way * 16 * n, 84 - 84 * k, max(128, 84 * len(ns))
+                i = g.tensor.matmul_mx(T[bank][:, 0:e], T.shc[:, s0:s0 + 128], T.shcp[:, s0:s0 + 128], T.zc[:, z0:z0 + e], T.zcp[:, z0:z0 + e], n == ns[0], n == ns[-1])
             count["t"] = count.get("t", 0) + 1
             i.then_inc(T.sem["t"], 1)
-            done(("t", count["t"], dict(known["t"])), ["zc", "zcr", "shc"], [bank])
+            done(("t", count["t"], dict(known["t"])), ["zc", "zcr", "zcs", "shc"], [bank])
         gap("list")
+        ls = T.ls
 
-        def left(n):
-            gather(T.R, n * C, "L%d" % n, T.R[:, (n - 1) * C:n * C], both("L%d" % (n - 1)), T.ls, (56, 112, 140, 168)[n - 1], ["ls1" if n == 1 else "lsB"], shares.get("L%d" % n, 14))
-            gap("L%d" % n)
+        def left(n, l0, lk):
+            gather(T.R, n * C, "L%d" % n, T.R[:, (n - 1) * C:n * C], both("L%d" % (n - 1)), ls, l0, [lk], shares.get("L%d" % n, 14))
 
-        def right(n, whole=False):
-            lst, l0, lk = ((T.ls, 28, "lsA"), (T.ls, 84, "lsB"), (T.ls, 196, "lsC"), (T.a8, 0, "a8"))[n]
-            a = 0 if whole else n
-            gather(T.iot, (n + 1) * C, "Q%d" % n, T.iot[:, a * C:(n + 1) * C], ["iot"] + [k for i in range(max(a - 1, 0), n) for k in both("Q%d" % i)], lst, l0, [lk], shares.get("Q%d" % n, 14))
-            if n == 0:
-                ts(["P1"], ["lsB"], T.ls[:, 84:196], T.P1[:, 0:112], 224.25, A.add)
-            if n == 1 and d == "F":
-                cp(["tC"], ["lsC"], T.ls[:, 196:224], T.tC[:])
-            gap("Q%d" % n)
+        def right(n, l0, lk, a):
+            gather(T.iot, (n + 1) * C, "Q%d" % n, T.iot[:, a * C:(n + 1) * C], ["iot"] + [k for i in range(max(a - 1, 0), n) for k in both("Q%d" % i)], ls, l0, [lk], shares.get("Q%d" % n, 14))
 
-        def wrap(n):
-            scan(["seg16"] + both("Q%d" % n), ["sc"], T.sc[:], T.seg16[:], T.iot[:, (n + 1) * C:(n + 2) * C])
-            gap("wrap")
+        def last_list():
+            ts(SC + ["kap", "cf" + d], ["lf"], T.lf[:], T.sc[:, 15:C:16], col("kap"), A.mult, col("cf" + d), A.add)
 
-        gather(T.R, 0, "L0", T.iot[:, 0:C], ["iot"], T.ls, 0, ["ls0"], shares.get("L0", 8))
-        ts(["P0"], ["lsA"], T.ls[:, 28:56], T.P0[:, 0:28], 224.25, A.add)
-        ts(["P3"], ["ls1"], T.ls[:, 56:84], T.P3[:, 0:28], 224.25, A.add)
+        gather(T.R, 0, "L0", T.iot[:, 0:C], ["iot"], T.ls0, 0, ["ls0"], shares.get("L0", 8))
+        ts(["P0"], ["lsA"], ls[:, 0:28], T.P0[:, 2:84:3], 224.25, A.add)
+        ts(["P3"], ["ls1"], ls[:, 28:56], T.P3[:, 2:84:3], 224.25, A.add)
         gap("L0")
-        right(0)
-        left(1)
+        right(0, 0, "lsA", 0)
+        ts(["P1"], ["lsG"], ls[:, 56:112], T.P1[:, 2:168:3], 224.25, A.add)
+        gap("Q0")
+        left(1, 28, "ls1")
+        ts(["P2"], ["lsH"], ls[:, 112:168], T.P2[:, 2:168:3], 224.25, A.add)
         if d == "F":
-            tt(["P2", "tabC"], ["tC"], T.tC[:], T.P2[:, 0:28], T.tabC[:], A.add)
+            tt(["P4", "tabC"], ["tC"], T.tC[:], T.P4[:, 2:84:3], T.tabC[:], A.add)
+            gap("L1")
+            right(1, 56, "lsG", 1)
+            cp(["tC"], ["lsC"], ls[:, 168:196], T.tC[:])
+            gap("Q1")
+            left(2, 84, "lsG")
+            gap("L2")
+            right(2, 168, "lsC", 0)
+            gap("Q2")
+            left(3, 112, "lsH")
+            scan(["seg16"] + both("Q2"), SC, T.sc[:], T.seg16[:], T.iot[:, 3 * C:4 * C])
+            gap("L3")
+            left(4, 140, "lsH")
+            last_list()
+            gap("L4")
         else:
-            ts(["P2"], ["lsC"], T.ls[:, 196:224], T.P2[:, 0:28], 224.25, A.add)
-        right(1)
-        left(2)
-        right(2, d == "F")
-        left(3)
-        if d == "F":
-            wrap(2)
-            left(4)
-        else:
-            right(3, True)
-            left(4)
-            wrap(3)
-        ts(["sc", "kap", "cf" + d], ["lf"], T.lf[:], T.sc[:, 15:C:16], col("kap"), A.mult, col("cf" + d), A.add)
-        gap("fin")
+            ts(["P4"], ["lsC"], ls[:, 168:196], T.P4[:, 2:84:3], 224.25, A.add)
+            gap("L1")
+            right(1, 56, "lsG", 1)
+            gap("Q1")
+            left(2, 84, "lsG")
+            gap("L2")
+            right(2, 168, "lsC", 2)
+            gap("Q2")
+            left(3, 112, "lsH")
+            gap("L3")
+            right(3, 196, "a8", 0)
+            gap("Q3")
+            left(4, 140, "lsH")
+            gap("L4")
+            scan(["seg16"] + both("Q3"), SC, T.sc[:], T.seg16[:], T.iot[:, 4 * C:5 * C])
+            gap("wrap")
+            last_list()
+            gap("fin")
         row = "arow" if d == "F" else "brow"
-        gather(T[row], 0, row, T.R[:, 0:5 * C], [k for i in range(5) for k in both("L%d" % i)], T.lf, 0, ["lf"], shares.get("last", 14))
+        gather(T[row], 0, row, T.R[:, 0:5 * C], [k for i in range(5) for k in both("L%d" % i)], T.lf, 0, ["lf"], shares.get("last", HEAD // 16))
         gap("last")
-        scan(["seg4"] + both(row), ["sc4"], T.sc4[:], T.seg4[:], T[row][:])
+        scan(["seg4", row + "v"], ["sc4a"], T.sc4[:, 0:HEAD], T.seg4[:, 0:HEAD], T[row][:, 0:HEAD])
+        scan(["seg4"] + both(row), ["sc4b"], T.sc4[:, HEAD:C], T.seg4[:, HEAD:C], T[row][:, HEAD:C])
         gap("scan4")
-        ts(["sc4", "k4", "c896"], ["l4"], T.l4[:], T.sc4[:, 3:C:4], col("k4"), A.mult, col("c896"), A.add)
+        ts(["sc4a", "k4", "c896"], ["l4a"], T.l4[:, 0:HEAD // 4], T.sc4[:, 3:HEAD:4], col("k4"), A.mult, col("c896"), A.add)
+        ts(["sc4b", "k4", "c896"], ["l4b"], T.l4[:, HEAD // 4:], T.sc4[:, HEAD + 3:C:4], col("k4"), A.mult, col("c896"), A.add)
         gap("l4")
 
     def move(out, okey, win, wkeys, base, bkey, a, b):
-        tt(wkeys + ["l4"] + cols(bkey, a, b), cols(okey, a, b), out[:, 4 * a:4 * b], win[:, 0:4 * C].indirect(T.l4[:, a // 4:b // 4]), base[:, 4 * a:4 * b], A.add)
+        tt(wkeys + ["l4a"] + ["l4b"] * (b > HEAD) + cols(bkey, a, b), cols(okey, a, b), out[:, 4 * a:4 * b], win[:, 0:4 * C].indirect(T.l4[:, a // 4:b // 4]), base[:, 4 * a:4 * b], A.add)
 
     def fetch(win, wkeys, a, b):
-        act(wkeys + ["l4"], cols("tg", a, b), T.tg[:, 4 * a:4 * b], win[:, 0:4 * C].indirect(T.l4[:, a // 4:b // 4]))
+        act(wkeys + ["l4b"], cols("tg", a, b), T.tg[:, 4 * a:4 * b], win[:, 0:4 * C].indirect(T.l4[:, a // 4:b // 4]))
 
     def add(out, okey, base, bkey, a, b):
         tt(cols("tg", a, b) + cols(bkey, a, b), cols(okey, a, b), out[:, 4 * a:4 * b], T.tg[:, 4 * a:4 * b], base[:, 4 * a:4 * b], A.add)
 
-    def turn_row(d):
-        act(["df0", "df1", "lo" + d, "kap", "kap2"], ["nu" + d], T["nu" + d][:], T.df[:, 0:C].indirect(T["lo" + d][:, 0:28]), F.Identity, bias=col("kap"), scale=col("kap2"))
+    def turn_row():
+        act(["df0", "df1", "loU", "kap", "kap2"], ["nu"], T.nu[:], T.df[:, 0:C].indirect(T.loU[:, 0:28]), F.Identity, bias=col("kap"), scale=col("kap2"))
 
-    def turn_scan(d):
-        scan(["seg16", "nu" + d], ["sn"], T.sn[:], T.seg16[:], T["nu" + d][:])
+    def turn_scan():
+        scan(["seg16", "nu"], ["sn"], T.sn[:], T.seg16[:], T.nu[:])
 
     def turn(d):
         for k, name in enumerate(("dhi", "dlo", "dh")):
-            v = T["d" + d][:, 28 * k:28 * k + 28]
+            v = tab(d, k, 1)
             tt(["sn"], [name + d], v, v, T.sn[:, 15:C:16], A.mult)
 
     def differ(k):
         tt(both("brow") + ["agrow", "ag0"], ["df%d" % k], T.df[:, 224 * k:224 * k + 224], T.brow[:, 224 * k:224 * k + 224], T.agrow[:, 224 * k:224 * k + 224], A.not_equal)
+
+    def wrap_a8():
+        scan(["seg16"] + both("arow"), ["sm"], T.sm[:], T.seg16[:], T.arow[:])
+
+    def list_a8():
+        ts(["sm", "kap"], ["a8w"], T.a8w[:], T.sm[:, 15:C:16], col("kap"), A.mult, 224.25, A.add)
+
+    def spread_n8():
+        ts(["sm", "kap"], ["n8w"], T.n8w[:], T.sm[:, 15:C:16], col("kap"), A.mult, 224.25, A.add)
+        dma("y", [(T.a8r[16 * k:16 * k + 16, :], T.n8w[112:128, :]) for k in range(8)], ["n8w"], ["a8r"])
 
     XH = cols("xh", 0, C)
     DD = ["dd%d%d" % (h, b) for h in range(len(HRUNS)) for b in range(4)]
@@ -405,28 +456,26 @@ def rank_program(g, core, T, topo):
         hc, lc = "hc%d" % r, "lc%d" % r
         src, skey = (T.x0, "x0") if r == 0 else (T.xt, "xt")
         if r == 0:
-            bt, late = back_tables(), late_constants()
-            vgap = {"signs": [scatter(0, 4)], "scan": [scatter(4, 8)], "times": [late[0]], "plus": [late[1]], "list": [late[2], scatter(8, 12)], "L0": [scatter(12, 14)],
-                    "Q0": [scatter(14, 18)], "Q1": [scatter(18, 22)], "L2": [scatter(22, 28)], "L3": [bt[0]], "wrap": [bt[1]],
-                    "last": [bt[2], late[3]], "scan4": [late[4], lambda: fill(["eb"], T.eb[:], 0.0)]}
-            sgap = {"signs": [lambda: halve(src, skey, 128, CUT), copy_half, lambda: halve(src, skey, CUT, C),
+            bt = back_tables()
+            vgap = {"signs": [scatter(4, 8)], "scan": [scatter(8, 12)], "times": [scatter(12, 14)], "list": [scatter(14, 24)],
+                    "L0": [scatter(24, 28), bt[0]], "Q1": [bt[9]], "L2": [bt[10]], "L3": [bt[2]], "L4": [bt[3]],
+                    "last": [bt[1]], "scan4": [wrap_a8], "l4": [list_a8, bt[4]]}
+            sgap = {"signs": [lambda: halve(src, skey, 0, CUT), copy_half, lambda: halve(src, skey, CUT, 320),
                               lambda: act(["sp4", "rep"], ["seg4"], T.seg4[:], T.sp[:, 16:32].indirect(T.rep[:, 0:28]))],
-                    "L4": [lambda: gather(T.rowm, 0, "rowm", T.iot[:, 0:C], ["iot"], T.mU, 0, ["mU"], 0)]}
-            shares = {"L0": 8, "Q0": 8, "L1": 10, "Q1": 8, "L2": 8, "Q2": 10, "L3": 10, "L4": 20, "last": 20}
+                    "L4": [lambda: halve(src, skey, 320, C)]}
+            sgap["signs"].append(back_constants)
             dma("y", [(T.agrow[0:16, :], T.iot[0:16, 0:C])], ["iot"], ["ag0"])
         else:
-            vgap = {"signs": [lambda: turn("F")]}
-            sgap = {"signs": [lambda: halve(src, skey, 0, CUT), copy_half, lambda: halve(src, skey, CUT, C)],
-                    "last": [lambda: turn_row("B")]}
-            shares = {"Q0": 12, "L4": 12}
-        chain("F", -1, shares, vgap, sgap)
+            vgap = {"signs": [lambda: turn("F")], "scan": [lambda: turn("B")], "scan4": [wrap_a8], "l4": [list_a8]}
+            sgap = {"signs": [lambda: halve(src, skey, 0, CUT), copy_half, lambda: halve(src, skey, CUT, 320)], "last": [lambda: halve(src, skey, 320, C)]}
+        chain("F", -1, SHARES["F0" if r == 0 else "F"], vgap, sgap)
         dma("y", [(T.agrow[16:128, :], T.arow[0:112, :])], both("arow"), ["agrow"])
 
-        def layer(h):
+        def layer(h, bs=range(4)):
             a, e = HRUNS[h]
-            for b in range(4):
+            for b in bs:
                 bank = "P%d" % (4 + b)
-                mm(["wqc", "wqp"] + ["vc%d" % k for k in range(3) if a <= VPARTS[k][0] < e], [bank], T[bank][:, 0:e - a], "wq", 128 * b, "vc", a, e - a)
+                mm(["wqc", "wqp"] + ["vc%d" % k for k in range(3) if a <= PARTS[k][0] < e], [bank], T[bank][:, 0:e - a], "wq", 128 * b, "vc", a, e - a)
 
         def layer_out(h, b):
             a, e = HRUNS[h]
@@ -458,59 +507,56 @@ def rank_program(g, core, T, topo):
             f([bank], ["dd%d%d" % (h, b)], T.dd[:, 4 * a + b:4 * e:4], T[bank][:, 0:e - a])
 
         first = (lambda k: bt[k]()) if r == 0 else (lambda k: None)
-        move(T.vt, "vt", T.xh, XH, T.xg, "xg", 0, 128)
+        move(T.vt, "vt", T.xh, XH, T.xg, "xg", 0, CUT)
         fetch(T.xh, XH, CUT, 320)
         fetch(T.xh, XH, 320, C)
-        first(3)
-        move(T.vt, "vt", T.xh, XH, T.xg, "xg", 128, CUT)
-        first(4)
-        score(T.vt, "vt", "vc", 0)
-        layer(0)
-        sign(0, act, VPARTS)
-        for b in range(4):
-            layer_out(0, b)
-        add(T.vt, "vt", T.xh, "xh", CUT, 320)
+        gather(T.nrow, 0, "nrow", T.rowqi[:, 0:C], ["rowqi"], T.a8w, 0, ["a8w"], 0)
         first(5)
+        add(T.vt, "vt", T.xh, "xh", CUT, 320)
+        first(6)
+        score(T.vt, "vt", "vc", 0)
+        layer(0, (0, 1, 2))
+        sign(0)
+        for b in range(3):
+            layer_out(0, b)
         add(T.vt, "vt", T.xh, "xh", 320, C)
         score(T.vt, "vt", "vc", 1)
+        layer(0, (3,))
+        layer_out(0, 3)
         score(T.vt, "vt", "vc", 2)
         layer(1)
-        sign(1, act, VPARTS)
-        first(6)
-        send(0)
-        scan(["seg16"] + both("arow"), ["sm"], T.sm[:], T.seg16[:], T.arow[:])
-        if r:
-            turn_scan("B")
-        sign(2, cp, VPARTS)
         first(7)
-
-        def spread_a8():
-            ts(["sm", "kap"], ["p16"], T.p16[:], T.sm[:, 15:C:16], col("kap"), A.mult, 224.25, A.add)
-            dma("y", [(T.a8r[16 * k:16 * k + 16, :], T.p16[112:128, :]) for k in range(8)], ["p16"], ["a8r"])
-        vgap = {"signs": [spread_a8], "list": [lambda: send(1)], "L2": [lambda: ts(["a8r", "c8"], ["a8"], T.a8[:], T.a8r[:], col("c8"), A.add)],
+        early_signs()
+        sign(1, cp)
+        sign(2, cp)
+        first(8)
+        early_scan()
+        vgap = {"signs": [lambda: scan(["seg16"] + both("nrow"), ["sm"], T.sm[:], T.seg16[:], T.nrow[:])], "scan": [lambda: send(0)], "times": [spread_n8],
+                "list": [lambda: send(1)], "Q2": [lambda: ts(["a8r", "c8"], ["a8"], T.ls[:, 196:224], T.a8r[:], col("c8"), A.add)],
                 "wrap": [lambda: unpack_out(1, 0, cp)], "fin": [lambda: unpack_out(1, 1, cp)],
                 "scan4": [lambda: differ(0)], "l4": [lambda: differ(1)]}
         if r == 0:
-            vgap["signs"] += [lambda: cp(["ident", "eb"], ["ebi"], T.eb[:, 4:516:4], T.ident[:])]
-            vgap["scan"] = [ebq(0)]
-            vgap["times"] = [ebq(1)]
-            vgap["plus"] = [ebq(2)]
-            vgap["L0"] = [ebq(3)]
-        else:
-            vgap["signs"] += [lambda: turn("B")]
+            vgap["times"] += [ebq(0)]
+            vgap["list"] += [ebq(1)]
+            vgap["L0"] = [ebq(2), ebq(3)]
         if r == 1:
-            vgap["scan"] = [lambda: quant(["vv"], ["vq"], "vq", 0, 128, T.vv, 0)]
+            vgap["L0"] = [lambda: quant(["vv"], ["vq"], "vq", 0, 128, T.vv, 0)]
         if r == 2:
-            vgap["scan"] = [lambda: ts(["dhF", "kq"], ["dq"], T.dq[:, 0:14], T.dF[:, 56:70], -K / 2, A.mult, col("kq"), A.mult),
-                            lambda: ts(["dhF", "kq"], ["dq1"], T.dq[:, 14:28], T.dF[:, 70:84], -K, A.mult, col("kq"), A.mult)]
-        sgap = {"signs": [lambda b=b: layer_out(1, b) for b in range(4)],
-                "L2": [lambda: unpack(0), lambda: unpack(1)], "L4": [lambda b=b: unpack_out(0, b) for b in range(4)],
-                "last": [lambda b=b: unpack_out(1, b) for b in (2, 3)]}
-        chain("B", 1, {"L0": 4, "Q0": 12, "L4": 10}, vgap, sgap)
+            vgap["L0"] = [lambda: ts(["dhF", "kq"], ["dq"], T.dq[:, 1:3 * NV:3], tab("F", 2, 1, 0, NV), -K / 2, A.mult, col("kq"), A.mult),
+                              lambda: ts(["dhF", "kq"], ["dq1"], T.dq[:, 3 * NV + 1:84:3], tab("F", 2, 1, NV, 28), -K, A.mult, col("kq"), A.mult)]
+        sgap = {"signs": [lambda b=b: layer_out(1, b) for b in range(4)] + [lambda e=e: act(["t0F", "wqF"], ["dq%d" % e], T.dq[:, e:84:3], tab("F", 2, e)) for e in (0, 2) if r == 2],
+                "Q2": [lambda: unpack(0), lambda: unpack(1)], "L4": [lambda b=b: unpack_out(0, b) for b in range(2)],
+                "last": [lambda h=h, b=b: unpack_out(h, b) for h, b in ((0, 3), (1, 2), (1, 3))]}
+        vgap["last"] = [lambda: unpack_out(0, 2, cp)]
+        if r == 0:
+            vgap.update({"signs": vgap["scan"], "scan": vgap["signs"], "wrap": [lambda: unpack_out(0, 2, cp)], "fin": [lambda: unpack_out(0, 3, cp)],
+                         "last": [lambda: unpack_out(1, 0, cp)]})
+            sgap["last"] = [lambda b=b: unpack_out(1, b) for b in (1, 2, 3)]
+        chain("B", 1, SHARES["B0" if r == 0 else "B"], vgap, sgap)
         if r < 2:
             fetch(T.dd, DD, CUT, 320)
             fetch(T.dd, DD, 320, C)
-            turn_row("F")
+            turn_row()
             move(T.xt, "xt", T.dd, DD, T.vt, "vt", 0, CUT)
             add(T.xt, "xt", T.vt, "vt", CUT, 320)
             score(T.xt, "xt", "xc", 0)
@@ -519,8 +565,10 @@ def rank_program(g, core, T, topo):
             score(T.xt, "xt", "xc", 1)
             score(T.xt, "xt", "xc", 2)
             sign(1)
-            turn_scan("F")
+            turn_scan()
+            early_signs()
             sign(2, cp)
+            early_scan()
         else:
             def product(k):
                 a, b = PARTS[k]
@@ -533,29 +581,31 @@ def rank_program(g, core, T, topo):
 
             def codes_out(a, b, keys):
                 dma("y", [(T.oc[:, 4 * a:4 * b], T.xc[:, a:b].bitcast(dt.uint8))], keys, ["oc%d" % a])
-            turn_row("F")
-            fetch(T.dd, DD, 288, C)
+            turn_row()
+            fetch(T.dd, DD, 256, 320)
+            fetch(T.dd, DD, 320, C)
             move(T.xt, "xt", T.dd, DD, T.vt, "vt", 0, CUT)
-            turn_scan("F")
+            move(T.xt, "xt", T.dd, DD, T.vt, "vt", CUT, 256)
+            scan(["seg16", "nu"], ["s3e", "s3m", "s3l"], T.s3[:, 0:3 * C:3], T.seg16[:], T.nu[:])
             product(0)
-            codes_out(0, CUT, ["xc0"])
+            e = PARTS[0][1]
+            codes_out(0, e, ["xc0"])
             result(0, act)
-            dma("s", [(T.y[:, 0:CUT], T.ysb[:, 0:CUT])], ["y0"], ["yo0"])
-            tt(["sn", "dq", "dq1"], ["t3"], T.t3[:], T.sn[:, 15:C:16], T.dq[:], A.mult)
-            move(T.xt, "xt", T.dd, DD, T.vt, "vt", CUT, 288)
-            tt(["t3", "wqF"], ["t4"], T.t4[:], T.t3[:], T.wF[:], A.add)
-            add(T.xt, "xt", T.vt, "vt", 288, 320)
+            dma("s", [(T.y[:, 0:e], T.ysb[:, 0:e])], ["y0"], ["yo0"])
+            op("v", ["s3e", "s3m", "s3l", "dq", "dq0", "dq1", "dq2"], ["t4"],
+               lambda: g.vector.tensor_tensor_scan(T.t4[:], T.dq[:], T.s3[:, 29:1358:16], 0.0, A.add, A.mult))
+            add(T.xt, "xt", T.vt, "vt", 256, 320)
+            ts(["t4"], ["qoU"], T.qoU[:], T.t4[:, 2:84:3], 224.25, A.add)
             add(T.xt, "xt", T.vt, "vt", 320, C)
-            ts(["t4"], ["qoU"], T.qoU[:], T.t4[:], 224.25, A.add)
             product(1)
             product(2)
             act(["iot", "qoU"], ["qrow"], T.qrow[:], T.iot[:, 0:C].indirect(T.qoU[:, 0:28]), F.Identity, bias=224.0)
             dma("s", [(T.qo[:], T.qrow[0:128:16, :])], ["qrow"], ["qo"])
-            codes_out(CUT, C, ["xc1", "xc2"])
+            codes_out(e, C, ["xc1", "xc2"])
             result(1, cp)
             result(2, cp)
             dma("y", [(T.osc[4 * k:4 * k + 4, :], T.xcp[32 * k:32 * k + 4, 0:C]) for k in range(4)], ["xc0", "xc1", "xc2"], ["osc"])
-            dma("y", [(T.y[:, CUT:C], T.ysb[:, CUT:C])], ["y1", "y2"], ["yo1"])
+            dma("y", [(T.y[:, e:C], T.ysb[:, e:C])], ["y1", "y2"], ["yo1"])
     for sem in count:
-        if known["g"].get(sem, 0) < count[sem]:
+        if max(known[q].get(sem, 0) for q in queue) < count[sem]:
             g.wait_ge(T.sem[sem], count[sem])

@@ -4,35 +4,37 @@ import comms_topo
 
 STEP = [1, 2, 3]
 C = 448
-PARTS = [(0, 192), (192, 320), (320, C)]
-EARLY, NV = 12, 20
-HRUNS = [(0, 192), (192, C)]
+PARTS = {"xc": [(0, 192), (192, 320), (320, C)], "vc": [(0, 128), (128, 320), (320, C)]}
+EARLY, NV = {"F": 12, "B": 8}, 20
+HRUNS = PARTS["vc"]
+LAYER = [(4, 5, 6, 7), (4, 5, 6, 7), (3, 0, 1, 2)]
+UNPACK = [(0, 1, 2, 3), (4, 5, 6, 7), (0, 1, 2, 3)]
 CUT = HEAD = 224
-SHARES = {"F0": {"L0": 4, "Q0": 8, "L2": 10, "Q2": 10, "L4": 12, "last": 20}, "F": {"L0": 10, "Q0": 12, "L1": 12, "L4": 12},
-          "B0": {"L0": 4, "Q0": 12, "L1": 12, "L4": 10}, "B": {"L0": 6, "Q0": 12, "L1": 12, "L4": 8}}
+SHARES = {"F": {}, "B": {"L4": 6}}
 K = 2.0 ** 24
 M = 1.5 * 2.0 ** 27
+LS = {"one": 0, "twoF": 32, "threeF": 64, "joinF": 96, "twoB": 132, "threeB": 160, "pair": 192, "end": 224}
 BF, F32, I32, U16, MX, U8 = "bfloat16", "float32", "int32", "uint16", "float8_e4m3fn_x4", "uint8"
 
 SCRATCH = {}
 for _n, _w in (("x0", 1792), ("xt", 1792), ("xh", 1792), ("xg", 1792), ("vt", 1792), ("ht", 1792), ("dd", 1792), ("tg", 1792), ("ut", 512), ("vv", 512),
-               ("wt", 1408), ("eb", 520), ("zt", 520), ("R", 5 * C), ("iot", 5 * C),
-               ("j16", 16), ("j4", 16), ("seg16", C), ("seg4", C), ("sa", 32), ("sb", 32), ("sp", 32),
-               ("rowq", C), ("rowqs", C), ("rowqi", C), ("rowt", C), ("arow", C), ("brow", C), ("agrow", C), ("df", C), ("nu", C), ("nrow", C),
-               ("mg", C), ("s3", 1360), ("sc", C), ("sn", C), ("sm", C), ("sc4", C), ("sg", C)):
+               ("wt", 896), ("eb", 520), ("zt", 520), ("R", 6 * C), ("iot", C),
+               ("j16", 17), ("j4", 32), ("seg16", C), ("seg4", C), ("sa", 32), ("sb", 32), ("sp", 32),
+               ("rowq", C), ("rowqs", C), ("rowt", C), ("arow", C), ("brow", C), ("agrow", C), ("df", C), ("nu", C),
+               ("mg", C), ("s3", 1360), ("sc", C), ("sd", C), ("sn", C), ("sm", C), ("sc4", C), ("sg", C)):
     SCRATCH[_n] = ("sbuf", [128, _w], BF)
-for _n, _w in (("uc", 128), ("uq", 128), ("vq", 128), ("wq", 512), ("xc", C), ("vc", C), ("ebc", 512), ("shc", 352), ("zc", 256),
+for _n, _w in (("uc", 128), ("uq", 128), ("vq", 128), ("wq", 512), ("xc", C), ("vc", C), ("ebc", 512), ("shc", 224), ("zc", 128),
                ("hc0", C), ("hc1", C), ("hc2", C), ("lc0", C), ("lc1", C), ("lc2", C)):
     SCRATCH[_n] = ("sbuf", [128, _w], MX)
     SCRATCH[_n + "p"] = ("sbuf", [128, _w], U8)
-for _n, _w in (("qU", 28), ("mU", 28), ("loU", 28), ("ls0", 28), ("ls", 224), ("l4", 112), ("a8w", 28), ("n8w", 28), ("a8r", 28),
-               ("ulist", 8), ("qoU", 28), ("rep", 28), ("lf", 28)):
+for _n, _w in (("qU", 28), ("sU", 28), ("mU", 28), ("loU", 28), ("ls0", 28), ("ls", 256), ("l4", 112), ("q7", 64),
+               ("ulist", 8), ("qoU", 28), ("rep", 28)):
     SCRATCH[_n] = ("sbuf", [128, _w], U16)
-for _n, _w in (("iwb", 28), ("iw", 28), ("tabC", 28), ("tC", 28), ("wB", 28),
-               ("ds", 28), ("tO", 56), ("tbF", 252), ("tbB", 252), ("t4", 84),
-               ("hq", 56), ("tq", 56), ("lo", 28), ("dq", 84), ("cq", 40), ("ysb", C), ("qrow", C)):
+for _n, _w in (("iwb", 84), ("fac", 84), ("iw", 28), ("tabC", 28), ("tC", 28),
+               ("tO", 56), ("tbF", 252), ("tbB", 252), ("t4", 84),
+               ("hq", 28), ("tq", 28), ("lo", 28), ("dq", 84), ("cq", 40), ("ysb", C), ("qrow", C)):
     SCRATCH[_n] = ("sbuf", [128, _w], F32)
-for _n, _w in (("gqi", 28), ("gmi", 28), ("pi", 8), ("uli", 16)):
+for _n, _w in (("gqi", 28), ("gsi", 28), ("gmi", 28), ("pi", 8), ("uli", 16)):
     SCRATCH[_n] = ("sbuf", [128, _w], I32)
 for _k in range(8):
     SCRATCH["P%d" % _k] = ("psum", [128, 512], F32)
@@ -123,6 +125,9 @@ def rank_program(g, core, T, topo):
     def scan(reads, writes, out, seg, a):
         op("v", reads, writes, lambda: g.vector.tensor_tensor_scan(out, seg, a, 0.0, A.mult, A.add))
 
+    def times(reads, writes, out, table):
+        op("v", ["s3e", "s3m", "s3l", "s30", "s31"] + reads, writes, lambda: g.vector.tensor_tensor_scan(out, table, T.s3[:, 29:1358:16], 0.0, A.add, A.mult))
+
     def iota(key, out, pat, base, cm, flag=True):
         if flag:
             op("g", [], [key], lambda: g.iota(out, pat, base, cm, allow_small_or_imprecise_dtypes=True))
@@ -130,7 +135,7 @@ def rank_program(g, core, T, topo):
             op("g", [], [key], lambda: g.iota(out, pat, base, cm))
 
     def cols(key, a, b):
-        return ["%s:%d" % (key, k) for k in range(a // 32, (b + 31) // 32)]
+        return ["%s:%d" % (key, k) for k in range(a // 16, (b + 15) // 16)]
 
     def both(key):
         return [key + "v", key + "s"]
@@ -141,273 +146,258 @@ def rank_program(g, core, T, topo):
         if nv < 28:
             act(wkeys + lkeys, both(okey) if nv == 0 else [okey + "s"], out[:, o + 16 * nv:o + C], win.indirect(lst[:, l0 + nv:l0 + 28]))
 
-    place = {}
+    place = {"c16": 0, "c4": 1, "c1": 2, "cg": 3}
 
-    def col(name, a=0):
+    def col(name, a=0, b=128):
         k = place.setdefault(name, len(place))
-        return T.cq[a:128, k:k + 1]
+        return T.cq[a:b, k:k + 1]
 
     def icol(name):
         k = ("pi", "p16", "p4", "p1", "grp").index(name)
         return T.pi[:, k:k + 1]
 
     def const(name, src, s1, o1, s2=None, o2=None):
-        ts([src], [name], col(name), icol(src) if src in ("pi", "p16", "p4", "p1", "grp") else col(src), s1, o1, s2, o2)
+        ts([src], [name], col(name), col(src), s1, o1, s2, o2)
+
+    def aconst(name, src, f, scale, bias):
+        act([src], [name], col(name), col(src), f, scale=scale, bias=bias)
+
+    def lst(name, a=0, b=128, n=28):
+        return T.ls[a:b, LS[name]:LS[name] + n]
 
     dma("y", [(T.gqi[:], T.gq[:])], [], ["gqi"])
     dma("s", [(T.gmi[:], T.gm[:])], [], ["gmi"])
     dma("y", [(T.ut[:], T.u[:])], [], ["ut"])
-    for k, (a, b) in enumerate(PARTS):
+    dma("s", [(T.gsi[16:128, :], T.gq[0:112, :]), (T.gsi[0:16, :], T.gq[112:128, :])], [], ["gsi"])
+    for k, (a, b) in enumerate(PARTS["xc"]):
         dma("sys"[k], [(T.x0[:, 4 * a:4 * b], T.x[:, 4 * a:4 * b])], [], cols("x0", a, b))
-    need("y", W[cols("x0", C - 1, C)[0]])
-    dma("y", [(T.wq[:].bitcast(dt.uint8), T.wc[:])], [], ["wqc"])
-    dma("y", [(T.wqp[:], T.ws[:])], [], ["wqp"])
-    dma("y", [(T.vv[:], T.v[:])], [], ["vv"])
+
+    def late_loads():
+        dma("y", [(T.wq[:].bitcast(dt.uint8), T.wc[:])], [], ["wqc"])
+        dma("y", [(T.wqp[:], T.ws[:])], [], ["wqp"])
+        dma("y", [(T.vv[:], T.v[:])], [], ["vv"])
 
     def score(src, key, c, k):
-        a, b = PARTS[k]
+        a, b = PARTS[c][k]
         quant(cols(key, a, b), [c + str(k)], c, a, b, src, 4 * a)
         mm(["uqc", "uqs", c + str(k)], ["P%d" % k], T["P%d" % k][:, 0:b - a], "uq", 0, c, a, b - a)
 
-    def sign(k, f=act):
-        a, b = PARTS[k]
-        f(["P%d" % k], ["sg%d" % k], T.sg[:, a:b], T["P%d" % k][:, 0:b - a])
+    def sign(c, k, q="s"):
+        a, b = PARTS[c][k]
+        if q == "s":
+            act(["P%d" % k], cols("sg", a, b), T.sg[:, a:b], T["P%d" % k][:, 0:b - a], F.Sign, bias=-(2.0 ** -93))
+        else:
+            cp(["P%d" % k], cols("sg", a, b), T.sg[:, a:b], T["P%d" % k][:, 0:b - a])
 
-    def early_signs():
-        ts(["sg0", "loU"], ["mge"], T.mg[:, 0:16 * EARLY], T.sg[:, 0:16 * EARLY].indirect(T.loU[:, 0:EARLY]), 0.0, A.is_gt, -0.5, A.add)
+    def early_signs(d, q="v"):
+        e = EARLY[d]
+        keys, out, src = cols("sg", 0, 16 * e) + ["loU"], T.mg[:, 0:16 * e], T.sg[:, 0:16 * e].indirect(T.loU[:, 0:e])
+        if q == "s":
+            act(keys, ["mge", "mgv"], out, src, F.Copy, scale=0.5)
+        else:
+            ts(keys, ["mge", "mgv"], out, src, 0.0, A.is_gt, -0.5, A.add)
 
-    def early_scan():
-        scan(["seg16", "mge"], ["s3e"], T.s3[:, 0:48 * EARLY:3], T.seg16[:, 0:16 * EARLY], T.mg[:, 0:16 * EARLY])
+    def early_scan(d):
+        e = EARLY[d]
+        scan(["seg16", "mge"], ["s3e", "s3m"], T.s3[:, 0:48 * e:3], T.seg16[:, 0:16 * e], T.mg[:, 0:16 * e])
 
     def halve(src, key, a, b):
-        act(cols(key, a, b), cols("xh", a, b), T.xh[:, 4 * a:4 * b], src[:, 4 * a:4 * b], F.Copy, scale=0.5)
+        return lambda: act(cols(key, a, b), cols("xh", a, b), T.xh[:, 4 * a:4 * b], src[:, 4 * a:4 * b], F.Copy, scale=0.5)
 
     def copy_half():
         dma("y", [(T.xg[:, 0:4 * CUT], T.xh[:, 0:4 * CUT])], cols("xh", 0, CUT), cols("xg", 0, CUT))
 
     def scatter(a, b):
-        return lambda: cp(["iot", "qU"], ["rowqi"], T.rowqi[:, 0:C].indirect(T.qU[:, a:b]), T.iot[:, 16 * a:16 * b])
+        return lambda: cp(["iot", "sU"], ["inv"], T.rowqs[:, 0:C].indirect(T.sU[:, a:b]), T.iot[:, 16 * a:16 * b])
 
     def ebq(b):
         return lambda: quant(["ebi"], ["ebc%d" % b], "ebc", 128 * b, 128 * b + 128, T.eb, 4 - b)
 
-    def halves(reads, key, out, a, s1, o1, s2, o2):
-        ts(reads, [key + "a"], out(0, NV), a(0, NV), s1[0], o1, s2[0], o2)
-        ts(reads, [key + "b"], out(NV, 28), a(NV, 28), s1[1], o1, s2[1], o2)
-
-    def tab(d, k, e, a=0, b=28):
-        return T["tb" + d][:, 84 * k + 3 * a + e:84 * k + 3 * b:3]
+    def tab(d, k, e, a=0, b=28, p=128):
+        return T["tb" + d][0:p, 84 * k + 3 * a + e:84 * k + 3 * b:3]
 
     def tables(d):
-        w, hi, lw = tab(d, 2, 2) if d == "F" else T.wB[:], tab(d, 0, 2), tab(d, 1, 2)
-        dh, dk = ((lambda a, b: tab(d, 2, 1, a, b)), "dhF") if d == "F" else ((lambda a, b: T.ds[:, a:b]), "ds")
-        return [
-            lambda: scan(["seg16"] + both("rowt"), ["sn"], T.sn[:], T.seg16[:], T.rowt[:]),
-            lambda: (ts(["sn", "kaph"], ["tq"], T.tq[:, 0:28], T.sn[:, 15:C:16], col("kaph"), A.mult),
-                     halves(["sn", "kaph", "kap"], "tk", lambda a, b: T.tq[:, 28 + a:28 + b], lambda a, b: T.sn[:, 16 * a + 15:16 * b:16],
-                            (col("kap"), col("kaph")), A.mult, (col("kap"), col("kap")), A.mult)),
-            lambda: (tt(["tq", "hq"], ["wq" + d], w, T.tq[:, 0:28], T.hq[:, 0:28], A.add),
-                     tt(["tka", "tkb", "hka", "hkb"], [dk], dh(0, 28), T.tq[:, 28:56], T.hq[:, 28:56], A.subtract)),
-            lambda: (ts(["wq" + d], ["hi" + d], hi, w, M, A.add, -M, A.add),
-                     halves([dk, "km", "km2"], "dhi" + d, lambda a, b: tab(d, 0, 1, a, b), dh, (col("km2"), col("km")), A.add, (col("km2"), col("km")), A.subtract)),
-            lambda: (tt(["hi" + d, "wq" + d], ["lw" + d], lw, w, hi, A.subtract),
-                     tt(["dhi%sa" % d, "dhi%sb" % d, dk], ["dlo" + d, "dhi" + d], tab(d, 1, 1), dh(0, 28), tab(d, 0, 1), A.subtract)),
-        ]
+        t, k0, k1, k2 = T["tb" + d], d + "0", d + "1", d + "2"
+        return {
+            "wrap": lambda: scan(["seg16"] + both("rowt"), ["sn"], T.sn[:], T.seg16[:], T.rowt[:]),
+            "half": lambda: ts(["sn", "kaph"], ["tq"], T.tq[:], T.sn[:, 15:C:16], col("kaph"), A.mult),
+            "mean": lambda: (tt(["tq", "hq"], [d + "q"], tab(d, 2, 2), T.tq[:], T.hq[:], A.add),
+                             tt(["tq", "hq"], [d + "d"], tab(d, 2, 1), T.tq[:], T.hq[:], A.subtract)),
+            "high": lambda: ts([d + "z", d + "q", d + "d"], [k0], t[:, 0:84], t[:, 168:252], M, A.add, -M, A.add),
+            "low": lambda: tt([d + "z", d + "q", d + "d", k0], [k1], t[:, 84:168], t[:, 168:252], t[:, 0:84], A.subtract),
+            "scale": lambda: tt(["fac", d + "z"], [k0, k1, k2, d + "q", d + "d"], t[:, 1:252:3], t[:, 1:252:3], T.fac[:], A.mult),
+        }
 
     def back_tables():
-        tb = tables("B")
-        return [
-            lambda: dma("y", [(T.rowqs[16:128, :], T.rowqi[0:112, :]), (T.rowqs[0:16, :], T.rowqi[112:128, :])], ["rowqi"], ["rowqs"]),
-            lambda: gather(T.rowt, 0, "rowt", T.rowqs[:, 0:C], ["rowqs"], T.mU, 0, ["mU"], 0),
-            lambda: scan(["seg16", "rowqs"], ["sn"], T.sn[:], T.seg16[:], T.rowqs[:]),
-            lambda: (ts(["sn", "kaph"], ["hq"], T.hq[:, 0:28], T.sn[:, 15:C:16], col("kaph"), A.mult),
-                     halves(["sn", "kaph", "kap"], "hk", lambda a, b: T.hq[:, 28 + a:28 + b], lambda a, b: T.sn[:, 16 * a + 15:16 * b:16],
-                            (col("kap"), col("kaph")), A.mult, (col("kap"), col("kap")), A.mult)),
-        ] + tb + [
-            lambda: (tt(["gmi", "iw"], ["tO0"], T.tO[:, 0:28], T.gmi[:], T.iw[:], A.add),
-                     tt(["gmi", "iw"], ["tO1"], T.tO[:, 28:56], T.gmi[:], T.iw[:], A.subtract)),
-            lambda: (ts(["tO0"], ["wO"], tab("B", 2, 2), T.tO[:, 0:28], 0.5, A.mult, -224.0, A.add),
-                     ts(["tO1", "kap"], ["dhB0"], tab("B", 2, 1, 0, NV), T.tO[:, 28:28 + NV], col("kap"), A.mult),
-                     ts(["tO1", "kaph"], ["dhB"], tab("B", 2, 1, NV, 28), T.tO[:, 28 + NV:56], col("kaph"), A.mult)),
-        ]
+        def inverse():
+            ts(["sd", "kaph"], ["hq"], T.hq[:], T.sd[:, 15:C:16], col("kaph"), A.mult)
+            for k in range(2):
+                ts(["sd", "kap"], ["q7%d" % k], T.q7[0:32, 32 * k:32 * k + 28], T.sd[0:32, 15:C:16], col("kap", 0, 32), A.mult, 224.25 + C * k, A.add)
+            dma("y", [(lst("twoB", 96, 112), T.q7[0:16, 32:60]), (lst("twoB", 112, 128), T.q7[0:16, 0:28])], ["q70", "q71", "lz"], ["q7"])
+        return dict(
+            tables("B"),
+            row=lambda: gather(T.rowt, 0, "rowt", T.rowqs[:, 0:C], ["inv"], T.mU, 0, ["mU"], 0),
+            wrapinv=lambda: scan(["seg16", "inv"], ["sd"], T.sd[:], T.seg16[:], T.rowqs[:]),
+            inverse=inverse,
+            places=lambda: (ts(["gmi"], ["tO0"], T.tO[:, 0:28], T.gmi[:], 0.5, A.mult, -112.0, A.add),
+                            ts(["iw"], ["tO1"], T.tO[:, 28:56], T.iw[:], 0.5, A.mult, -112.0, A.add)),
+            own=lambda: (tt(["tO0", "tO1"], ["Bq"], tab("B", 2, 2, p=64), T.tO[0:64, 0:28], T.tO[0:64, 28:56], A.add),
+                         tt(["tO0", "tO1"], ["Bd"], tab("B", 2, 1, p=64), T.tO[0:64, 0:28], T.tO[0:64, 28:56], A.subtract)))
 
+    def late_constants():
+        act(["iw", "short", "from"], ["tabC"], T.tabC[:], T.iw[:], F.Identity, scale=col("short"), bias=col("from"))
+        aconst("r2", "c4", F.Relu, 1.0, -2.0)
+        aconst("kap2", "kap", F.Identity, -2.0, 0.0)
+        aconst("r14", "c16", F.Relu, 1.0, -14.0)
+        aconst("c896", "c1", F.Identity, 1.0, 896.25)
+        aconst("k4", "r2", F.Identity, 4.0, 4 / K)
+        aconst("kq", "r14", F.Identity, 1 / K - 1, 1.0)
+
+    tf, bt = tables("F"), back_tables()
     iota("pi", icol("pi"), [[0, 1]], 0, 1, False)
-    iota("j16", T.j16[:], [[1, 16]], 0, 0)
-    iota("j4", T.j4[:], [[0, 4], [1, 4]], 0, 0)
+    iota("j16", T.j16[:], [[1, 17]], -1, 0)
     iota("iot", T.iot[:, 0:C], [[1, C]], -224, 0)
-    iota("iwb", T.iwb[:], [[16, 28]], 0, 0)
     iota("uli", T.uli[:, 1:8], [[16, 7]], 0, 0, False)
     iota("uli0", T.uli[:, 0:1], [[0, 1]], 112, 0, False)
+    iota("iwb", T.iwb[:], [[0, 3], [16, 28]], 0, 0)
+    iota("j4", T.j4[:], [[1, 2], [0, 4], [1, 4]], -1, 0)
     fill(["z"], T.zt[:], 0.0)
-    op("g", ["z"], ["wi"], lambda: g.affine_select(T.wt[:, C:960], T.zt[:, 0:512], [[1, 128], [0, 4]], A.not_equal, 1.0, 0, -1))
+    op("g", ["z"], ["wi"], lambda: g.affine_select(T.wt[:, 192:704], T.zt[:, 0:512], [[1, 128], [0, 4]], A.not_equal, 1.0, 0, -1))
     op("g", ["z"], ["ebi"], lambda: g.affine_select(T.eb[:], T.zt[:], [[1, 520]], A.not_equal, 1.0, -4, -4))
     ts(["pi"], ["p16"], icol("p16"), icol("pi"), 15, A.bitwise_and)
     ts(["pi"], ["p4"], icol("p4"), icol("pi"), 2, A.arith_shift_right, 3, A.bitwise_and)
     ts(["pi"], ["p1"], icol("p1"), icol("pi"), 3, A.bitwise_and)
     ts(["pi"], ["grp"], icol("grp"), icol("pi"), 4, A.arith_shift_right)
-    const("c16", "p16", 0.0, A.add)
-    const("c16n", "p16", 1.0, A.add)
-    const("kap", "p16", 15.0, A.is_equal, 1 / K, A.max)
-    const("c4", "p4", 0.0, A.add)
-    const("c4n", "p4", 1.0, A.add)
-    ts(["j16", "c16"], ["sa"], T.sa[:, 0:16], T.j16[:], col("c16"), A.not_equal)
-    ts(["j16", "c16n"], ["sb"], T.sb[:, 0:16], T.j16[:], col("c16n"), A.is_equal, K, A.mult)
-    ts(["z", "c16"], ["rep"], T.rep[:], T.zt[:, 0:28], col("c16"), A.add)
-    const("c896", "p1", 896.25, A.add)
-    const("cg", "grp", 0.0, A.add)
-    const("kaph", "kap", 0.5, A.mult)
-    tt(["sa", "sb"], ["sp"], T.sp[:, 0:16], T.sa[:, 0:16], T.sb[:, 0:16], A.max)
-    act(["z"], ["wt0"], T.wt[:, 0:C], T.zt[:, 0:C])
-    act(["z"], ["wt2"], T.wt[:, 960:1408], T.zt[:, 0:C])
-    for d in "FB":
-        act(["z"], ["t0" + d], T["tb" + d][:, 0:252:3], T.zt[:, 0:84])
-    act(["sp", "rep"], ["seg16"], T.seg16[:], T.sp[:, 0:16].indirect(T.rep[:, 0:28]))
-    quant(["z"], ["zcr", "zc"], "zc", 0, 128, T.zt, 0)
-    quant(["z"], ["zcs"], "zc", 128, 256, T.zt, 0)
     fill(["s30"], T.s3[:, 29:1360:48], 0.0)
     fill(["s31"], T.s3[:, 13:1360:48], 1.0)
-    ts(["j4", "c4"], ["sa4"], T.sa[:, 16:32], T.j4[:], col("c4"), A.not_equal)
-    ts(["j4", "c4n"], ["sb4"], T.sb[:, 16:32], T.j4[:], col("c4n"), A.is_equal, K, A.mult)
-    ts(["iwb", "c16"], ["iw"], T.iw[:], T.iwb[:], col("c16"), A.add)
+    cp(["p16", "p4", "p1", "grp"], ["c16", "c4", "c1", "cg"], T.cq[:, 0:4], T.pi[:, 1:5])
+    fill(["lz"], T.ls[:], 0)
+    ts(["j16", "c16"], ["sa"], T.sa[:, 0:16], T.j16[:, 1:17], col("c16"), A.not_equal)
+    ts(["j16", "c16"], ["sb"], T.sb[:, 0:16], T.j16[:, 0:16], col("c16"), A.is_equal, K, A.mult)
+    ts(["z", "c16"], ["rep"], T.rep[:], T.zt[:, 0:28], col("c16"), A.add)
+    const("kap", "c16", 15.0, A.is_equal, 1 / K, A.max)
+    const("short", "cg", 3.0, A.is_lt)
+    const("g448", "cg", float(C), A.mult, 0.25, A.add)
+    tt(["sa", "sb"], ["sp"], T.sp[:, 0:16], T.sa[:, 0:16], T.sb[:, 0:16], A.max)
+    act(["z"], ["wt0"], T.wt[:, 0:192], T.zt[:, 0:192])
+    act(["z"], ["wt2"], T.wt[:, 704:896], T.zt[:, 0:192])
+    for d in "FB":
+        act(["z"], [d + "z"], T["tb" + d][:, 168:252:3], T.zt[:, 0:28])
+    act(["sp", "rep"], ["seg16"], T.seg16[:], T.sp[:, 0:16].indirect(T.rep[:, 0:28]))
     cp(["gqi"], ["qU"], T.qU[:], T.gqi[:])
+    const("kaph", "kap", 0.5, A.mult)
+    const("from", "g448", 224.25 + 2 * C, A.min)
     cp(["gmi"], ["mU"], T.mU[:], T.gmi[:])
-    tt(["sa4", "sb4"], ["sp4"], T.sp[:, 16:32], T.sa[:, 16:32], T.sb[:, 16:32], A.max)
-    ts(["gqi"], ["hq"], T.hq[:, 0:28], T.gqi[:], 0.5, A.mult, -112.0, A.add)
-    halves(["gqi", "kaph", "kap"], "hk", lambda a, b: T.hq[:, 28 + a:28 + b], lambda a, b: T.gqi[:, a:b], (-224.0, -224.0), A.add, (col("kap"), col("kaph")), A.mult)
-    gather(T.rowq, 0, "rowq", T.iot[:, 0:C], ["iot"], T.qU, 0, ["qU"], 14)
-    tt(["gmi", "iw"], ["lo"], T.lo[:], T.gmi[:], T.iw[:], A.min)
-    cp(["uli", "uli0"], ["ulist"], T.ulist[:], T.uli[:, 0:8])
-    gather(T.rowt, 0, "rowt", T.rowq[:, 0:C], both("rowq"), T.mU, 0, ["mU"], 14)
+    ts(["gqi"], ["hq"], T.hq[:], T.gqi[:], 0.5, A.mult, -112.0, A.add)
+    gather(T.rowq, 0, "rowq", T.iot[:, 0:C], ["iot"], T.qU, 0, ["qU"], 28)
     quant(["ut"], ["uc"], "uc", 0, 128, T.ut, 0)
-    cp(["lo"], ["loU"], T.loU[:], T.lo[:])
-    tf = tables("F")
-    tf[0]()
+    cp(["uli", "uli0"], ["ulist"], T.ulist[:], T.uli[:, 0:8])
+    ts(["iwb", "c16"], ["iw"], T.iw[:], T.iwb[:, 0:28], col("c16"), A.add)
+    ts(["iwb"], ["fac"], T.fac[:], T.iwb[:], 16.0 * NV, A.is_lt, 1.0, A.add)
+    gather(T.rowt, 0, "rowt", T.rowq[:, 0:C], both("rowq"), T.mU, 0, ["mU"], 14)
     act(["uc", "ulist"], ["uqs"], T.uqp[:, 0:128], T.ucp[:, 0:128].indirect(T.ulist[:, 0:8]))
     cp(["uc", "ulist"], ["uqc"], T.uq[:, 0:128].bitcast(dt.uint32), T.uc[:, 0:128].bitcast(dt.uint32).indirect(T.ulist[:, 0:8]))
+    tt(["gmi", "iw"], ["lo"], T.lo[:], T.gmi[:], T.iw[:], A.min)
+    tf["wrap"]()
     score(T.x0, "x0", "xc", 0)
-    tf[1]()
-
-    def aconst(name, src, f, scale, bias, more=()):
-        act([src] + list(more), [name], col(name), col(src), f, scale=scale, bias=bias)
-    aconst("km", "kap", F.Identity, M, 0.0)
-    aconst("km2", "kap", F.Identity, 2 * M, 0.0)
-    aconst("r4", "cg", F.Relu, 448.0, 0.25 - 4 * C)
-    aconst("r6", "cg", F.Relu, 1.0, -6.0)
-    aconst("rF", "cg", F.Relu, -448.0, 4.0 * C)
-    aconst("r2", "c4", F.Relu, 1.0, -2.0)
-    aconst("cg7", "r6", F.Identity, -1.0, 1.0)
-    aconst("cgk", "r6", F.Identity, -224.0, col("r4"), ["r4"])
-    aconst("cfF", "rF", F.Identity, -1.0, 224.25 + 4 * C)
-    aconst("k4", "r2", F.Identity, 4.0, 4 / K)
-    act(["iw", "cg7", "cgk"], ["tabC"], T.tabC[:], T.iw[:], F.Identity, scale=col("cg7"), bias=col("cgk"))
-
-    def back_constants():
-        aconst("rB", "cg", F.Relu, 448.0, -3.0 * C)
-        aconst("c8", "cg", F.Relu, -448.0, 3.0 * C)
-        aconst("kap2", "kap", F.Identity, -2.0, 0.0)
-        aconst("r14", "c16", F.Relu, 1.0, -14.0)
-        aconst("cfB", "rB", F.Identity, -1.0, 224.25 + 4 * C)
-        aconst("kq", "r14", F.Identity, 1 / K - 1, 1.0)
+    cp(["lo"], ["loU"], T.loU[:], T.lo[:])
+    ts(["kap"], ["fac"], T.fac[:], T.fac[:], col("kap"), A.mult)
+    cp(["gsi"], ["sU"], T.sU[:], T.gsi[:])
+    tf["half"]()
     score(T.x0, "x0", "xc", 1)
-    tf[2]()
     score(T.x0, "x0", "xc", 2)
-    sign(0)
-    sign(1)
-    tf[3]()
-    quant(["wt0", "wt2", "wi"], ["shc"], "shc", 0, 352, T.wt, 0)
-    early_signs()
-    sign(2)
-    tf[4]()
+    tf["mean"]()
     scatter(0, 4)()
-    early_scan()
-
-    SC = ["sc"]
+    halve(T.x0, "x0", 0, CUT)()
+    copy_half()
+    late_loads()
+    sign("xc", 0)
+    sign("xc", 1)
+    tf["high"]()
+    ts(["j4", "c4"], ["sa4"], T.sa[:, 16:32], T.j4[:, 16:32], col("c4"), A.not_equal)
+    ts(["j4", "c4"], ["sb4"], T.sb[:, 16:32], T.j4[:, 0:16], col("c4"), A.is_equal, K, A.mult)
+    scatter(4, 8)()
+    early_signs("F", "s")
+    tf["low"]()
+    sign("xc", 2, "v")
+    early_scan("F")
+    tt(["sa4", "sb4"], ["sp4"], T.sp[:, 16:32], T.sa[:, 16:32], T.sb[:, 16:32], A.max)
+    tf["scale"]()
 
     def chain(d, way, shares, vgap, sgap):
         def gap(name):
             for f in vgap.get(name, []) + sgap.get(name, []):
                 f()
-        wk = "wqF" if d == "F" else "wO"
-        ts(["sg0", "sg1", "loU"], ["mgv"], T.mg[:, 16 * EARLY:16 * NV], T.sg[:, 0:16 * NV].indirect(T.loU[:, EARLY:NV]), 0.0, A.is_gt, -0.5, A.add)
-        act(["sg0", "sg1", "sg2", "loU"], ["mgs"], T.mg[:, 16 * NV:C], T.sg[:, 0:C].indirect(T.loU[:, NV:28]), F.Sign, bias=-(2.0 ** -93))
+        early = EARLY[d]
+        ts(cols("sg", 0, 16 * NV) + ["loU"], ["mgv"], T.mg[:, 16 * early:16 * NV], T.sg[:, 0:16 * NV].indirect(T.loU[:, early:NV]), 0.0, A.is_gt, -0.5, A.add)
+        act(cols("sg", 0, C) + ["loU"], ["mgs"], T.mg[:, 16 * NV:C], T.sg[:, 0:C].indirect(T.loU[:, NV:28]), F.Sign, bias=-(2.0 ** -93))
         gap("signs")
-        scan(["seg16", "mgv"], ["s3m"], T.s3[:, 48 * EARLY:48 * NV:3], T.seg16[:, 16 * EARLY:16 * NV], T.mg[:, 16 * EARLY:16 * NV])
+        scan(["seg16", "mgv"], ["s3m"], T.s3[:, 48 * early:48 * NV:3], T.seg16[:, 16 * early:16 * NV], T.mg[:, 16 * early:16 * NV])
+        gap("mid")
         scan(["seg16", "mgs"], ["s3l"], T.s3[:, 48 * NV:3 * C:3], T.seg16[:, 16 * NV:C], T.mg[:, 16 * NV:C])
         gap("scan")
-        made = ((0, ["dhi" + d, "hi" + d], ["z0", "z"], T.zt[:, 0:336:4]), (1, ["dlo" + d, "lw" + d], ["z1"], T.zt[:, 1:336:4]),
-                (2, ["dh" + d, wk] + ["dhB0"] * (d == "B"), ["t4"], T.t4[:]))
-        for k, keys, okeys, out in made:
-            op("v", ["s3e", "s3m", "s3l", "s30", "s31", "t0" + d] + keys, okeys,
-               lambda: g.vector.tensor_tensor_scan(out, T["tb" + d][:, 84 * k:84 * k + 84], T.s3[:, 29:1358:16], 0.0, A.add, A.mult))
+        for k, okeys, out in ((0, ["z0", "z"], T.zt[:, 0:336:4]), (1, ["z1"], T.zt[:, 1:336:4]), (2, ["t4"], T.t4[:])):
+            times([d + str(k)], okeys, out, T["tb" + d][:, 84 * k:84 * k + 84])
         gap("times")
-        quant(["z0", "z1"], ["zc"], "zc", 84, 212, T.zt, 0)
+        quant(["z0", "z1"], ["zc"], "zc", 0, 128, T.zt, 0)
         ts(["t4"], ["ls0"], T.ls0[:], T.t4[:, 2:84:3], 224.25, A.add)
-        for bank, ns in (("P0", (5,)), ("P3", (1,)), ("P1", (6, 2)), ("P2", (3, 4)), ("P4", (7,))):
-            need("t", deps(["zc", "zcr", "zcs", "shc"], [bank]))
-            for k, n in enumerate(ns):
-                s0, z0, e = 112 + way * 16 * n, 84 - 84 * k, max(128, 84 * len(ns))
-                i = g.tensor.matmul_mx(T[bank][:, 0:e], T.shc[:, s0:s0 + 128], T.shcp[:, s0:s0 + 128], T.zc[:, z0:z0 + e], T.zcp[:, z0:z0 + e], n == ns[0], n == ns[-1])
-            count["t"] = count.get("t", 0) + 1
-            i.then_inc(T.sem["t"], 1)
-            done(("t", count["t"], dict(known["t"])), ["zc", "zcr", "zcs", "shc"], [bank])
+        for n in (1, 2, 3):
+            bank = "P%d" % (3 + n)
+            mm(["zc", "shc"], [bank], T[bank][:, 0:128], "shc", 48 + way * 16 * n, "zc", 0, 128)
         gap("list")
-        ls = T.ls
 
-        def left(n, l0, lk):
-            gather(T.R, n * C, "L%d" % n, T.R[:, (n - 1) * C:n * C], both("L%d" % (n - 1)), ls, l0, [lk], shares.get("L%d" % n, 14))
+        def window(a, b):
+            return T.R[:, (a + 1) * C:(b + 1) * C], [k for i in range(a, b) for k in (both("L%d" % i) if i >= 0 else ["qs"])]
 
-        def right(n, l0, lk, a):
-            gather(T.iot, (n + 1) * C, "Q%d" % n, T.iot[:, a * C:(n + 1) * C], ["iot"] + [k for i in range(max(a - 1, 0), n) for k in both("Q%d" % i)], ls, l0, [lk], shares.get("Q%d" % n, 14))
+        def step(n, a, name, keys):
+            win, wkeys = window(a, n)
+            gather(T.R, (n + 1) * C, "L%d" % n, win, wkeys, T.ls, LS[name], keys + ["lz"], shares.get("L%d" % n, 14))
 
-        def last_list():
-            ts(SC + ["kap", "cf" + d], ["lf"], T.lf[:], T.sc[:, 15:C:16], col("kap"), A.mult, col("cf" + d), A.add)
+        def wrap(key, n, p, w=32):
+            scan(["seg16"] + both("L%d" % n), [key], T[key][p:p + w, :], T.seg16[p:p + w, :], T.R[p:p + w, (n + 1) * C:(n + 2) * C])
 
-        gather(T.R, 0, "L0", T.iot[:, 0:C], ["iot"], T.ls0, 0, ["ls0"], shares.get("L0", 8))
-        ts(["P0"], ["lsA"], ls[:, 0:28], T.P0[:, 2:84:3], 224.25, A.add)
-        ts(["P3"], ["ls1"], ls[:, 28:56], T.P3[:, 2:84:3], 224.25, A.add)
-        gap("L0")
-        right(0, 0, "lsA", 0)
-        ts(["P1"], ["lsG"], ls[:, 56:112], T.P1[:, 2:168:3], 224.25, A.add)
-        gap("Q0")
-        left(1, 28, "ls1")
-        ts(["P2"], ["lsH"], ls[:, 112:168], T.P2[:, 2:168:3], 224.25, A.add)
+        def hand(key, p, name, to, w=32):
+            for q, row in to:
+                ts([key, "kap", "lz"], ["%s%d" % (name, q)], lst(name, q, q + w), T[key][p:p + w, 15:C:16], col("kap", p, p + w), A.mult, 224.25 + row * C, A.add)
+            return ["%s%d" % (name, q) for q, row in to]
+
+        gather(T.R, C, "L0", T.iot[:, 0:C], ["iot"], T.ls0, 0, ["ls0"], shares.get("L0", 14))
+        gap("own")
+        ts(["P4", "lz"], ["one"], lst("one"), T.P4[:, 2:84:3], 224.25, A.add)
         if d == "F":
-            tt(["P4", "tabC"], ["tC"], T.tC[:], T.P4[:, 2:84:3], T.tabC[:], A.add)
+            ts(["P5", "lz"], ["twoF"], lst("twoF"), T.P5[:, 2:84:3], 224.25, A.add)
+            tt(["P6", "tabC"], ["tC"], T.tC[:], T.P6[:, 2:84:3], T.tabC[:], A.add)
+            gap("L0")
+            step(1, 0, "one", ["one"])
+            cp(["tC", "lz"], ["threeF"], lst("threeF"), T.tC[:])
             gap("L1")
-            right(1, 56, "lsG", 1)
-            cp(["tC"], ["lsC"], ls[:, 168:196], T.tC[:])
-            gap("Q1")
-            left(2, 84, "lsG")
+            step(2, 1, "twoF", ["twoF"])
             gap("L2")
-            right(2, 168, "lsC", 0)
-            gap("Q2")
-            left(3, 112, "lsH")
-            scan(["seg16"] + both("Q2"), SC, T.sc[:], T.seg16[:], T.iot[:, 3 * C:4 * C])
+            step(3, 0, "threeF", ["threeF"])
             gap("L3")
-            left(4, 140, "lsH")
-            last_list()
-            gap("L4")
-        else:
-            ts(["P4"], ["lsC"], ls[:, 168:196], T.P4[:, 2:84:3], 224.25, A.add)
-            gap("L1")
-            right(1, 56, "lsG", 1)
-            gap("Q1")
-            left(2, 84, "lsG")
-            gap("L2")
-            right(2, 168, "lsC", 2)
-            gap("Q2")
-            left(3, 112, "lsH")
-            gap("L3")
-            right(3, 196, "a8", 0)
-            gap("Q3")
-            left(4, 140, "lsH")
-            gap("L4")
-            scan(["seg16"] + both("Q3"), SC, T.sc[:], T.seg16[:], T.iot[:, 4 * C:5 * C])
+            wrap("sc", 3, 0, 64)
             gap("wrap")
-            last_list()
-            gap("fin")
+            name, keys, rows = "joinF", hand("sc", 0, "joinF", ((64, 0),), 64) + ["joinF0"], (3, 4)
+        else:
+            ts(["P5", "lz"], ["twoB"], lst("twoB", 0, 64), T.P5[0:64, 2:84:3], 224.25 + C, A.add)
+            ts(["P6", "lz"], ["threeB"], lst("threeB", 0, 64), T.P6[0:64, 2:84:3], 224.25 + C, A.add)
+            gap("L0")
+            step(1, 0, "one", ["one"])
+            gap("L1")
+            step(2, 0, "twoB", ["twoB", "q7"])
+            wrap("sc", 1, 64)
+            gap("L2")
+            step(3, 1, "threeB", ["threeB", "a8", "a8d"])
+            keys = hand("sc", 64, "pair", ((0, 4), (64, 0)))
+            gap("L3")
+            wrap("sd", 3, 96)
+            step(4, -1, "pair", keys)
+            gap("wrap")
+            name, keys, rows = "end", hand("sd", 96, "end", ((0, 5), (32, 4), (64, 5), (96, 0))), (-1, 5)
+        gap("fin")
         row = "arow" if d == "F" else "brow"
-        gather(T[row], 0, row, T.R[:, 0:5 * C], [k for i in range(5) for k in both("L%d" % i)], T.lf, 0, ["lf"], shares.get("last", HEAD // 16))
+        win, wkeys = window(*rows)
+        gather(T[row], 0, row, win, wkeys, T.ls, LS[name], keys, shares.get("last", HEAD // 16))
         gap("last")
         scan(["seg4", row + "v"], ["sc4a"], T.sc4[:, 0:HEAD], T.seg4[:, 0:HEAD], T[row][:, 0:HEAD])
         scan(["seg4"] + both(row), ["sc4b"], T.sc4[:, HEAD:C], T.seg4[:, HEAD:C], T[row][:, HEAD:C])
@@ -420,34 +410,32 @@ def rank_program(g, core, T, topo):
         tt(wkeys + ["l4a"] + ["l4b"] * (b > HEAD) + cols(bkey, a, b), cols(okey, a, b), out[:, 4 * a:4 * b], win[:, 0:4 * C].indirect(T.l4[:, a // 4:b // 4]), base[:, 4 * a:4 * b], A.add)
 
     def fetch(win, wkeys, a, b):
-        act(wkeys + ["l4b"], cols("tg", a, b), T.tg[:, 4 * a:4 * b], win[:, 0:4 * C].indirect(T.l4[:, a // 4:b // 4]))
+        act(wkeys + ["l4a"] * (a < HEAD) + ["l4b"], cols("tg", a, b), T.tg[:, 4 * a:4 * b], win[:, 0:4 * C].indirect(T.l4[:, a // 4:b // 4]))
 
     def add(out, okey, base, bkey, a, b):
         tt(cols("tg", a, b) + cols(bkey, a, b), cols(okey, a, b), out[:, 4 * a:4 * b], T.tg[:, 4 * a:4 * b], base[:, 4 * a:4 * b], A.add)
 
-    def turn_row():
-        act(["df0", "df1", "loU", "kap", "kap2"], ["nu"], T.nu[:], T.df[:, 0:C].indirect(T.loU[:, 0:28]), F.Identity, bias=col("kap"), scale=col("kap2"))
+    def turn_row(k):
+        act(["df0", "df1"][0:k + 1] + ["loU", "kap", "kap2"], ["nu%d" % k], T.nu[:, 224 * k:224 * k + 224], T.df[:, 0:224 * k + 224].indirect(T.loU[:, 14 * k:14 * k + 14]),
+            F.Identity, bias=col("kap"), scale=col("kap2"))
 
     def turn_scan():
-        scan(["seg16", "nu"], ["sn"], T.sn[:], T.seg16[:], T.nu[:])
+        scan(["seg16", "nu0", "nu1"], ["sn"], T.sn[:], T.seg16[:], T.nu[:])
 
     def turn(d):
-        for k, name in enumerate(("dhi", "dlo", "dh")):
+        for k in (0, 1, 2):
             v = tab(d, k, 1)
-            tt(["sn"], [name + d], v, v, T.sn[:, 15:C:16], A.mult)
+            tt(["sn"], [d + str(k)], v, v, T.sn[:, 15:C:16], A.mult)
 
     def differ(k):
         tt(both("brow") + ["agrow", "ag0"], ["df%d" % k], T.df[:, 224 * k:224 * k + 224], T.brow[:, 224 * k:224 * k + 224], T.agrow[:, 224 * k:224 * k + 224], A.not_equal)
 
     def wrap_a8():
-        scan(["seg16"] + both("arow"), ["sm"], T.sm[:], T.seg16[:], T.arow[:])
+        scan(["seg16"] + both("arow"), ["sm"], T.sm[96:128, :], T.seg16[96:128, :], T.arow[96:128, :])
 
     def list_a8():
-        ts(["sm", "kap"], ["a8w"], T.a8w[:], T.sm[:, 15:C:16], col("kap"), A.mult, 224.25, A.add)
-
-    def spread_n8():
-        ts(["sm", "kap"], ["n8w"], T.n8w[:], T.sm[:, 15:C:16], col("kap"), A.mult, 224.25, A.add)
-        dma("y", [(T.a8r[16 * k:16 * k + 16, :], T.n8w[112:128, :]) for k in range(8)], ["n8w"], ["a8r"])
+        ts(["sm", "kap", "lz"], ["a8", "a8d"], lst("threeB", 96, 128), T.sm[96:128, 15:C:16], col("kap", 96, 128), A.mult, 224.25 + C, A.add)
+        dma("y", [(lst("threeB", 96, 112), lst("threeB", 112, 128))], ["a8"], ["a8d"])
 
     XH = cols("xh", 0, C)
     DD = ["dd%d%d" % (h, b) for h in range(len(HRUNS)) for b in range(4)]
@@ -455,32 +443,33 @@ def rank_program(g, core, T, topo):
         dst = T.cores[rank ^ STEP[r]]
         hc, lc = "hc%d" % r, "lc%d" % r
         src, skey = (T.x0, "x0") if r == 0 else (T.xt, "xt")
+        sgap = {"L1": [halve(src, skey, CUT, 272)], "L2": [halve(src, skey, 272, 320)]}
         if r == 0:
-            bt = back_tables()
-            vgap = {"signs": [scatter(4, 8)], "scan": [scatter(8, 12)], "times": [scatter(12, 14)], "list": [scatter(14, 24)],
-                    "L0": [scatter(24, 28), bt[0]], "Q1": [bt[9]], "L2": [bt[10]], "L3": [bt[2]], "L4": [bt[3]],
-                    "last": [bt[1]], "scan4": [wrap_a8], "l4": [list_a8, bt[4]]}
-            sgap = {"signs": [lambda: halve(src, skey, 0, CUT), copy_half, lambda: halve(src, skey, CUT, 320),
-                              lambda: act(["sp4", "rep"], ["seg4"], T.seg4[:], T.sp[:, 16:32].indirect(T.rep[:, 0:28]))],
-                    "L4": [lambda: halve(src, skey, 320, C)]}
-            sgap["signs"].append(back_constants)
+            vgap = {"signs": [scatter(8, 12)], "scan": [lambda: quant(["wt0", "wt2", "wi"], ["shc"], "shc", 0, 224, T.wt, 0)],
+                    "times": [scatter(12, 14)], "list": [scatter(14, 16)], "L0": [scatter(16, 18)], "L1": [scatter(18, 22)], "L2": [scatter(22, 26)],
+                    "L3": [scatter(26, 28), lambda: cp(["iw", "lz"], ["joinF0"], lst("joinF", 0, 64), T.iw[0:64, :]), bt["row"]],
+                    "wrap": [bt["wrapinv"]], "fin": [bt["places"]], "last": [bt["inverse"], bt["wrap"]], "scan4": [wrap_a8], "l4": [bt["half"]]}
+            sgap.update({"signs": [lambda: act(["sp4", "rep"], ["seg4"], T.seg4[:], T.sp[:, 16:32].indirect(T.rep[:, 0:28])), late_constants],
+                         "last": [halve(src, skey, 320, C)]})
             dma("y", [(T.agrow[0:16, :], T.iot[0:16, 0:C])], ["iot"], ["ag0"])
+            dma("y", [(T.R[64:128, 0:C], T.rowq[48:112, :]), (T.R[0:64, 0:C], T.rowq[0:64, :])], both("rowq"), ["qs"])
         else:
-            vgap = {"signs": [lambda: turn("F")], "scan": [lambda: turn("B")], "scan4": [wrap_a8], "l4": [list_a8]}
-            sgap = {"signs": [lambda: halve(src, skey, 0, CUT), copy_half, lambda: halve(src, skey, CUT, 320)], "last": [lambda: halve(src, skey, 320, C)]}
-        chain("F", -1, SHARES["F0" if r == 0 else "F"], vgap, sgap)
+            vgap = {"signs": [lambda: turn("F")], "scan": [lambda: turn("B")], "scan4": [wrap_a8]}
+            sgap.update({"signs": [halve(src, skey, 0, CUT), copy_half], "L3": [halve(src, skey, 320, C)]})
+        chain("F", -1, SHARES["F"], vgap, sgap)
         dma("y", [(T.agrow[16:128, :], T.arow[0:112, :])], both("arow"), ["agrow"])
 
-        def layer(h, bs=range(4)):
+        def layer(h):
             a, e = HRUNS[h]
-            for b in bs:
-                bank = "P%d" % (4 + b)
-                mm(["wqc", "wqp"] + ["vc%d" % k for k in range(3) if a <= PARTS[k][0] < e], [bank], T[bank][:, 0:e - a], "wq", 128 * b, "vc", a, e - a)
+            for b in range(4):
+                bank = "P%d" % LAYER[h][b]
+                mm(["wqc", "wqp", "vc%d" % h], [bank], T[bank][:, 0:e - a], "wq", 128 * b, "vc", a, e - a)
 
-        def layer_out(h, b):
+        def scaled(h, b, q="s"):
             a, e = HRUNS[h]
-            bank = "P%d" % (4 + b)
-            act([bank], ["ht%d%d" % (h, b)], T.ht[:, 4 * a + b:4 * e:4], T[bank][:, 0:e - a], F.Copy, scale=0.03125)
+            bank = "P%d" % LAYER[h][b]
+            args = ([bank], ["ht%d%d" % (h, b)], T.ht[:, 4 * a + b:4 * e:4], T[bank][:, 0:e - a])
+            return (lambda: act(*args, F.Copy, scale=0.03125)) if q == "s" else (lambda: ts(*args, 0.03125, A.mult))
 
         def send(h):
             a, e = HRUNS[h]
@@ -498,114 +487,120 @@ def rank_program(g, core, T, topo):
         def unpack(h):
             a, e = HRUNS[h]
             for b in range(4):
-                bank = "P%d" % (4 - 4 * h + b)
+                bank = "P%d" % UNPACK[h][b]
                 mm(["ebc%d" % b, lc + str(h)], [bank], T[bank][:, 0:e - a], "ebc", 128 * b, lc, a, e - a)
 
-        def unpack_out(h, b, f=act):
+        def out(h, b, f=act):
             a, e = HRUNS[h]
-            bank = "P%d" % (4 - 4 * h + b)
-            f([bank], ["dd%d%d" % (h, b)], T.dd[:, 4 * a + b:4 * e:4], T[bank][:, 0:e - a])
+            bank = "P%d" % UNPACK[h][b]
+            return lambda: f([bank], ["dd%d%d" % (h, b)], T.dd[:, 4 * a + b:4 * e:4], T[bank][:, 0:e - a])
 
         first = (lambda k: bt[k]()) if r == 0 else (lambda k: None)
-        move(T.vt, "vt", T.xh, XH, T.xg, "xg", 0, CUT)
+        e = HRUNS[0][1]
+        move(T.vt, "vt", T.xh, XH, T.xg, "xg", 0, e)
         fetch(T.xh, XH, CUT, 320)
         fetch(T.xh, XH, 320, C)
-        gather(T.nrow, 0, "nrow", T.rowqi[:, 0:C], ["rowqi"], T.a8w, 0, ["a8w"], 0)
-        first(5)
-        add(T.vt, "vt", T.xh, "xh", CUT, 320)
-        first(6)
+        list_a8()
+        move(T.vt, "vt", T.xh, XH, T.xg, "xg", e, CUT)
         score(T.vt, "vt", "vc", 0)
-        layer(0, (0, 1, 2))
-        sign(0)
-        for b in range(3):
-            layer_out(0, b)
+        layer(0)
+        sign("vc", 0)
+        for b in range(4):
+            scaled(0, b)()
+        add(T.vt, "vt", T.xh, "xh", CUT, 320)
         add(T.vt, "vt", T.xh, "xh", 320, C)
         score(T.vt, "vt", "vc", 1)
-        layer(0, (3,))
-        layer_out(0, 3)
         score(T.vt, "vt", "vc", 2)
         layer(1)
-        first(7)
-        early_signs()
-        sign(1, cp)
-        sign(2, cp)
-        first(8)
-        early_scan()
-        vgap = {"signs": [lambda: scan(["seg16"] + both("nrow"), ["sm"], T.sm[:], T.seg16[:], T.nrow[:])], "scan": [lambda: send(0)], "times": [spread_n8],
-                "list": [lambda: send(1)], "Q2": [lambda: ts(["a8r", "c8"], ["a8"], T.ls[:, 196:224], T.a8r[:], col("c8"), A.add)],
-                "wrap": [lambda: unpack_out(1, 0, cp)], "fin": [lambda: unpack_out(1, 1, cp)],
+        first("mean")
+        send(0)
+        first("high")
+        early_signs("B")
+        sign("vc", 1)
+        sign("vc", 2, "v")
+        layer(2)
+        first("low")
+        early_scan("B")
+        vgap = {"signs": [scaled(1, 0, "v")], "scan": [scaled(1, 3, "v")], "times": [lambda: send(1)], "list": [lambda: send(2)], "last": [out(1, 2, cp)],
                 "scan4": [lambda: differ(0)], "l4": [lambda: differ(1)]}
+        sgap = {"signs": [scaled(1, 1), scaled(1, 2)] + [scaled(2, b) for b in range(4)],
+                "L1": [lambda: unpack(0), out(0, 0), out(0, 1)], "L2": [out(0, 2), out(0, 3)], "L3": [lambda: unpack(1), out(1, 0)], "fin": [lambda: unpack(2), out(1, 1)],
+                "last": [out(1, 3)] + [out(2, b) for b in range(4)]}
         if r == 0:
-            vgap["times"] += [ebq(0)]
-            vgap["list"] += [ebq(1)]
-            vgap["L0"] = [ebq(2), ebq(3)]
+            vgap["signs"] += [bt["own"]]
+            vgap.update({"mid": [bt["scale"]], "L0": [ebq(0)], "L1": [ebq(1)], "L2": [ebq(2)], "L3": [ebq(3)], "last": [out(2, 2, cp), out(2, 3, cp)]})
+            sgap.update({"L1": [], "L2": [], "L3": [lambda: unpack(0), lambda: unpack(1)], "fin": [out(0, b) for b in range(4)] + [lambda: unpack(2)],
+                         "last": [out(1, b) for b in range(4)] + [out(2, b) for b in range(2)]})
         if r == 1:
-            vgap["L0"] = [lambda: quant(["vv"], ["vq"], "vq", 0, 128, T.vv, 0)]
+            vgap["L1"] = [lambda: quant(["vv"], ["vq"], "vq", 0, 128, T.vv, 0)]
         if r == 2:
-            vgap["L0"] = [lambda: ts(["dhF", "kq"], ["dq"], T.dq[:, 1:3 * NV:3], tab("F", 2, 1, 0, NV), -K / 2, A.mult, col("kq"), A.mult),
-                              lambda: ts(["dhF", "kq"], ["dq1"], T.dq[:, 3 * NV + 1:84:3], tab("F", 2, 1, NV, 28), -K, A.mult, col("kq"), A.mult)]
-        sgap = {"signs": [lambda b=b: layer_out(1, b) for b in range(4)] + [lambda e=e: act(["t0F", "wqF"], ["dq%d" % e], T.dq[:, e:84:3], tab("F", 2, e)) for e in (0, 2) if r == 2],
-                "Q2": [lambda: unpack(0), lambda: unpack(1)], "L4": [lambda b=b: unpack_out(0, b) for b in range(2)],
-                "last": [lambda h=h, b=b: unpack_out(h, b) for h, b in ((0, 3), (1, 2), (1, 3))]}
-        vgap["last"] = [lambda: unpack_out(0, 2, cp)]
-        if r == 0:
-            vgap.update({"signs": vgap["scan"], "scan": vgap["signs"], "wrap": [lambda: unpack_out(0, 2, cp)], "fin": [lambda: unpack_out(0, 3, cp)],
-                         "last": [lambda: unpack_out(1, 0, cp)]})
-            sgap["last"] = [lambda b=b: unpack_out(1, b) for b in (1, 2, 3)]
-        chain("B", 1, SHARES["B0" if r == 0 else "B"], vgap, sgap)
+            vgap["L1"] = [lambda: ts(["F2", "kq"], ["dq"], T.dq[:, 1:3 * NV:3], tab("F", 2, 1, 0, NV), -K / 2, A.mult, col("kq"), A.mult),
+                          lambda: ts(["F2", "kq"], ["dq1"], T.dq[:, 3 * NV + 1:84:3], tab("F", 2, 1, NV, 28), -K, A.mult, col("kq"), A.mult)]
+            sgap.update({"L0": [lambda e=e: act(["F2"], ["dq%d" % e], T.dq[:, e:84:3], tab("F", 2, e)) for e in (0, 2)],
+                         "scan4": [lambda: turn_row(0)], "l4": [lambda: turn_row(1)]})
+        chain("B", 1, SHARES["B"], vgap, sgap)
         if r < 2:
             fetch(T.dd, DD, CUT, 320)
             fetch(T.dd, DD, 320, C)
-            turn_row()
+            turn_row(0)
+            turn_row(1)
             move(T.xt, "xt", T.dd, DD, T.vt, "vt", 0, CUT)
             add(T.xt, "xt", T.vt, "vt", CUT, 320)
             score(T.xt, "xt", "xc", 0)
-            sign(0)
+            sign("xc", 0)
             add(T.xt, "xt", T.vt, "vt", 320, C)
             score(T.xt, "xt", "xc", 1)
             score(T.xt, "xt", "xc", 2)
-            sign(1)
+            sign("xc", 1)
             turn_scan()
-            early_signs()
-            sign(2, cp)
-            early_scan()
+            early_signs("F")
+            sign("xc", 2, "v")
+            early_scan("F")
         else:
             def product(k):
-                a, b = PARTS[k]
+                a, b = PARTS["xc"][k]
                 quant(cols("xt", a, b), ["xc%d" % k], "xc", a, b, T.xt, 4 * a)
                 mm(["vq", "xc%d" % k], ["P%d" % k], T["P%d" % k][:, 0:b - a], "vq", 0, "xc", a, b - a)
 
             def result(k, f):
-                a, b = PARTS[k]
+                a, b = PARTS["xc"][k]
                 f(["P%d" % k], ["y%d" % k], T.ysb[:, a:b], T["P%d" % k][:, 0:b - a])
+
+            def store(k):
+                a, b = PARTS["xc"][k]
+                dma("y", [(T.y[:, a:b], T.ysb[:, a:b])], ["y%d" % k], ["yo%d" % k])
 
             def codes_out(a, b, keys):
                 dma("y", [(T.oc[:, 4 * a:4 * b], T.xc[:, a:b].bitcast(dt.uint8))], keys, ["oc%d" % a])
-            turn_row()
+
+            def scales_out(q, ks):
+                dma(q, [(T.osc[4 * k:4 * k + 4, :], T.xcp[32 * k:32 * k + 4, 0:C]) for k in ks], ["xc0", "xc1", "xc2"], ["osc" + q])
             fetch(T.dd, DD, 256, 320)
             fetch(T.dd, DD, 320, C)
             move(T.xt, "xt", T.dd, DD, T.vt, "vt", 0, CUT)
             move(T.xt, "xt", T.dd, DD, T.vt, "vt", CUT, 256)
-            scan(["seg16", "nu"], ["s3e", "s3m", "s3l"], T.s3[:, 0:3 * C:3], T.seg16[:], T.nu[:])
+            scan(["seg16", "nu0", "nu1"], ["s3e", "s3m", "s3l"], T.s3[:, 0:3 * C:3], T.seg16[:], T.nu[:])
             product(0)
-            e = PARTS[0][1]
+            e = PARTS["xc"][0][1]
             codes_out(0, e, ["xc0"])
             result(0, act)
-            dma("s", [(T.y[:, 0:e], T.ysb[:, 0:e])], ["y0"], ["yo0"])
-            op("v", ["s3e", "s3m", "s3l", "dq", "dq0", "dq1", "dq2"], ["t4"],
-               lambda: g.vector.tensor_tensor_scan(T.t4[:], T.dq[:], T.s3[:, 29:1358:16], 0.0, A.add, A.mult))
+            store(0)
             add(T.xt, "xt", T.vt, "vt", 256, 320)
-            ts(["t4"], ["qoU"], T.qoU[:], T.t4[:, 2:84:3], 224.25, A.add)
+            times(["dq", "dq0", "dq1", "dq2"], ["t4"], T.t4[:], T.dq[:])
             add(T.xt, "xt", T.vt, "vt", 320, C)
             product(1)
+            ts(["t4"], ["qoU"], T.qoU[:], T.t4[:, 2:84:3], 224.25, A.add)
             product(2)
-            act(["iot", "qoU"], ["qrow"], T.qrow[:], T.iot[:, 0:C].indirect(T.qoU[:, 0:28]), F.Identity, bias=224.0)
-            dma("s", [(T.qo[:], T.qrow[0:128:16, :])], ["qrow"], ["qo"])
+            ts(["iot", "qoU"], ["qrowv"], T.qrow[:, 0:160], T.iot[:, 0:C].indirect(T.qoU[:, 0:10]), 224.0, A.add)
+            act(["iot", "qoU"], ["qrows"], T.qrow[:, 160:C], T.iot[:, 0:C].indirect(T.qoU[:, 10:28]), F.Identity, bias=224.0)
+            dma("s", [(T.qo[:], T.qrow[0:128:16, :])], both("qrow"), ["qo"])
             codes_out(e, C, ["xc1", "xc2"])
             result(1, cp)
             result(2, cp)
-            dma("y", [(T.osc[4 * k:4 * k + 4, :], T.xcp[32 * k:32 * k + 4, 0:C]) for k in range(4)], ["xc0", "xc1", "xc2"], ["osc"])
-            dma("y", [(T.y[:, e:C], T.ysb[:, e:C])], ["y1", "y2"], ["yo1"])
+            scales_out("y", (0, 1))
+            store(1)
+            store(2)
+            scales_out("s", (2, 3))
     for sem in count:
         if max(known[q].get(sem, 0) for q in queue) < count[sem]:
             g.wait_ge(T.sem[sem], count[sem])

@@ -10,7 +10,7 @@ HRUNS = PARTS["vc"]
 LAYER = [(4, 5, 6, 7), (4, 5, 6, 7), (3, 0, 1, 2)]
 UNPACK = [(0, 1, 2, 3), (4, 5, 6, 7), (0, 1, 2, 3)]
 CUT = HEAD = 224
-SHARES = {"F": {}, "B": {"L4": 6}}
+SHARES = {"F0": {"L0": 10, "L1": 10, "L2": 10}, "F": {}, "B": {"L4": 6}}
 K = 2.0 ** 24
 M = 1.5 * 2.0 ** 27
 LS = {"one": 0, "twoF": 32, "threeF": 64, "joinF": 96, "twoB": 132, "threeB": 160, "pair": 192, "end": 224}
@@ -31,7 +31,7 @@ for _n, _w in (("qU", 28), ("sU", 28), ("mU", 28), ("loU", 28), ("ls0", 28), ("l
                ("ulist", 8), ("qoU", 28), ("rep", 28)):
     SCRATCH[_n] = ("sbuf", [128, _w], U16)
 for _n, _w in (("iwb", 84), ("fac", 84), ("iw", 28), ("tabC", 28), ("tC", 28),
-               ("tO", 56), ("tbF", 252), ("tbB", 252), ("t4", 84),
+               ("tO", 56), ("tbF", 252), ("tbB", 336), ("t4", 84),
                ("hq", 28), ("tq", 28), ("lo", 28), ("dq", 84), ("cq", 40), ("ysb", C), ("qrow", C)):
     SCRATCH[_n] = ("sbuf", [128, _w], F32)
 for _n, _w in (("gqi", 28), ("gsi", 28), ("gmi", 28), ("pi", 8), ("uli", 16)):
@@ -125,8 +125,11 @@ def rank_program(g, core, T, topo):
     def scan(reads, writes, out, seg, a):
         op("v", reads, writes, lambda: g.vector.tensor_tensor_scan(out, seg, a, 0.0, A.mult, A.add))
 
+    def cols(key, a, b):
+        return ["%s:%d" % (key, k) for k in range(a // 16, (b + 15) // 16)]
+
     def times(reads, writes, out, table):
-        op("v", ["s3e", "s3m", "s3l", "s30", "s31"] + reads, writes, lambda: g.vector.tensor_tensor_scan(out, table, T.s3[:, 29:1358:16], 0.0, A.add, A.mult))
+        op("v", cols("s3", 0, C) + ["s30", "s31"] + reads, writes, lambda: g.vector.tensor_tensor_scan(out, table, T.s3[:, 29:1358:16], 0.0, A.add, A.mult))
 
     def iota(key, out, pat, base, cm, flag=True):
         if flag:
@@ -134,17 +137,17 @@ def rank_program(g, core, T, topo):
         else:
             op("g", [], [key], lambda: g.iota(out, pat, base, cm))
 
-    def cols(key, a, b):
-        return ["%s:%d" % (key, k) for k in range(a // 16, (b + 15) // 16)]
-
     def both(key):
         return [key + "v", key + "s"]
 
-    def gather(out, o, okey, win, wkeys, lst, l0, lkeys, nv):
-        if nv:
-            cp(wkeys + lkeys, both(okey) if nv == 28 else [okey + "v"], out[:, o:o + 16 * nv], win.indirect(lst[:, l0:l0 + nv]))
-        if nv < 28:
-            act(wkeys + lkeys, both(okey) if nv == 0 else [okey + "s"], out[:, o + 16 * nv:o + C], win.indirect(lst[:, l0 + nv:l0 + 28]))
+    def gather(okey, out, win, lst, keys, a, nv, b):
+        if nv > a:
+            cp(keys, okey[0], out(16 * a, 16 * nv), win.indirect(lst(a, nv)))
+        if b > nv:
+            act(keys, okey[1], out(16 * nv, 16 * b), win.indirect(lst(nv, b)))
+
+    def view(t, o=0):
+        return lambda a, b: t[:, o + a:o + b]
 
     place = {"c16": 0, "c4": 1, "c1": 2, "cg": 3}
 
@@ -158,9 +161,6 @@ def rank_program(g, core, T, topo):
 
     def const(name, src, s1, o1, s2=None, o2=None):
         ts([src], [name], col(name), col(src), s1, o1, s2, o2)
-
-    def aconst(name, src, f, scale, bias):
-        act([src], [name], col(name), col(src), f, scale=scale, bias=bias)
 
     def lst(name, a=0, b=128, n=28):
         return T.ls[a:b, LS[name]:LS[name] + n]
@@ -193,13 +193,15 @@ def rank_program(g, core, T, topo):
         e = EARLY[d]
         keys, out, src = cols("sg", 0, 16 * e) + ["loU"], T.mg[:, 0:16 * e], T.sg[:, 0:16 * e].indirect(T.loU[:, 0:e])
         if q == "s":
-            act(keys, ["mge", "mgv"], out, src, F.Copy, scale=0.5)
+            act(keys, cols("mg", 0, 16 * e), out, src, F.Copy, scale=0.5)
         else:
-            ts(keys, ["mge", "mgv"], out, src, 0.0, A.is_gt, -0.5, A.add)
+            ts(keys, cols("mg", 0, 16 * e), out, src, 0.0, A.is_gt, -0.5, A.add)
+
+    def wrap_signs(a, b):
+        scan(["seg16"] + cols("mg", 16 * a, 16 * b), cols("s3", 16 * a, 16 * b), T.s3[:, 48 * a:48 * b:3], T.seg16[:, 16 * a:16 * b], T.mg[:, 16 * a:16 * b])
 
     def early_scan(d):
-        e = EARLY[d]
-        scan(["seg16", "mge"], ["s3e", "s3m"], T.s3[:, 0:48 * e:3], T.seg16[:, 0:16 * e], T.mg[:, 0:16 * e])
+        wrap_signs(0, EARLY[d])
 
     def halve(src, key, a, b):
         return lambda: act(cols(key, a, b), cols("xh", a, b), T.xh[:, 4 * a:4 * b], src[:, 4 * a:4 * b], F.Copy, scale=0.5)
@@ -218,40 +220,34 @@ def rank_program(g, core, T, topo):
 
     def tables(d):
         t, k0, k1, k2 = T["tb" + d], d + "0", d + "1", d + "2"
+        n = 2 if d == "F" else 3
+        u = t[:, 84 * n:84 * n + 84]
         return {
             "wrap": lambda: scan(["seg16"] + both("rowt"), ["sn"], T.sn[:], T.seg16[:], T.rowt[:]),
             "half": lambda: ts(["sn", "kaph"], ["tq"], T.tq[:], T.sn[:, 15:C:16], col("kaph"), A.mult),
-            "mean": lambda: (tt(["tq", "hq"], [d + "q"], tab(d, 2, 2), T.tq[:], T.hq[:], A.add),
-                             tt(["tq", "hq"], [d + "d"], tab(d, 2, 1), T.tq[:], T.hq[:], A.subtract)),
-            "high": lambda: ts([d + "z", d + "q", d + "d"], [k0], t[:, 0:84], t[:, 168:252], M, A.add, -M, A.add),
-            "low": lambda: tt([d + "z", d + "q", d + "d", k0], [k1], t[:, 84:168], t[:, 168:252], t[:, 0:84], A.subtract),
-            "scale": lambda: tt(["fac", d + "z"], [k0, k1, k2, d + "q", d + "d"], t[:, 1:252:3], t[:, 1:252:3], T.fac[:], A.mult),
+            "mean": lambda: (tt(["tq", "hq"], [d + "q"], tab(d, n, 2), T.tq[:], T.hq[:], A.add),
+                             tt(["tq", "hq"], [d + "d"], tab(d, n, 1), T.tq[:], T.hq[:], A.subtract)),
+            "high": lambda: ts([d + "z", d + "q", d + "d"], [k0], t[:, 0:84], u, M, A.add, -M, A.add),
+            "low": lambda: tt([d + "z", d + "q", d + "d", k0], [k1], t[:, 84:168], u, t[:, 0:84], A.subtract),
+            "scale": lambda: tt(["fac", d + "z"], [k0, k1, k2, d + "q", d + "d"] + ["Bo0", "Bo1", "Bu"] * (d == "B"), t[:, 1:252:3], t[:, 1:252:3], T.fac[:], A.mult),
         }
 
     def back_tables():
         def inverse():
-            ts(["sd", "kaph"], ["hq"], T.hq[:], T.sd[:, 15:C:16], col("kaph"), A.mult)
+            ts(["sda", "kaph"], ["hq"], T.hq[:], T.sd[:, 15:C:16], col("kaph"), A.mult)
             for k in range(2):
-                ts(["sd", "kap"], ["q7%d" % k], T.q7[0:32, 32 * k:32 * k + 28], T.sd[0:32, 15:C:16], col("kap", 0, 32), A.mult, 224.25 + C * k, A.add)
+                ts(["sda", "kap"], ["q7%d" % k], T.q7[0:32, 32 * k:32 * k + 28], T.sd[0:32, 15:C:16], col("kap", 0, 32), A.mult, 224.25 + C * k, A.add)
             dma("y", [(lst("twoB", 96, 112), T.q7[0:16, 32:60]), (lst("twoB", 112, 128), T.q7[0:16, 0:28])], ["q70", "q71", "lz"], ["q7"])
         return dict(
             tables("B"),
-            row=lambda: gather(T.rowt, 0, "rowt", T.rowqs[:, 0:C], ["inv"], T.mU, 0, ["mU"], 0),
-            wrapinv=lambda: scan(["seg16", "inv"], ["sd"], T.sd[:], T.seg16[:], T.rowqs[:]),
+            row=lambda: gather((None, both("rowt")), view(T.rowt), T.rowqs[:, 0:C], view(T.mU), ["inv", "mU"], 0, 0, 28),
+            wrapinv=lambda: scan(["seg16", "inv"], ["sda", "sdb"], T.sd[:], T.seg16[:], T.rowqs[:]),
             inverse=inverse,
+            upper=lambda: cp(["Bz", "Bq", "Bd"], ["Bu"], T.tbB[64:128, 168:252], T.tbB[64:128, 252:336]),
             places=lambda: (ts(["gmi"], ["tO0"], T.tO[:, 0:28], T.gmi[:], 0.5, A.mult, -112.0, A.add),
                             ts(["iw"], ["tO1"], T.tO[:, 28:56], T.iw[:], 0.5, A.mult, -112.0, A.add)),
-            own=lambda: (tt(["tO0", "tO1"], ["Bq"], tab("B", 2, 2, p=64), T.tO[0:64, 0:28], T.tO[0:64, 28:56], A.add),
-                         tt(["tO0", "tO1"], ["Bd"], tab("B", 2, 1, p=64), T.tO[0:64, 0:28], T.tO[0:64, 28:56], A.subtract)))
-
-    def late_constants():
-        act(["iw", "short", "from"], ["tabC"], T.tabC[:], T.iw[:], F.Identity, scale=col("short"), bias=col("from"))
-        aconst("r2", "c4", F.Relu, 1.0, -2.0)
-        aconst("kap2", "kap", F.Identity, -2.0, 0.0)
-        aconst("r14", "c16", F.Relu, 1.0, -14.0)
-        aconst("c896", "c1", F.Identity, 1.0, 896.25)
-        aconst("k4", "r2", F.Identity, 4.0, 4 / K)
-        aconst("kq", "r14", F.Identity, 1 / K - 1, 1.0)
+            own=lambda: (tt(["tO0", "tO1"], ["Bo0"], tab("B", 2, 2, p=64), T.tO[0:64, 0:28], T.tO[0:64, 28:56], A.add),
+                         tt(["tO0", "tO1"], ["Bo1"], tab("B", 2, 1, p=64), T.tO[0:64, 0:28], T.tO[0:64, 28:56], A.subtract)))
 
     tf, bt = tables("F"), back_tables()
     iota("pi", icol("pi"), [[0, 1]], 0, 1, False)
@@ -278,23 +274,26 @@ def rank_program(g, core, T, topo):
     const("kap", "c16", 15.0, A.is_equal, 1 / K, A.max)
     const("short", "cg", 3.0, A.is_lt)
     const("g448", "cg", float(C), A.mult, 0.25, A.add)
+    const("k1", "c4", 3.0, A.is_equal, 1 / K, A.max)
+    const("c896", "c1", 896.25, A.add)
     tt(["sa", "sb"], ["sp"], T.sp[:, 0:16], T.sa[:, 0:16], T.sb[:, 0:16], A.max)
     act(["z"], ["wt0"], T.wt[:, 0:192], T.zt[:, 0:192])
     act(["z"], ["wt2"], T.wt[:, 704:896], T.zt[:, 0:192])
-    for d in "FB":
-        act(["z"], [d + "z"], T["tb" + d][:, 168:252:3], T.zt[:, 0:28])
+    act(["z"], ["Fz"], T.tbF[:, 168:252:3], T.zt[:, 0:28])
+    act(["z"], ["Bz"], T.tbB[:, 168:336:3], T.zt[:, 0:56])
     act(["sp", "rep"], ["seg16"], T.seg16[:], T.sp[:, 0:16].indirect(T.rep[:, 0:28]))
     cp(["gqi"], ["qU"], T.qU[:], T.gqi[:])
     const("kaph", "kap", 0.5, A.mult)
     const("from", "g448", 224.25 + 2 * C, A.min)
     cp(["gmi"], ["mU"], T.mU[:], T.gmi[:])
     ts(["gqi"], ["hq"], T.hq[:], T.gqi[:], 0.5, A.mult, -112.0, A.add)
-    gather(T.rowq, 0, "rowq", T.iot[:, 0:C], ["iot"], T.qU, 0, ["qU"], 28)
+    const("k4", "k1", 4.0, A.mult)
+    gather((both("rowq"), None), view(T.rowq), T.iot[:, 0:C], view(T.qU), ["iot", "qU"], 0, 28, 28)
     quant(["ut"], ["uc"], "uc", 0, 128, T.ut, 0)
     cp(["uli", "uli0"], ["ulist"], T.ulist[:], T.uli[:, 0:8])
     ts(["iwb", "c16"], ["iw"], T.iw[:], T.iwb[:, 0:28], col("c16"), A.add)
     ts(["iwb"], ["fac"], T.fac[:], T.iwb[:], 16.0 * NV, A.is_lt, 1.0, A.add)
-    gather(T.rowt, 0, "rowt", T.rowq[:, 0:C], both("rowq"), T.mU, 0, ["mU"], 14)
+    gather((["rowtv"], ["rowts"]), view(T.rowt), T.rowq[:, 0:C], view(T.mU), both("rowq") + ["mU"], 0, 14, 28)
     act(["uc", "ulist"], ["uqs"], T.uqp[:, 0:128], T.ucp[:, 0:128].indirect(T.ulist[:, 0:8]))
     cp(["uc", "ulist"], ["uqc"], T.uq[:, 0:128].bitcast(dt.uint32), T.uc[:, 0:128].bitcast(dt.uint32).indirect(T.ulist[:, 0:8]))
     tt(["gmi", "iw"], ["lo"], T.lo[:], T.gmi[:], T.iw[:], A.min)
@@ -316,25 +315,28 @@ def rank_program(g, core, T, topo):
     tf["high"]()
     ts(["j4", "c4"], ["sa4"], T.sa[:, 16:32], T.j4[:, 16:32], col("c4"), A.not_equal)
     ts(["j4", "c4"], ["sb4"], T.sb[:, 16:32], T.j4[:, 0:16], col("c4"), A.is_equal, K, A.mult)
-    scatter(4, 8)()
     early_signs("F", "s")
-    tf["low"]()
     sign("xc", 2, "v")
-    early_scan("F")
+    tf["low"]()
     tt(["sa4", "sb4"], ["sp4"], T.sp[:, 16:32], T.sa[:, 16:32], T.sb[:, 16:32], A.max)
-    tf["scale"]()
+
+    H = HEAD // 16
+    HALF = {"a": (0, H), "b": (H, 28), "ab": (0, 28)}
+
+    def row_keys(i, hs="ab"):
+        return ["qs"] if i == -1 else [k for h in hs for k in both("L%s%s" % (i, h))]
 
     def chain(d, way, shares, vgap, sgap):
         def gap(name):
             for f in vgap.get(name, []) + sgap.get(name, []):
                 f()
         early = EARLY[d]
-        ts(cols("sg", 0, 16 * NV) + ["loU"], ["mgv"], T.mg[:, 16 * early:16 * NV], T.sg[:, 0:16 * NV].indirect(T.loU[:, early:NV]), 0.0, A.is_gt, -0.5, A.add)
-        act(cols("sg", 0, C) + ["loU"], ["mgs"], T.mg[:, 16 * NV:C], T.sg[:, 0:C].indirect(T.loU[:, NV:28]), F.Sign, bias=-(2.0 ** -93))
+        ts(cols("sg", 0, 16 * NV) + ["loU"], cols("mg", 16 * early, 16 * NV), T.mg[:, 16 * early:16 * NV], T.sg[:, 0:16 * NV].indirect(T.loU[:, early:NV]), 0.0, A.is_gt, -0.5, A.add)
+        act(cols("sg", 0, C) + ["loU"], cols("mg", 16 * NV, C), T.mg[:, 16 * NV:C], T.sg[:, 0:C].indirect(T.loU[:, NV:28]), F.Sign, bias=-(2.0 ** -93))
         gap("signs")
-        scan(["seg16", "mgv"], ["s3m"], T.s3[:, 48 * early:48 * NV:3], T.seg16[:, 16 * early:16 * NV], T.mg[:, 16 * early:16 * NV])
+        wrap_signs(early, NV)
         gap("mid")
-        scan(["seg16", "mgs"], ["s3l"], T.s3[:, 48 * NV:3 * C:3], T.seg16[:, 16 * NV:C], T.mg[:, 16 * NV:C])
+        wrap_signs(NV, 28)
         gap("scan")
         for k, okeys, out in ((0, ["z0", "z"], T.zt[:, 0:336:4]), (1, ["z1"], T.zt[:, 1:336:4]), (2, ["t4"], T.t4[:])):
             times([d + str(k)], okeys, out, T["tb" + d][:, 84 * k:84 * k + 84])
@@ -345,65 +347,83 @@ def rank_program(g, core, T, topo):
             bank = "P%d" % (3 + n)
             mm(["zc", "shc"], [bank], T[bank][:, 0:128], "shc", 48 + way * 16 * n, "zc", 0, 128)
         gap("list")
+        row = "arow" if d == "F" else "brow"
 
-        def window(a, b):
-            return T.R[:, (a + 1) * C:(b + 1) * C], [k for i in range(a, b) for k in (both("L%d" % i) if i >= 0 else ["qs"])]
+        def compose(n, out, win, lists, keys, hs):
+            a, b = HALF[hs]
+            nv = a + shares.get("L%s" % n, {"a": 8, "b": 6, "ab": 14}[hs])
+            gather((["L%s%sv" % (n, h) for h in hs], ["L%s%ss" % (n, h) for h in hs]), out, win, lists, keys, a, nv, b)
 
-        def step(n, a, name, keys):
-            win, wkeys = window(a, n)
-            gather(T.R, (n + 1) * C, "L%d" % n, win, wkeys, T.ls, LS[name], keys + ["lz"], shares.get("L%d" % n, 14))
+        def step(n, a, b, name, keys, hs="ab"):
+            out = view(T[row]) if n == row else view(T.R, (n + 1) * C)
+            compose(n, out, T.R[:, (a + 1) * C:(b + 1) * C], view(T.ls, LS[name]), [k for i in range(a, b) for k in row_keys(i)] + keys + ["lz"], hs)
 
-        def wrap(key, n, p, w=32):
-            scan(["seg16"] + both("L%d" % n), [key], T[key][p:p + w, :], T.seg16[p:p + w, :], T.R[p:p + w, (n + 1) * C:(n + 2) * C])
+        def wrap(key, n, p, w, hs="ab"):
+            a, b = 16 * HALF[hs][0], 16 * HALF[hs][1]
+            scan(["seg16"] + row_keys(n, hs), [key + h for h in hs], T[key][p:p + w, a:b], T.seg16[p:p + w, a:b], T.R[p:p + w, (n + 1) * C + a:(n + 1) * C + b])
 
-        def hand(key, p, name, to, w=32):
-            for q, row in to:
-                ts([key, "kap", "lz"], ["%s%d" % (name, q)], lst(name, q, q + w), T[key][p:p + w, 15:C:16], col("kap", p, p + w), A.mult, 224.25 + row * C, A.add)
-            return ["%s%d" % (name, q) for q, row in to]
+        def hand(key, p, w, name, to, hs="ab"):
+            a, b = HALF[hs]
+            for q, at in to:
+                ts([key + h for h in hs] + ["kap", "lz"], ["%s%d%s" % (name, q, h) for h in hs], T.ls[q:q + w, LS[name] + a:LS[name] + b],
+                   T[key][p:p + w, 16 * a + 15:16 * b:16], col("kap", p, p + w), A.mult, 224.25 + at * C, A.add)
+            return ["%s%d%s" % (name, q, h) for q, at in to for h in hs]
 
-        gather(T.R, C, "L0", T.iot[:, 0:C], ["iot"], T.ls0, 0, ["ls0"], shares.get("L0", 14))
+        def wrap4(h):
+            a, b = 16 * HALF[h][0], 16 * HALF[h][1]
+            scan(["seg4"] + row_keys(row, h), ["sc4" + h], T.sc4[:, a:b], T.seg4[:, a:b], T[row][:, a:b])
+
+        def offsets(h):
+            a, b = 16 * HALF[h][0], 16 * HALF[h][1]
+            ts(["sc4" + h, "k4", "c896"], ["l4" + h], T.l4[:, a // 4:b // 4], T.sc4[:, a + 3:b:4], col("k4"), A.mult, col("c896"), A.add)
+
+        compose(0, view(T.R, C), T.iot[:, 0:C], view(T.ls0), ["iot", "ls0"], "ab")
         gap("own")
         ts(["P4", "lz"], ["one"], lst("one"), T.P4[:, 2:84:3], 224.25, A.add)
         if d == "F":
             ts(["P5", "lz"], ["twoF"], lst("twoF"), T.P5[:, 2:84:3], 224.25, A.add)
             tt(["P6", "tabC"], ["tC"], T.tC[:], T.P6[:, 2:84:3], T.tabC[:], A.add)
             gap("L0")
-            step(1, 0, "one", ["one"])
+            step(1, 0, 1, "one", ["one"])
             cp(["tC", "lz"], ["threeF"], lst("threeF"), T.tC[:])
             gap("L1")
-            step(2, 1, "twoF", ["twoF"])
+            step(2, 1, 2, "twoF", ["twoF"])
             gap("L2")
-            step(3, 0, "threeF", ["threeF"])
+            for h in "ab":
+                step(3, 0, 3, "threeF", ["threeF"], h)
             gap("L3")
-            wrap("sc", 3, 0, 64)
+            for h in "ab":
+                wrap("sc", 3, 0, 64, h)
             gap("wrap")
-            name, keys, rows = "joinF", hand("sc", 0, "joinF", ((64, 0),), 64) + ["joinF0"], (3, 4)
+            keys = {h: hand("sc", 0, 64, "joinF", ((64, 0),), h) + ["joinF0"] for h in "ab"}
+            name, rows = "joinF", (3, 4)
         else:
             ts(["P5", "lz"], ["twoB"], lst("twoB", 0, 64), T.P5[0:64, 2:84:3], 224.25 + C, A.add)
             ts(["P6", "lz"], ["threeB"], lst("threeB", 0, 64), T.P6[0:64, 2:84:3], 224.25 + C, A.add)
             gap("L0")
-            step(1, 0, "one", ["one"])
+            step(1, 0, 1, "one", ["one"])
             gap("L1")
-            step(2, 0, "twoB", ["twoB", "q7"])
-            wrap("sc", 1, 64)
+            step(2, 0, 2, "twoB", ["twoB", "q7"])
+            wrap("sc", 1, 64, 32)
             gap("L2")
-            step(3, 1, "threeB", ["threeB", "a8", "a8d"])
-            keys = hand("sc", 64, "pair", ((0, 4), (64, 0)))
+            step(3, 1, 3, "threeB", ["threeB", "a8", "a8d"])
+            pair = hand("sc", 64, 32, "pair", ((0, 4), (64, 0)))
             gap("L3")
-            wrap("sd", 3, 96)
-            step(4, -1, "pair", keys)
+            wrap("sd", 3, 96, 32)
+            step(4, -1, 4, "pair", pair)
             gap("wrap")
-            name, keys, rows = "end", hand("sd", 96, "end", ((0, 5), (32, 4), (64, 5), (96, 0))), (-1, 5)
+            keys = dict.fromkeys("ab", hand("sd", 96, 32, "end", ((0, 5), (32, 4), (64, 5), (96, 0))))
+            name, rows = "end", (-1, 5)
         gap("fin")
-        row = "arow" if d == "F" else "brow"
-        win, wkeys = window(*rows)
-        gather(T[row], 0, row, win, wkeys, T.ls, LS[name], keys, shares.get("last", HEAD // 16))
+        for h in "ab":
+            step(row, rows[0], rows[1], name, keys[h], h)
         gap("last")
-        scan(["seg4", row + "v"], ["sc4a"], T.sc4[:, 0:HEAD], T.seg4[:, 0:HEAD], T[row][:, 0:HEAD])
-        scan(["seg4"] + both(row), ["sc4b"], T.sc4[:, HEAD:C], T.seg4[:, HEAD:C], T[row][:, HEAD:C])
+        wrap4("a")
+        gap("four")
+        wrap4("b")
+        offsets("a")
         gap("scan4")
-        ts(["sc4a", "k4", "c896"], ["l4a"], T.l4[:, 0:HEAD // 4], T.sc4[:, 3:HEAD:4], col("k4"), A.mult, col("c896"), A.add)
-        ts(["sc4b", "k4", "c896"], ["l4b"], T.l4[:, HEAD // 4:], T.sc4[:, HEAD + 3:C:4], col("k4"), A.mult, col("c896"), A.add)
+        offsets("b")
         gap("l4")
 
     def move(out, okey, win, wkeys, base, bkey, a, b):
@@ -428,10 +448,10 @@ def rank_program(g, core, T, topo):
             tt(["sn"], [d + str(k)], v, v, T.sn[:, 15:C:16], A.mult)
 
     def differ(k):
-        tt(both("brow") + ["agrow", "ag0"], ["df%d" % k], T.df[:, 224 * k:224 * k + 224], T.brow[:, 224 * k:224 * k + 224], T.agrow[:, 224 * k:224 * k + 224], A.not_equal)
+        return lambda: tt(row_keys("brow", "ab"[k]) + ["agrow", "ag0"], ["df%d" % k], T.df[:, 224 * k:224 * k + 224], T.brow[:, 224 * k:224 * k + 224], T.agrow[:, 224 * k:224 * k + 224], A.not_equal)
 
     def wrap_a8():
-        scan(["seg16"] + both("arow"), ["sm"], T.sm[96:128, :], T.seg16[96:128, :], T.arow[96:128, :])
+        scan(["seg16"] + row_keys("arow"), ["sm"], T.sm[96:128, :], T.seg16[96:128, :], T.arow[96:128, :])
 
     def list_a8():
         ts(["sm", "kap", "lz"], ["a8", "a8d"], lst("threeB", 96, 128), T.sm[96:128, 15:C:16], col("kap", 96, 128), A.mult, 224.25 + C, A.add)
@@ -443,25 +463,33 @@ def rank_program(g, core, T, topo):
         dst = T.cores[rank ^ STEP[r]]
         hc, lc = "hc%d" % r, "lc%d" % r
         src, skey = (T.x0, "x0") if r == 0 else (T.xt, "xt")
-        sgap = {"L1": [halve(src, skey, CUT, 272)], "L2": [halve(src, skey, 272, 320)]}
         if r == 0:
-            vgap = {"signs": [scatter(8, 12)], "scan": [lambda: quant(["wt0", "wt2", "wi"], ["shc"], "shc", 0, 224, T.wt, 0)],
-                    "times": [scatter(12, 14)], "list": [scatter(14, 16)], "L0": [scatter(16, 18)], "L1": [scatter(18, 22)], "L2": [scatter(22, 26)],
-                    "L3": [scatter(26, 28), lambda: cp(["iw", "lz"], ["joinF0"], lst("joinF", 0, 64), T.iw[0:64, :]), bt["row"]],
-                    "wrap": [bt["wrapinv"]], "fin": [bt["places"]], "last": [bt["inverse"], bt["wrap"]], "scan4": [wrap_a8], "l4": [bt["half"]]}
-            sgap.update({"signs": [lambda: act(["sp4", "rep"], ["seg4"], T.seg4[:], T.sp[:, 16:32].indirect(T.rep[:, 0:28])), late_constants],
-                         "last": [halve(src, skey, 320, C)]})
+            vgap = {"signs": [tf["scale"], lambda: early_scan("F")], "scan": [lambda: quant(["wt0", "wt2", "wi"], ["shc"], "shc", 0, 224, T.wt, 0)],
+                    "times": [scatter(4, 6)], "list": [scatter(6, 10)],
+                    "own": [lambda: ts(["iw", "short", "from"], ["tabC"], T.tabC[:], T.iw[:], col("short"), A.mult, col("from"), A.add)],
+                    "L0": [scatter(10, 16)], "L1": [scatter(16, 22)], "L2": [scatter(22, 28)],
+                    "L3": [lambda: cp(["iw", "lz"], ["joinF0"], lst("joinF", 0, 64), T.iw[0:64, :]), bt["row"], bt["places"]], "wrap": [bt["wrapinv"]],
+                    "fin": [lambda: const("kap2", "kap", -2.0, A.mult), lambda: const("kq", "c16", 15.0, A.not_equal, 1 / K, A.max)],
+                    "last": [bt["inverse"]], "four": [bt["wrap"]], "scan4": [wrap_a8], "l4": [bt["half"]]}
+            sgap = {"signs": [lambda: act(["sp4", "rep"], ["seg4"], T.seg4[:], T.sp[:, 16:32].indirect(T.rep[:, 0:28])), halve(src, skey, CUT, 320)],
+                    "last": [halve(src, skey, 320, C)]}
             dma("y", [(T.agrow[0:16, :], T.iot[0:16, 0:C])], ["iot"], ["ag0"])
             dma("y", [(T.R[64:128, 0:C], T.rowq[48:112, :]), (T.R[0:64, 0:C], T.rowq[0:64, :])], both("rowq"), ["qs"])
         else:
             vgap = {"signs": [lambda: turn("F")], "scan": [lambda: turn("B")], "scan4": [wrap_a8]}
-            sgap.update({"signs": [halve(src, skey, 0, CUT), copy_half], "L3": [halve(src, skey, 320, C)]})
-        chain("F", -1, SHARES["F"], vgap, sgap)
-        dma("y", [(T.agrow[16:128, :], T.arow[0:112, :])], both("arow"), ["agrow"])
+            sgap = {"signs": [halve(src, skey, 0, CUT), copy_half, halve(src, skey, CUT, 320)], "L3": [halve(src, skey, 320, C)]}
+        if r == 1:
+            vgap["L1"] = [lambda: quant(["vv"], ["vq"], "vq", 0, 128, T.vv, 0)]
+        if r == 2:
+            vgap["L1"] = [lambda: ts(["F2", "kq"], ["dq"], T.dq[:, 1:3 * NV:3], tab("F", 2, 1, 0, NV), -K / 2, A.mult, col("kq"), A.mult),
+                          lambda: ts(["F2", "kq"], ["dq1"], T.dq[:, 3 * NV + 1:84:3], tab("F", 2, 1, NV, 28), -K, A.mult, col("kq"), A.mult)]
+            vgap["L2"] = [lambda e=e: cp(["F2"], ["dq%d" % e], T.dq[:, e:84:3], tab("F", 2, e)) for e in (0, 2)]
+        chain("F", -1, SHARES["F" if r else "F0"], vgap, sgap)
+        dma("y", [(T.agrow[16:128, :], T.arow[0:112, :])], row_keys("arow"), ["agrow"])
 
-        def layer(h):
+        def layer(h, bs=range(4)):
             a, e = HRUNS[h]
-            for b in range(4):
+            for b in bs:
                 bank = "P%d" % LAYER[h][b]
                 mm(["wqc", "wqp", "vc%d" % h], [bank], T[bank][:, 0:e - a], "wq", 128 * b, "vc", a, e - a)
 
@@ -471,31 +499,33 @@ def rank_program(g, core, T, topo):
             args = ([bank], ["ht%d%d" % (h, b)], T.ht[:, 4 * a + b:4 * e:4], T[bank][:, 0:e - a])
             return (lambda: act(*args, F.Copy, scale=0.03125)) if q == "s" else (lambda: ts(*args, 0.03125, A.mult))
 
-        def send(h):
+        def pack(h):
             a, e = HRUNS[h]
             quant(["ht%d%d" % (h, b) for b in range(4)], [hc + str(h)], hc, a, e, T.ht, 4 * a)
-            need("g", W[hc + str(h)])
+
+        def send(*hs):
+            pack(hs[-1])
+            a, e = HRUNS[hs[0]][0], HRUNS[hs[-1]][1]
+            need("g", [t for h in hs for t in W[hc + str(h)]])
             rid, pid, _ = topo.addr(dst)
             mask, ne = topo.mask(core, dst), len(topo.engines(core, dst))
-            arr = "arr%d" % (3 * r + h)
-            g.remote_dma(out_ap=T[lc][:, a:e].bitcast(dt.uint8), in_ap=T[hc][:, a:e].bitcast(dt.uint8), remote_sem=T.sem[arr], local_sem=T.sem["snt"], pid=pid, routing_id=rid, dma_engine_mask=mask)
-            g.remote_dma(out_ap=T[lc + "p"][:, a:e], in_ap=T[hc + "p"][:, a:e], remote_sem=T.sem[arr], local_sem=T.sem["snt"], pid=pid, routing_id=rid, dma_engine_mask=mask)
+            arr = "arr%d" % (3 * r + hs[0])
+            for o, i in ((T[lc][:, a:e].bitcast(dt.uint8), T[hc][:, a:e].bitcast(dt.uint8)), (T[lc + "p"][:, a:e], T[hc + "p"][:, a:e])):
+                g.remote_dma(out_ap=o, in_ap=i, remote_sem=T.sem[arr], local_sem=T.sem["snt"], pid=pid, routing_id=rid, dma_engine_mask=mask)
             count[arr] = 2 * ne
             count["snt"] = count.get("snt", 0) + 2 * ne
-            W[lc + str(h)] = [(arr, 2 * ne, {})]
+            for h in hs:
+                W[lc + str(h)] = [(arr, 2 * ne, {})]
 
         def unpack(h):
             a, e = HRUNS[h]
-            for b in range(4):
-                bank = "P%d" % UNPACK[h][b]
-                mm(["ebc%d" % b, lc + str(h)], [bank], T[bank][:, 0:e - a], "ebc", 128 * b, lc, a, e - a)
+            return lambda: [mm(["ebc%d" % b, lc + str(h)], ["P%d" % k], T["P%d" % k][:, 0:e - a], "ebc", 128 * b, lc, a, e - a) for b, k in enumerate(UNPACK[h])]
 
         def out(h, b, f=act):
             a, e = HRUNS[h]
             bank = "P%d" % UNPACK[h][b]
             return lambda: f([bank], ["dd%d%d" % (h, b)], T.dd[:, 4 * a + b:4 * e:4], T[bank][:, 0:e - a])
 
-        first = (lambda k: bt[k]()) if r == 0 else (lambda k: None)
         e = HRUNS[0][1]
         move(T.vt, "vt", T.xh, XH, T.xg, "xg", 0, e)
         fetch(T.xh, XH, CUT, 320)
@@ -505,39 +535,50 @@ def rank_program(g, core, T, topo):
         score(T.vt, "vt", "vc", 0)
         layer(0)
         sign("vc", 0)
-        for b in range(4):
-            scaled(0, b)()
+        scaled(0, 0)()
+        scaled(0, 1)()
         add(T.vt, "vt", T.xh, "xh", CUT, 320)
         add(T.vt, "vt", T.xh, "xh", 320, C)
         score(T.vt, "vt", "vc", 1)
+        layer(1, (0,))
         score(T.vt, "vt", "vc", 2)
-        layer(1)
-        first("mean")
-        send(0)
-        first("high")
-        early_signs("B")
-        sign("vc", 1)
-        sign("vc", 2, "v")
-        layer(2)
-        first("low")
-        early_scan("B")
-        vgap = {"signs": [scaled(1, 0, "v")], "scan": [scaled(1, 3, "v")], "times": [lambda: send(1)], "list": [lambda: send(2)], "last": [out(1, 2, cp)],
-                "scan4": [lambda: differ(0)], "l4": [lambda: differ(1)]}
-        sgap = {"signs": [scaled(1, 1), scaled(1, 2)] + [scaled(2, b) for b in range(4)],
-                "L1": [lambda: unpack(0), out(0, 0), out(0, 1)], "L2": [out(0, 2), out(0, 3)], "L3": [lambda: unpack(1), out(1, 0)], "fin": [lambda: unpack(2), out(1, 1)],
-                "last": [out(1, 3)] + [out(2, b) for b in range(4)]}
+        scaled(0, 2, "v")()
+        scaled(0, 3, "v")()
+        layer(1, (1, 2, 3))
         if r == 0:
-            vgap["signs"] += [bt["own"]]
-            vgap.update({"mid": [bt["scale"]], "L0": [ebq(0)], "L1": [ebq(1)], "L2": [ebq(2)], "L3": [ebq(3)], "last": [out(2, 2, cp), out(2, 3, cp)]})
-            sgap.update({"L1": [], "L2": [], "L3": [lambda: unpack(0), lambda: unpack(1)], "fin": [out(0, b) for b in range(4)] + [lambda: unpack(2)],
-                         "last": [out(1, b) for b in range(4)] + [out(2, b) for b in range(2)]})
-        if r == 1:
-            vgap["L1"] = [lambda: quant(["vv"], ["vq"], "vq", 0, 128, T.vv, 0)]
+            bt["mean"]()
+            bt["own"]()
+            send(0)
+            sign("vc", 1)
+            scaled(1, 0)()
+            sign("vc", 2, "v")
+            layer(2)
+            bt["high"]()
+            early_signs("B")
+            bt["low"]()
+            bt["upper"]()
+        else:
+            early_signs("B")
+            send(0)
+            sign("vc", 1)
+            scaled(1, 0)()
+            scaled(1, 1)()
+            sign("vc", 2, "v")
+            layer(2)
+        early_scan("B")
+        if r == 0:
+            vgap = {"signs": [bt["scale"]], "scan": [scaled(1, 2, "v")], "times": [lambda: pack(1)], "list": [ebq(0), lambda: send(1, 2)], "L0": [ebq(1)], "L1": [ebq(2), ebq(3)],
+                    "L3": [out(0, 2, cp)], "fin": [out(0, 3, cp)], "last": [out(1, 2, cp)], "four": [out(1, 3, cp)],
+                    "scan4": [out(2, 2, cp), out(2, 3, cp)], "l4": [differ(0), differ(1)]}
+            sgap = {"signs": [scaled(1, 1), scaled(1, 3)] + [scaled(2, b) for b in range(4)],
+                    "L2": [unpack(0)], "L3": [out(0, 0), unpack(1)], "fin": [out(0, 1), unpack(2)], "last": [out(1, 0), out(1, 1), out(2, 0), out(2, 1)]}
+        else:
+            vgap = {"signs": [scaled(1, 2, "v")], "scan": [lambda: send(1)], "list": [lambda: send(2)], "L1": [out(0, 2, cp), out(0, 3, cp)], "L3": [out(1, 2, cp)],
+                    "wrap": [unpack(2)], "fin": [out(1, 3, cp)], "last": [out(2, 3, cp)], "four": [differ(0)], "scan4": [differ(1)]}
+            sgap = {"signs": [scaled(1, 3)] + [scaled(2, b) for b in range(4)],
+                    "own": [unpack(0)], "L1": [out(0, 0)], "L2": [out(0, 1), unpack(1)], "L3": [out(1, 0)], "fin": [out(1, 1)], "last": [out(2, b) for b in range(3)]}
         if r == 2:
-            vgap["L1"] = [lambda: ts(["F2", "kq"], ["dq"], T.dq[:, 1:3 * NV:3], tab("F", 2, 1, 0, NV), -K / 2, A.mult, col("kq"), A.mult),
-                          lambda: ts(["F2", "kq"], ["dq1"], T.dq[:, 3 * NV + 1:84:3], tab("F", 2, 1, NV, 28), -K, A.mult, col("kq"), A.mult)]
-            sgap.update({"L0": [lambda e=e: act(["F2"], ["dq%d" % e], T.dq[:, e:84:3], tab("F", 2, e)) for e in (0, 2)],
-                         "scan4": [lambda: turn_row(0)], "l4": [lambda: turn_row(1)]})
+            sgap.update({"four": [lambda: turn_row(0)], "scan4": [lambda: turn_row(1)]})
         chain("B", 1, SHARES["B"], vgap, sgap)
         if r < 2:
             fetch(T.dd, DD, CUT, 320)
@@ -579,7 +620,7 @@ def rank_program(g, core, T, topo):
             fetch(T.dd, DD, 320, C)
             move(T.xt, "xt", T.dd, DD, T.vt, "vt", 0, CUT)
             move(T.xt, "xt", T.dd, DD, T.vt, "vt", CUT, 256)
-            scan(["seg16", "nu0", "nu1"], ["s3e", "s3m", "s3l"], T.s3[:, 0:3 * C:3], T.seg16[:], T.nu[:])
+            scan(["seg16", "nu0", "nu1"], cols("s3", 0, C), T.s3[:, 0:3 * C:3], T.seg16[:], T.nu[:])
             product(0)
             e = PARTS["xc"][0][1]
             codes_out(0, e, ["xc0"])

from concourse.bass import DstId, RemoteDMATransfer
from concourse.mybir import dt, AluOpType, ActivationFunctionType
import comms_topo

STEP = [1, 2, 3]
C = 448
PARTS = {"xc": [(0, 192), (192, 320), (320, C)], "vc": [(0, 128), (128, 320), (320, C)]}
EARLY, NV = {"F": 12, "B": 8}, 20
HRUNS = PARTS["vc"]
LAYER = [(4, 5, 6, 7), (4, 5, 6, 7), (3, 0, 1, 2)]
UNPACK = [(0, 1, 2, 3), (4, 5, 6, 7), (0, 1, 2, 3)]
CUT = HEAD = 224
SHARES = {"F0": {"L0": 10, "L1": 10, "L2": 10}, "F": {}, "B": {"L4": 6}}
K = 2.0 ** 24
M = 1.5 * 2.0 ** 27
LS = {"one": 0, "twoF": 32, "threeF": 64, "joinF": 96, "twoB": 132, "threeB": 160, "pair": 192, "end": 224}
BF, F32, I32, U16, MX, U8 = "bfloat16", "float32", "int32", "uint16", "float8_e4m3fn_x4", "uint8"

SCRATCH = {}
for _n, _w in (("x0", 1792), ("xt", 1792), ("xh", 1792), ("xg", 1792), ("vt", 1792), ("ht", 1792), ("dd", 1792), ("tg", 1792), ("ut", 512), ("vv", 512),
               ("wt", 896), ("eb", 520), ("zt", 520), ("R", 6 * C), ("iot", C),
               ("j16", 17), ("j4", 32), ("seg16", C), ("seg4", C), ("sa", 32), ("sb", 32), ("sp", 32),
               ("rowq", C), ("rowqs", C), ("rowt", C), ("arow", C), ("brow", C), ("agrow", C), ("df", C), ("nu", C),
               ("mg", C), ("s3", 1360), ("sc", C), ("sd", C), ("sn", C), ("sm", C), ("sc4", C), ("sg", C)):
    SCRATCH[_n] = ("sbuf", [128, _w], BF)
for _n, _w in (("uc", 128), ("uq", 128), ("vq", 128), ("wq", 512), ("xc", C), ("vc", C), ("ebc", 512), ("shc", 224), ("zc", 128),
               ("hc0", C), ("hc1", C), ("hc2", C), ("lc0", C), ("lc1", C), ("lc2", C)):
    SCRATCH[_n] = ("sbuf", [128, _w], MX)
    SCRATCH[_n + "p"] = ("sbuf", [128, _w], U8)
for _n, _w in (("qU", 28), ("sU", 28), ("mU", 28), ("loU", 28), ("ls0", 28), ("ls", 256), ("l4", 112), ("q7", 64),
               ("ulist", 8), ("qoU", 28), ("rep", 28)):
    SCRATCH[_n] = ("sbuf", [128, _w], U16)
for _n, _w in (("iwb", 84), ("fac", 84), ("iw", 28), ("tabC", 28), ("tC", 28),
               ("tO", 56), ("tbF", 252), ("tbB", 336), ("t4", 84),
               ("hq", 28), ("tq", 28), ("lo", 28), ("dq", 84), ("cq", 40), ("ysb", C), ("qrow", C)):
    SCRATCH[_n] = ("sbuf", [128, _w], F32)
for _n, _w in (("gqi", 28), ("gsi", 28), ("gmi", 28), ("pi", 8), ("uli", 16)):
    SCRATCH[_n] = ("sbuf", [128, _w], I32)
for _k in range(8):
    SCRATCH["P%d" % _k] = ("psum", [128, 512], F32)
SEMAPHORES = ["v", "s", "t", "gc"] + ["d%d" % k for k in range(60)] + ["arr%d" % k for k in range(9)] + ["snt"]


def rank_program(g, core, T, topo):
    rank = T.rank_of(core)
    if rank is None:
        return
    A = AluOpType
    F = ActivationFunctionType
    queue = {"v": g.vector, "s": g.scalar, "t": g.tensor, "g": g, "y": g.sync}
    own = {"v": "v", "s": "s", "t": "t", "g": "gc"}
    known = {q: {} for q in queue}
    count, W, R, nd = {}, {}, {}, [0]

    def need(q, toks):
        best = {}
        for tok in toks:
            if tok[0] not in best or best[tok[0]][1] < tok[1]:
                best[tok[0]] = tok
        order = sorted(best.values(), key=lambda k: -len(k[2]))
        for sem, val, snap in order:
            if known[q].get(sem, 0) < val:
                queue[q].wait_ge(T.sem[sem], val)
                known[q][sem] = val
            for k, x in snap.items():
                if known[q].get(k, 0) < x:
                    known[q][k] = x

    def deps(reads, writes):
        toks = []
        for k in reads:
            toks += W[k]
        for k in writes:
            toks += W.get(k, []) + list(R.get(k, {}).values())
        return toks

    def done(tok, reads, writes):
        for k in writes:
            W[k] = [tok]
            R[k] = {}
        for k in reads:
            if k not in writes:
                R.setdefault(k, {})[tok[0]] = tok

    def op(q, reads, writes, call):
        need(q, deps(reads, writes))
        sem = own[q]
        count[sem] = count.get(sem, 0) + 1
        call().then_inc(T.sem[sem], 1)
        done((sem, count[sem], dict(known[q])), reads, writes)

    def dma(q, pairs, reads, writes):
        need(q, deps(reads, writes))
        sem = "d%d" % nd[0]
        nd[0] += 1
        for o, i in pairs:
            queue[q].dma_start(o, i).then_inc(T.sem[sem], 16)
        count[sem] = 16 * len(pairs)
        done((sem, count[sem], dict(known[q])), reads, writes)

    def tt(reads, writes, out, a, b, o):
        op("v", reads, writes, lambda: g.vector.tensor_tensor(out, a, b, o))

    def ts(reads, writes, out, a, s1, o1, s2=None, o2=None):
        if o2 is None:
            op("v", reads, writes, lambda: g.vector.tensor_scalar(out, a, s1, None, o1))
        else:
            op("v", reads, writes, lambda: g.vector.tensor_scalar(out, a, s1, s2, o1, o2))

    def cp(reads, writes, out, a):
        op("v", reads, writes, lambda: g.vector.tensor_copy(out, a))

    def fill(writes, out, c):
        op("v", [], writes, lambda: g.vector.memset(out, c))

    def act(reads, writes, out, a, f=F.Copy, **kw):
        op("s", reads, writes, lambda: g.scalar.activation(out, a, f, **kw))

    def quant(reads, writes, c, a, b, src, e):
        op("v", reads, writes, lambda: g.vector.quantize_mx(T[c][:, a:b], T[c + "p"][:, a:b], src[:, e:e + 4 * (b - a)]))

    def mm(reads, writes, out, w, wa, x, xa, n):
        op("t", reads, writes, lambda: g.tensor.matmul_mx(out, T[w][:, wa:wa + 128], T[w + "p"][:, wa:wa + 128], T[x][:, xa:xa + n], T[x + "p"][:, xa:xa + n], True, True))

    def scan(reads, writes, out, seg, a):
        op("v", reads, writes, lambda: g.vector.tensor_tensor_scan(out, seg, a, 0.0, A.mult, A.add))

    def cols(key, a, b):
        return ["%s:%d" % (key, k) for k in range(a // 16, (b + 15) // 16)]

    def times(reads, writes, out, table):
        op("v", cols("s3", 0, C) + ["s30", "s31"] + reads, writes, lambda: g.vector.tensor_tensor_scan(out, table, T.s3[:, 29:1358:16], 0.0, A.add, A.mult))

    def iota(key, out, pat, base, cm, flag=True):
        if flag:
            op("g", [], [key], lambda: g.iota(out, pat, base, cm, allow_small_or_imprecise_dtypes=True))
        else:
            op("g", [], [key], lambda: g.iota(out, pat, base, cm))

    def both(key):
        return [key + "v", key + "s"]

    def gather(okey, out, win, lst, keys, a, nv, b):
        if nv > a:
            cp(keys, okey[0], out(16 * a, 16 * nv), win.indirect(lst(a, nv)))
        if b > nv:
            act(keys, okey[1], out(16 * nv, 16 * b), win.indirect(lst(nv, b)))

    def view(t, o=0):
        return lambda a, b: t[:, o + a:o + b]

    place = {"c16": 0, "c4": 1, "c1": 2, "cg": 3}

    def col(name, a=0, b=128):
        k = place.setdefault(name, len(place))
        return T.cq[a:b, k:k + 1]

    def icol(name):
        k = ("pi", "p16", "p4", "p1", "grp").index(name)
        return T.pi[:, k:k + 1]

    def const(name, src, s1, o1, s2=None, o2=None):
        ts([src], [name], col(name), col(src), s1, o1, s2, o2)

    def lst(name, a=0, b=128, n=28):
        return T.ls[a:b, LS[name]:LS[name] + n]

    dma("y", [(T.gqi[:], T.gq[:])], [], ["gqi"])
    dma("s", [(T.gmi[:], T.gm[:])], [], ["gmi"])
    dma("y", [(T.ut[:], T.u[:])], [], ["ut"])
    dma("s", [(T.gsi[16:128, :], T.gq[0:112, :]), (T.gsi[0:16, :], T.gq[112:128, :])], [], ["gsi"])
    for k, (a, b) in enumerate(PARTS["xc"]):
        dma("sys"[k], [(T.x0[:, 4 * a:4 * b], T.x[:, 4 * a:4 * b])], [], cols("x0", a, b))

    def late_loads():
        dma("y", [(T.wq[:].bitcast(dt.uint8), T.wc[:])], [], ["wqc"])
        dma("y", [(T.wqp[:], T.ws[:])], [], ["wqp"])
        dma("y", [(T.vv[:], T.v[:])], [], ["vv"])

    def score(src, key, c, k):
        a, b = PARTS[c][k]
        quant(cols(key, a, b), [c + str(k)], c, a, b, src, 4 * a)
        mm(["uqc", "uqs", c + str(k)], ["P%d" % k], T["P%d" % k][:, 0:b - a], "uq", 0, c, a, b - a)

    def sign(c, k, q="s"):
        a, b = PARTS[c][k]
        if q == "s":
            act(["P%d" % k], cols("sg", a, b), T.sg[:, a:b], T["P%d" % k][:, 0:b - a], F.Sign, bias=-(2.0 ** -93))
        else:
            cp(["P%d" % k], cols("sg", a, b), T.sg[:, a:b], T["P%d" % k][:, 0:b - a])

    def early_signs(d, q="v"):
        e = EARLY[d]
        keys, out, src = cols("sg", 0, 16 * e) + ["loU"], T.mg[:, 0:16 * e], T.sg[:, 0:16 * e].indirect(T.loU[:, 0:e])
        if q == "s":
            act(keys, cols("mg", 0, 16 * e), out, src, F.Copy, scale=0.5)
        else:
            ts(keys, cols("mg", 0, 16 * e), out, src, 0.0, A.is_gt, -0.5, A.add)

    def wrap_signs(a, b):
        scan(["seg16"] + cols("mg", 16 * a, 16 * b), cols("s3", 16 * a, 16 * b), T.s3[:, 48 * a:48 * b:3], T.seg16[:, 16 * a:16 * b], T.mg[:, 16 * a:16 * b])

    def early_scan(d):
        wrap_signs(0, EARLY[d])

    def halve(src, key, a, b):
        return lambda: act(cols(key, a, b), cols("xh", a, b), T.xh[:, 4 * a:4 * b], src[:, 4 * a:4 * b], F.Copy, scale=0.5)

    def copy_half():
        dma("y", [(T.xg[:, 0:4 * CUT], T.xh[:, 0:4 * CUT])], cols("xh", 0, CUT), cols("xg", 0, CUT))

    def scatter(a, b):
        return lambda: cp(["iot", "sU"], ["inv"], T.rowqs[:, 0:C].indirect(T.sU[:, a:b]), T.iot[:, 16 * a:16 * b])

    def ebq(b):
        return lambda: quant(["ebi"], ["ebc%d" % b], "ebc", 128 * b, 128 * b + 128, T.eb, 4 - b)

    def tab(d, k, e, a=0, b=28, p=128):
        return T["tb" + d][0:p, 84 * k + 3 * a + e:84 * k + 3 * b:3]

    def tables(d):
        t, k0, k1, k2 = T["tb" + d], d + "0", d + "1", d + "2"
        n = 2 if d == "F" else 3
        u = t[:, 84 * n:84 * n + 84]
        return {
            "wrap": lambda: scan(["seg16"] + both("rowt"), ["sn"], T.sn[:], T.seg16[:], T.rowt[:]),
            "half": lambda: ts(["sn", "kaph"], ["tq"], T.tq[:], T.sn[:, 15:C:16], col("kaph"), A.mult),
            "mean": lambda: (tt(["tq", "hq"], [d + "q"], tab(d, n, 2), T.tq[:], T.hq[:], A.add),
                             tt(["tq", "hq"], [d + "d"], tab(d, n, 1), T.tq[:], T.hq[:], A.subtract)),
            "high": lambda: ts([d + "z", d + "q", d + "d"], [k0], t[:, 0:84], u, M, A.add, -M, A.add),
            "low": lambda: tt([d + "z", d + "q", d + "d", k0], [k1], t[:, 84:168], u, t[:, 0:84], A.subtract),
            "scale": lambda: tt(["fac", d + "z"], [k0, k1, k2, d + "q", d + "d"] + ["Bo0", "Bo1", "Bu"] * (d == "B"), t[:, 1:252:3], t[:, 1:252:3], T.fac[:], A.mult),
        }

    def back_tables():
        def inverse():
            ts(["sda", "kaph"], ["hq"], T.hq[:], T.sd[:, 15:C:16], col("kaph"), A.mult)
            for k in range(2):
                ts(["sda", "kap"], ["q7%d" % k], T.q7[0:32, 32 * k:32 * k + 28], T.sd[0:32, 15:C:16], col("kap", 0, 32), A.mult, 224.25 + C * k, A.add)
            dma("y", [(lst("twoB", 96, 112), T.q7[0:16, 32:60]), (lst("twoB", 112, 128), T.q7[0:16, 0:28])], ["q70", "q71", "lz"], ["q7"])
        return dict(
            tables("B"),
            row=lambda: gather((None, both("rowt")), view(T.rowt), T.rowqs[:, 0:C], view(T.mU), ["inv", "mU"], 0, 0, 28),
            wrapinv=lambda: scan(["seg16", "inv"], ["sda", "sdb"], T.sd[:], T.seg16[:], T.rowqs[:]),
            inverse=inverse,
            upper=lambda: cp(["Bz", "Bq", "Bd"], ["Bu"], T.tbB[64:128, 168:252], T.tbB[64:128, 252:336]),
            places=lambda: (ts(["gmi"], ["tO0"], T.tO[:, 0:28], T.gmi[:], 0.5, A.mult, -112.0, A.add),
                            ts(["iw"], ["tO1"], T.tO[:, 28:56], T.iw[:], 0.5, A.mult, -112.0, A.add)),
            own=lambda: (tt(["tO0", "tO1"], ["Bo0"], tab("B", 2, 2, p=64), T.tO[0:64, 0:28], T.tO[0:64, 28:56], A.add),
                         tt(["tO0", "tO1"], ["Bo1"], tab("B", 2, 1, p=64), T.tO[0:64, 0:28], T.tO[0:64, 28:56], A.subtract)))

    tf, bt = tables("F"), back_tables()
    iota("pi", icol("pi"), [[0, 1]], 0, 1, False)
    iota("j16", T.j16[:], [[1, 17]], -1, 0)
    iota("iot", T.iot[:, 0:C], [[1, C]], -224, 0)
    iota("uli", T.uli[:, 1:8], [[16, 7]], 0, 0, False)
    iota("uli0", T.uli[:, 0:1], [[0, 1]], 112, 0, False)
    iota("iwb", T.iwb[:], [[0, 3], [16, 28]], 0, 0)
    iota("j4", T.j4[:], [[1, 2], [0, 4], [1, 4]], -1, 0)
    fill(["z"], T.zt[:], 0.0)
    op("g", ["z"], ["wi"], lambda: g.affine_select(T.wt[:, 192:704], T.zt[:, 0:512], [[1, 128], [0, 4]], A.not_equal, 1.0, 0, -1))
    op("g", ["z"], ["ebi"], lambda: g.affine_select(T.eb[:], T.zt[:], [[1, 520]], A.not_equal, 1.0, -4, -4))
    ts(["pi"], ["p16"], icol("p16"), icol("pi"), 15, A.bitwise_and)
    ts(["pi"], ["p4"], icol("p4"), icol("pi"), 2, A.arith_shift_right, 3, A.bitwise_and)
    ts(["pi"], ["p1"], icol("p1"), icol("pi"), 3, A.bitwise_and)
    ts(["pi"], ["grp"], icol("grp"), icol("pi"), 4, A.arith_shift_right)
    fill(["s30"], T.s3[:, 29:1360:48], 0.0)
    fill(["s31"], T.s3[:, 13:1360:48], 1.0)
    cp(["p16", "p4", "p1", "grp"], ["c16", "c4", "c1", "cg"], T.cq[:, 0:4], T.pi[:, 1:5])
    fill(["lz"], T.ls[:], 0)
    ts(["j16", "c16"], ["sa"], T.sa[:, 0:16], T.j16[:, 1:17], col("c16"), A.not_equal)
    ts(["j16", "c16"], ["sb"], T.sb[:, 0:16], T.j16[:, 0:16], col("c16"), A.is_equal, K, A.mult)
    ts(["z", "c16"], ["rep"], T.rep[:], T.zt[:, 0:28], col("c16"), A.add)
    const("kap", "c16", 15.0, A.is_equal, 1 / K, A.max)
    const("short", "cg", 3.0, A.is_lt)
    const("g448", "cg", float(C), A.mult, 0.25, A.add)
    const("k1", "c4", 3.0, A.is_equal, 1 / K, A.max)
    const("c896", "c1", 896.25, A.add)
    tt(["sa", "sb"], ["sp"], T.sp[:, 0:16], T.sa[:, 0:16], T.sb[:, 0:16], A.max)
    act(["z"], ["wt0"], T.wt[:, 0:192], T.zt[:, 0:192])
    act(["z"], ["wt2"], T.wt[:, 704:896], T.zt[:, 0:192])
    act(["z"], ["Fz"], T.tbF[:, 168:252:3], T.zt[:, 0:28])
    act(["z"], ["Bz"], T.tbB[:, 168:336:3], T.zt[:, 0:56])
    act(["sp", "rep"], ["seg16"], T.seg16[:], T.sp[:, 0:16].indirect(T.rep[:, 0:28]))
    cp(["gqi"], ["qU"], T.qU[:], T.gqi[:])
    const("kaph", "kap", 0.5, A.mult)
    const("from", "g448", 224.25 + 2 * C, A.min)
    cp(["gmi"], ["mU"], T.mU[:], T.gmi[:])
    ts(["gqi"], ["hq"], T.hq[:], T.gqi[:], 0.5, A.mult, -112.0, A.add)
    const("k4", "k1", 4.0, A.mult)
    gather((both("rowq"), None), view(T.rowq), T.iot[:, 0:C], view(T.qU), ["iot", "qU"], 0, 28, 28)
    quant(["ut"], ["uc"], "uc", 0, 128, T.ut, 0)
    cp(["uli", "uli0"], ["ulist"], T.ulist[:], T.uli[:, 0:8])
    ts(["iwb", "c16"], ["iw"], T.iw[:], T.iwb[:, 0:28], col("c16"), A.add)
    ts(["iwb"], ["fac"], T.fac[:], T.iwb[:], 16.0 * NV, A.is_lt, 1.0, A.add)
    gather((["rowtv"], ["rowts"]), view(T.rowt), T.rowq[:, 0:C], view(T.mU), both("rowq") + ["mU"], 0, 14, 28)
    act(["uc", "ulist"], ["uqs"], T.uqp[:, 0:128], T.ucp[:, 0:128].indirect(T.ulist[:, 0:8]))
    cp(["uc", "ulist"], ["uqc"], T.uq[:, 0:128].bitcast(dt.uint32), T.uc[:, 0:128].bitcast(dt.uint32).indirect(T.ulist[:, 0:8]))
    tt(["gmi", "iw"], ["lo"], T.lo[:], T.gmi[:], T.iw[:], A.min)
    tf["wrap"]()
    score(T.x0, "x0", "xc", 0)
    cp(["lo"], ["loU"], T.loU[:], T.lo[:])
    ts(["kap"], ["fac"], T.fac[:], T.fac[:], col("kap"), A.mult)
    cp(["gsi"], ["sU"], T.sU[:], T.gsi[:])
    tf["half"]()
    score(T.x0, "x0", "xc", 1)
    score(T.x0, "x0", "xc", 2)
    tf["mean"]()
    scatter(0, 4)()
    halve(T.x0, "x0", 0, CUT)()
    copy_half()
    late_loads()
    sign("xc", 0)
    sign("xc", 1)
    tf["high"]()
    ts(["j4", "c4"], ["sa4"], T.sa[:, 16:32], T.j4[:, 16:32], col("c4"), A.not_equal)
    ts(["j4", "c4"], ["sb4"], T.sb[:, 16:32], T.j4[:, 0:16], col("c4"), A.is_equal, K, A.mult)
    early_signs("F", "s")
    sign("xc", 2, "v")
    tf["low"]()
    tt(["sa4", "sb4"], ["sp4"], T.sp[:, 16:32], T.sa[:, 16:32], T.sb[:, 16:32], A.max)

    H = HEAD // 16
    HALF = {"a": (0, H), "b": (H, 28), "ab": (0, 28)}

    def row_keys(i, hs="ab"):
        return ["qs"] if i == -1 else [k for h in hs for k in both("L%s%s" % (i, h))]

    def chain(d, way, shares, vgap, sgap):
        def gap(name):
            for f in vgap.get(name, []) + sgap.get(name, []):
                f()
        early = EARLY[d]
        ts(cols("sg", 0, 16 * NV) + ["loU"], cols("mg", 16 * early, 16 * NV), T.mg[:, 16 * early:16 * NV], T.sg[:, 0:16 * NV].indirect(T.loU[:, early:NV]), 0.0, A.is_gt, -0.5, A.add)
        act(cols("sg", 0, C) + ["loU"], cols("mg", 16 * NV, C), T.mg[:, 16 * NV:C], T.sg[:, 0:C].indirect(T.loU[:, NV:28]), F.Sign, bias=-(2.0 ** -93))
        gap("signs")
        wrap_signs(early, NV)
        gap("mid")
        wrap_signs(NV, 28)
        gap("scan")
        for k, okeys, out in ((0, ["z0", "z"], T.zt[:, 0:336:4]), (1, ["z1"], T.zt[:, 1:336:4]), (2, ["t4"], T.t4[:])):
            times([d + str(k)], okeys, out, T["tb" + d][:, 84 * k:84 * k + 84])
        gap("times")
        quant(["z0", "z1"], ["zc"], "zc", 0, 128, T.zt, 0)
        ts(["t4"], ["ls0"], T.ls0[:], T.t4[:, 2:84:3], 224.25, A.add)
        for n in (1, 2, 3):
            bank = "P%d" % (3 + n)
            mm(["zc", "shc"], [bank], T[bank][:, 0:128], "shc", 48 + way * 16 * n, "zc", 0, 128)
        gap("list")
        row = "arow" if d == "F" else "brow"

        def compose(n, out, win, lists, keys, hs):
            a, b = HALF[hs]
            nv = a + shares.get("L%s" % n, {"a": 8, "b": 6, "ab": 14}[hs])
            gather((["L%s%sv" % (n, h) for h in hs], ["L%s%ss" % (n, h) for h in hs]), out, win, lists, keys, a, nv, b)

        def step(n, a, b, name, keys, hs="ab"):
            out = view(T[row]) if n == row else view(T.R, (n + 1) * C)
            compose(n, out, T.R[:, (a + 1) * C:(b + 1) * C], view(T.ls, LS[name]), [k for i in range(a, b) for k in row_keys(i)] + keys + ["lz"], hs)

        def wrap(key, n, p, w, hs="ab"):
            a, b = 16 * HALF[hs][0], 16 * HALF[hs][1]
            scan(["seg16"] + row_keys(n, hs), [key + h for h in hs], T[key][p:p + w, a:b], T.seg16[p:p + w, a:b], T.R[p:p + w, (n + 1) * C + a:(n + 1) * C + b])

        def hand(key, p, w, name, to, hs="ab"):
            a, b = HALF[hs]
            for q, at in to:
                ts([key + h for h in hs] + ["kap", "lz"], ["%s%d%s" % (name, q, h) for h in hs], T.ls[q:q + w, LS[name] + a:LS[name] + b],
                   T[key][p:p + w, 16 * a + 15:16 * b:16], col("kap", p, p + w), A.mult, 224.25 + at * C, A.add)
            return ["%s%d%s" % (name, q, h) for q, at in to for h in hs]

        def wrap4(h):
            a, b = 16 * HALF[h][0], 16 * HALF[h][1]
            scan(["seg4"] + row_keys(row, h), ["sc4" + h], T.sc4[:, a:b], T.seg4[:, a:b], T[row][:, a:b])

        def offsets(h):
            a, b = 16 * HALF[h][0], 16 * HALF[h][1]
            ts(["sc4" + h, "k4", "c896"], ["l4" + h], T.l4[:, a // 4:b // 4], T.sc4[:, a + 3:b:4], col("k4"), A.mult, col("c896"), A.add)

        compose(0, view(T.R, C), T.iot[:, 0:C], view(T.ls0), ["iot", "ls0"], "ab")
        gap("own")
        ts(["P4", "lz"], ["one"], lst("one"), T.P4[:, 2:84:3], 224.25, A.add)
        if d == "F":
            ts(["P5", "lz"], ["twoF"], lst("twoF"), T.P5[:, 2:84:3], 224.25, A.add)
            tt(["P6", "tabC"], ["tC"], T.tC[:], T.P6[:, 2:84:3], T.tabC[:], A.add)
            gap("L0")
            step(1, 0, 1, "one", ["one"])
            cp(["tC", "lz"], ["threeF"], lst("threeF"), T.tC[:])
            gap("L1")
            step(2, 1, 2, "twoF", ["twoF"])
            gap("L2")
            for h in "ab":
                step(3, 0, 3, "threeF", ["threeF"], h)
            gap("L3")
            for h in "ab":
                wrap("sc", 3, 0, 64, h)
            gap("wrap")
            keys = {h: hand("sc", 0, 64, "joinF", ((64, 0),), h) + ["joinF0"] for h in "ab"}
            name, rows = "joinF", (3, 4)
        else:
            ts(["P5", "lz"], ["twoB"], lst("twoB", 0, 64), T.P5[0:64, 2:84:3], 224.25 + C, A.add)
            ts(["P6", "lz"], ["threeB"], lst("threeB", 0, 64), T.P6[0:64, 2:84:3], 224.25 + C, A.add)
            gap("L0")
            step(1, 0, 1, "one", ["one"])
            gap("L1")
            step(2, 0, 2, "twoB", ["twoB", "q7"])
            wrap("sc", 1, 64, 32)
            gap("L2")
            step(3, 1, 3, "threeB", ["threeB", "a8", "a8d"])
            pair = hand("sc", 64, 32, "pair", ((0, 4), (64, 0)))
            gap("L3")
            wrap("sd", 3, 96, 32)
            step(4, -1, 4, "pair", pair)
            gap("wrap")
            keys = dict.fromkeys("ab", hand("sd", 96, 32, "end", ((0, 5), (32, 4), (64, 5), (96, 0))))
            name, rows = "end", (-1, 5)
        gap("fin")
        for h in "ab":
            step(row, rows[0], rows[1], name, keys[h], h)
        gap("last")
        wrap4("a")
        gap("four")
        wrap4("b")
        offsets("a")
        gap("scan4")
        offsets("b")
        gap("l4")

    def move(out, okey, win, wkeys, base, bkey, a, b):
        tt(wkeys + ["l4a"] + ["l4b"] * (b > HEAD) + cols(bkey, a, b), cols(okey, a, b), out[:, 4 * a:4 * b], win[:, 0:4 * C].indirect(T.l4[:, a // 4:b // 4]), base[:, 4 * a:4 * b], A.add)

    def fetch(win, wkeys, a, b):
        act(wkeys + ["l4a"] * (a < HEAD) + ["l4b"], cols("tg", a, b), T.tg[:, 4 * a:4 * b], win[:, 0:4 * C].indirect(T.l4[:, a // 4:b // 4]))

    def add(out, okey, base, bkey, a, b):
        tt(cols("tg", a, b) + cols(bkey, a, b), cols(okey, a, b), out[:, 4 * a:4 * b], T.tg[:, 4 * a:4 * b], base[:, 4 * a:4 * b], A.add)

    def turn_row(k):
        act(["df0", "df1"][0:k + 1] + ["loU", "kap", "kap2"], ["nu%d" % k], T.nu[:, 224 * k:224 * k + 224], T.df[:, 0:224 * k + 224].indirect(T.loU[:, 14 * k:14 * k + 14]),
            F.Identity, bias=col("kap"), scale=col("kap2"))

    def turn_scan():
        scan(["seg16", "nu0", "nu1"], ["sn"], T.sn[:], T.seg16[:], T.nu[:])

    def turn(d):
        for k in (0, 1, 2):
            v = tab(d, k, 1)
            tt(["sn"], [d + str(k)], v, v, T.sn[:, 15:C:16], A.mult)

    def differ(k):
        return lambda: tt(row_keys("brow", "ab"[k]) + ["agrow", "ag0"], ["df%d" % k], T.df[:, 224 * k:224 * k + 224], T.brow[:, 224 * k:224 * k + 224], T.agrow[:, 224 * k:224 * k + 224], A.not_equal)

    def wrap_a8():
        scan(["seg16"] + row_keys("arow"), ["sm"], T.sm[96:128, :], T.seg16[96:128, :], T.arow[96:128, :])

    def list_a8():
        ts(["sm", "kap", "lz"], ["a8", "a8d"], lst("threeB", 96, 128), T.sm[96:128, 15:C:16], col("kap", 96, 128), A.mult, 224.25 + C, A.add)
        dma("y", [(lst("threeB", 96, 112), lst("threeB", 112, 128))], ["a8"], ["a8d"])

    XH = cols("xh", 0, C)
    DD = ["dd%d%d" % (h, b) for h in range(len(HRUNS)) for b in range(4)]
    for r in range(3):
        dst = T.cores[rank ^ STEP[r]]
        hc, lc = "hc%d" % r, "lc%d" % r
        src, skey = (T.x0, "x0") if r == 0 else (T.xt, "xt")
        if r == 0:
            vgap = {"signs": [tf["scale"], lambda: early_scan("F")], "scan": [lambda: quant(["wt0", "wt2", "wi"], ["shc"], "shc", 0, 224, T.wt, 0)],
                    "times": [scatter(4, 6)], "list": [scatter(6, 10)],
                    "own": [lambda: ts(["iw", "short", "from"], ["tabC"], T.tabC[:], T.iw[:], col("short"), A.mult, col("from"), A.add)],
                    "L0": [scatter(10, 16)], "L1": [scatter(16, 22)], "L2": [scatter(22, 28)],
                    "L3": [lambda: cp(["iw", "lz"], ["joinF0"], lst("joinF", 0, 64), T.iw[0:64, :]), bt["row"], bt["places"]], "wrap": [bt["wrapinv"]],
                    "fin": [lambda: const("kap2", "kap", -2.0, A.mult), lambda: const("kq", "c16", 15.0, A.not_equal, 1 / K, A.max)],
                    "last": [bt["inverse"]], "four": [bt["wrap"]], "scan4": [wrap_a8], "l4": [bt["half"]]}
            sgap = {"signs": [lambda: act(["sp4", "rep"], ["seg4"], T.seg4[:], T.sp[:, 16:32].indirect(T.rep[:, 0:28])), halve(src, skey, CUT, 320)],
                    "last": [halve(src, skey, 320, C)]}
            dma("y", [(T.agrow[0:16, :], T.iot[0:16, 0:C])], ["iot"], ["ag0"])
            dma("y", [(T.R[64:128, 0:C], T.rowq[48:112, :]), (T.R[0:64, 0:C], T.rowq[0:64, :])], both("rowq"), ["qs"])
        else:
            vgap = {"signs": [lambda: turn("F")], "scan": [lambda: turn("B")], "scan4": [wrap_a8]}
            sgap = {"signs": [halve(src, skey, 0, CUT), copy_half, halve(src, skey, CUT, 320)], "L3": [halve(src, skey, 320, C)]}
        if r == 1:
            vgap["L1"] = [lambda: quant(["vv"], ["vq"], "vq", 0, 128, T.vv, 0)]
        if r == 2:
            vgap["L1"] = [lambda: ts(["F2", "kq"], ["dq"], T.dq[:, 1:3 * NV:3], tab("F", 2, 1, 0, NV), -K / 2, A.mult, col("kq"), A.mult),
                          lambda: ts(["F2", "kq"], ["dq1"], T.dq[:, 3 * NV + 1:84:3], tab("F", 2, 1, NV, 28), -K, A.mult, col("kq"), A.mult)]
            vgap["L2"] = [lambda e=e: cp(["F2"], ["dq%d" % e], T.dq[:, e:84:3], tab("F", 2, e)) for e in (0, 2)]
        chain("F", -1, SHARES["F" if r else "F0"], vgap, sgap)
        dma("y", [(T.agrow[16:128, :], T.arow[0:112, :])], row_keys("arow"), ["agrow"])

        def layer(h, bs=range(4)):
            a, e = HRUNS[h]
            for b in bs:
                bank = "P%d" % LAYER[h][b]
                mm(["wqc", "wqp", "vc%d" % h], [bank], T[bank][:, 0:e - a], "wq", 128 * b, "vc", a, e - a)

        def scaled(h, b, q="s"):
            a, e = HRUNS[h]
            bank = "P%d" % LAYER[h][b]
            args = ([bank], ["ht%d%d" % (h, b)], T.ht[:, 4 * a + b:4 * e:4], T[bank][:, 0:e - a])
            return (lambda: act(*args, F.Copy, scale=0.03125)) if q == "s" else (lambda: ts(*args, 0.03125, A.mult))

        def pack(h):
            a, e = HRUNS[h]
            quant(["ht%d%d" % (h, b) for b in range(4)], [hc + str(h)], hc, a, e, T.ht, 4 * a)

        def send(*hs):
            pack(hs[-1])
            a, e = HRUNS[hs[0]][0], HRUNS[hs[-1]][1]
            need("g", [t for h in hs for t in W[hc + str(h)]])
            rid, pid, _ = topo.addr(dst)
            mask, ne = topo.mask(core, dst), len(topo.engines(core, dst))
            arr = "arr%d" % (3 * r + hs[0])
            for o, i in ((T[lc][:, a:e].bitcast(dt.uint8), T[hc][:, a:e].bitcast(dt.uint8)), (T[lc + "p"][:, a:e], T[hc + "p"][:, a:e])):
                g.remote_dma(out_ap=o, in_ap=i, remote_sem=T.sem[arr], local_sem=T.sem["snt"], pid=pid, routing_id=rid, dma_engine_mask=mask)
            count[arr] = 2 * ne
            count["snt"] = count.get("snt", 0) + 2 * ne
            for h in hs:
                W[lc + str(h)] = [(arr, 2 * ne, {})]

        def unpack(h):
            a, e = HRUNS[h]
            return lambda: [mm(["ebc%d" % b, lc + str(h)], ["P%d" % k], T["P%d" % k][:, 0:e - a], "ebc", 128 * b, lc, a, e - a) for b, k in enumerate(UNPACK[h])]

        def out(h, b, f=act):
            a, e = HRUNS[h]
            bank = "P%d" % UNPACK[h][b]
            return lambda: f([bank], ["dd%d%d" % (h, b)], T.dd[:, 4 * a + b:4 * e:4], T[bank][:, 0:e - a])

        e = HRUNS[0][1]
        move(T.vt, "vt", T.xh, XH, T.xg, "xg", 0, e)
        fetch(T.xh, XH, CUT, 320)
        fetch(T.xh, XH, 320, C)
        list_a8()
        move(T.vt, "vt", T.xh, XH, T.xg, "xg", e, CUT)
        score(T.vt, "vt", "vc", 0)
        layer(0)
        sign("vc", 0)
        scaled(0, 0)()
        scaled(0, 1)()
        add(T.vt, "vt", T.xh, "xh", CUT, 320)
        add(T.vt, "vt", T.xh, "xh", 320, C)
        score(T.vt, "vt", "vc", 1)
        layer(1, (0,))
        score(T.vt, "vt", "vc", 2)
        scaled(0, 2, "v")()
        scaled(0, 3, "v")()
        layer(1, (1, 2, 3))
        if r == 0:
            bt["mean"]()
            bt["own"]()
            send(0)
            sign("vc", 1)
            scaled(1, 0)()
            sign("vc", 2, "v")
            layer(2)
            bt["high"]()
            early_signs("B")
            bt["low"]()
            bt["upper"]()
        else:
            early_signs("B")
            send(0)
            sign("vc", 1)
            scaled(1, 0)()
            scaled(1, 1)()
            sign("vc", 2, "v")
            layer(2)
        early_scan("B")
        if r == 0:
            vgap = {"signs": [bt["scale"]], "scan": [scaled(1, 2, "v")], "times": [lambda: pack(1)], "list": [ebq(0), lambda: send(1, 2)], "L0": [ebq(1)], "L1": [ebq(2), ebq(3)],
                    "L3": [out(0, 2, cp)], "fin": [out(0, 3, cp)], "last": [out(1, 2, cp)], "four": [out(1, 3, cp)],
                    "scan4": [out(2, 2, cp), out(2, 3, cp)], "l4": [differ(0), differ(1)]}
            sgap = {"signs": [scaled(1, 1), scaled(1, 3)] + [scaled(2, b) for b in range(4)],
                    "L2": [unpack(0)], "L3": [out(0, 0), unpack(1)], "fin": [out(0, 1), unpack(2)], "last": [out(1, 0), out(1, 1), out(2, 0), out(2, 1)]}
        else:
            vgap = {"signs": [scaled(1, 2, "v")], "scan": [lambda: send(1)], "list": [lambda: send(2)], "L1": [out(0, 2, cp), out(0, 3, cp)], "L3": [out(1, 2, cp)],
                    "wrap": [unpack(2)], "fin": [out(1, 3, cp)], "last": [out(2, 3, cp)], "four": [differ(0)], "scan4": [differ(1)]}
            sgap = {"signs": [scaled(1, 3)] + [scaled(2, b) for b in range(4)],
                    "own": [unpack(0)], "L1": [out(0, 0)], "L2": [out(0, 1), unpack(1)], "L3": [out(1, 0)], "fin": [out(1, 1)], "last": [out(2, b) for b in range(3)]}
        if r == 2:
            sgap.update({"four": [lambda: turn_row(0)], "scan4": [lambda: turn_row(1)]})
        chain("B", 1, SHARES["B"], vgap, sgap)
        if r < 2:
            fetch(T.dd, DD, CUT, 320)
            fetch(T.dd, DD, 320, C)
            turn_row(0)
            turn_row(1)
            move(T.xt, "xt", T.dd, DD, T.vt, "vt", 0, CUT)
            add(T.xt, "xt", T.vt, "vt", CUT, 320)
            score(T.xt, "xt", "xc", 0)
            sign("xc", 0)
            add(T.xt, "xt", T.vt, "vt", 320, C)
            score(T.xt, "xt", "xc", 1)
            score(T.xt, "xt", "xc", 2)
            sign("xc", 1)
            turn_scan()
            early_signs("F")
            sign("xc", 2, "v")
            early_scan("F")
        else:
            def product(k):
                a, b = PARTS["xc"][k]
                quant(cols("xt", a, b), ["xc%d" % k], "xc", a, b, T.xt, 4 * a)
                mm(["vq", "xc%d" % k], ["P%d" % k], T["P%d" % k][:, 0:b - a], "vq", 0, "xc", a, b - a)

            def result(k, f):
                a, b = PARTS["xc"][k]
                f(["P%d" % k], ["y%d" % k], T.ysb[:, a:b], T["P%d" % k][:, 0:b - a])

            def store(k):
                a, b = PARTS["xc"][k]
                dma("y", [(T.y[:, a:b], T.ysb[:, a:b])], ["y%d" % k], ["yo%d" % k])

            def codes_out(a, b, keys):
                dma("y", [(T.oc[:, 4 * a:4 * b], T.xc[:, a:b].bitcast(dt.uint8))], keys, ["oc%d" % a])

            def scales_out(q, ks):
                dma(q, [(T.osc[4 * k:4 * k + 4, :], T.xcp[32 * k:32 * k + 4, 0:C]) for k in ks], ["xc0", "xc1", "xc2"], ["osc" + q])
            fetch(T.dd, DD, 256, 320)
            fetch(T.dd, DD, 320, C)
            move(T.xt, "xt", T.dd, DD, T.vt, "vt", 0, CUT)
            move(T.xt, "xt", T.dd, DD, T.vt, "vt", CUT, 256)
            scan(["seg16", "nu0", "nu1"], cols("s3", 0, C), T.s3[:, 0:3 * C:3], T.seg16[:], T.nu[:])
            product(0)
            e = PARTS["xc"][0][1]
            codes_out(0, e, ["xc0"])
            result(0, act)
            store(0)
            add(T.xt, "xt", T.vt, "vt", 256, 320)
            times(["dq", "dq0", "dq1", "dq2"], ["t4"], T.t4[:], T.dq[:])
            add(T.xt, "xt", T.vt, "vt", 320, C)
            product(1)
            ts(["t4"], ["qoU"], T.qoU[:], T.t4[:, 2:84:3], 224.25, A.add)
            product(2)
            ts(["iot", "qoU"], ["qrowv"], T.qrow[:, 0:160], T.iot[:, 0:C].indirect(T.qoU[:, 0:10]), 224.0, A.add)
            act(["iot", "qoU"], ["qrows"], T.qrow[:, 160:C], T.iot[:, 0:C].indirect(T.qoU[:, 10:28]), F.Identity, bias=224.0)
            dma("s", [(T.qo[:], T.qrow[0:128:16, :])], both("qrow"), ["qo"])
            codes_out(e, C, ["xc1", "xc2"])
            result(1, cp)
            result(2, cp)
            scales_out("y", (0, 1))
            store(1)
            store(2)
            scales_out("s", (2, 3))
    for sem in count:
        if max(known[q].get(sem, 0) for q in queue) < count[sem]:
            g.wait_ge(T.sem[sem], count[sem])
